import numpy as np
import ml_dtypes


def mxq(x, axis, fmt="e4m3"):
    dtype, down = {"e4m3": (ml_dtypes.float8_e4m3fn, 7), "e5m2": (ml_dtypes.float8_e5m2, 14)}[fmt]
    v = np.moveaxis(np.asarray(x, np.float32).astype(ml_dtypes.bfloat16).astype(np.float64), axis, -1)
    blocks = v.reshape(v.shape[:-1] + (-1, 32))
    amax = np.abs(blocks).max(-1, keepdims=True)
    byte = np.maximum(np.where(amax > 0, np.frexp(amax)[1] - 1 + 127, 0) - down, 1)
    scale = np.exp2(byte - 127.0)
    codes = (blocks / scale).astype(np.float32).astype(dtype).astype(np.float64)
    return np.moveaxis((codes * scale).reshape(v.shape), -1, axis)


WIDE = False


def mx_kscale(k):
    if not WIDE:
        return np.ones(k)
    levels = np.array([10, -10, 5, -5, 0])
    if k % 512:
        return np.exp2(np.random.permutation(np.resize(levels, k // 32))).repeat(32)
    a = np.empty((k // 512, 16))
    for p in range(k // 512):
        a[p, :8] = np.random.permutation(np.resize(levels, 8))
        for g in range(8):
            far = levels[np.abs(levels - a[p, g]) >= 10]
            a[p, g + 8] = far[np.random.randint(len(far))]
    return np.exp2(a.ravel()).repeat(32)


def f64(x):
    return np.asarray(x).astype(np.float64)


def striped(idx):
    return np.tile(idx.reshape(-1, 16).T, (8, 1)).astype(np.uint16)


def unstriped(offs):
    return offs[:16].T.reshape(-1).astype(np.int64)


E2M1 = np.array([0.0, 0.5, 1.0, 1.5, 2.0, 3.0, 4.0, 6.0, -0.0, -0.5, -1.0, -1.5, -2.0, -3.0, -4.0, -6.0])


def pack_weight(w, fmt):
    k, n = w.shape
    w = f64(np.asarray(w, np.float32).astype(ml_dtypes.bfloat16)).reshape(k // 32, 32, n)
    amax = np.abs(w).max(1)
    if fmt == "e4m3":
        byte = np.frexp(amax)[1] - 1 + 127 - 7
    else:
        mant, ex = np.frexp(amax / 6.0)
        byte = np.where(mant > 0.5, ex, ex - 1) + 127
    byte = np.clip(np.where(amax > 0, byte, 1), 1, 254)
    scaled = (w * np.exp2(127.0 - byte)[:, None, :]).reshape(k, n).astype(np.float32)
    by_word = np.ascontiguousarray(scaled.reshape(k // 512, 128, 4, n).transpose(0, 1, 3, 2))
    if fmt == "e4m3":
        words = by_word.astype(ml_dtypes.float8_e4m3fn).view(np.uint8)
    else:
        c = by_word.astype(ml_dtypes.float4_e2m1fn).view(np.uint8) & 0xF
        words = (c[..., 0::2] | (c[..., 1::2] << 4)).reshape(k // 512, 128, 2 * n)
    return np.ascontiguousarray(words), np.ascontiguousarray(byte.astype(np.uint8).reshape(k // 512, 16, n))


def unpack_weight(words, scales, fmt):
    g, _, n = scales.shape
    words = np.ascontiguousarray(words).reshape(g, 128, n, -1)
    if fmt == "e4m3":
        vals = words.view(ml_dtypes.float8_e4m3fn).astype(np.float64)
    else:
        nib = np.empty((g, 128, n, 4), np.uint8)
        nib[..., 0::2] = words & 0xF
        nib[..., 1::2] = words >> 4
        vals = E2M1[nib]
    vals = vals * np.repeat(np.exp2(scales.astype(np.float64) - 127.0), 8, axis=1)[..., None]
    return vals.transpose(0, 1, 3, 2).reshape(g * 512, n)


def gelu(v):
    return 0.5 * v * (1.0 + np.tanh(np.sqrt(2.0 / np.pi) * (v + 0.044715 * v**3)))


def striped8(idx):
    return np.concatenate([v.reshape(-1, 16).T for v in idx]).astype(np.uint16)


def unstriped8(offs):
    return np.stack([offs[16 * g:16 * g + 16].T.reshape(-1) for g in range(8)]).astype(np.int64)


def runs(v, idx8):
    k = np.arange(v.shape[0])
    return v[k[:, None], idx8[k % 512 // 64]]


K, T, S, H, H2, N = 1024, 2048, 1024, 512, 1024, 256

def setup_inputs():
    n = np.random.standard_normal
    s = mx_kscale(K)[:, None]
    u = mx_kscale(H)[:, None]
    tab_words, tab_scales = pack_weight(n((K, T)) * s, "e4m3")
    offs = striped8(np.stack([np.random.permutation(T)[:S] for _ in range(8)]))
    wg_words, wg_scales = pack_weight(1.5 * n((K, H2)) / np.sqrt(K) / s, "e2m1")
    wu = (n((K, H)) / np.sqrt(K) / s).astype(np.float32)
    cell = n((H, S)).astype(np.float32)
    gain = (np.exp(0.3 * n(H)) * u[:, 0]).astype(np.float32)
    wo_words, wo_scales = pack_weight(2.0 * n((H, N)) / np.sqrt(H) / u, "e4m3")
    return {"tab_words": tab_words, "tab_scales": tab_scales, "offs": offs,
            "wg_words": wg_words, "wg_scales": wg_scales, "wu": wu,
            "cell": cell, "gain": gain,
            "wo_words": wo_words, "wo_scales": wo_scales}

def reference(tab_words, tab_scales, offs, wg_words, wg_scales, wu, cell, gain,
              wo_words, wo_scales):
    v = runs(unpack_weight(tab_words, tab_scales, "e4m3"), unstriped8(offs))
    wg = unpack_weight(wg_words, wg_scales, "e2m1")
    wo = unpack_weight(wo_words, wo_scales, "e4m3")
    e = 1.0 / (1.0 + np.exp(-(wg.T @ v)))
    d = np.tanh(mxq(f64(wu), 0, "e4m3").T @ v)
    h = f64(gain)[:, None] * (e[:H] * d + e[H:] * f64(cell))
    return wo.T @ mxq(h, 0, "e4m3")

@@ -1,0 +1,193 @@
+from contextlib import ExitStack
+
+import concourse.mybir as mybir
+
+K, T, S, H, N = 1024, 2048, 1024, 512, 256
+FLOPS = 2 * K * 3 * H * S + 2 * H * N * S
+
+F32 = mybir.dt.float32
+BF16 = mybir.dt.bfloat16
+I32 = mybir.dt.int32
+U32 = mybir.dt.uint32
+U16 = mybir.dt.uint16
+U8 = mybir.dt.uint8
+FP8X4 = mybir.dt.float8_e4m3fn_x4
+FP4X4 = mybir.dt.float4_e2m1fn_x4
+ACT = mybir.ActivationFunctionType
+MULT = mybir.AluOpType.mult
+ADD = mybir.AluOpType.add
+
+P = 128
+PACK = 4
+PASSES = K // (P * PACK)
+COLS = 512
+HALVES = S // COLS
+WG0 = S
+WO0 = S + 2 * H
+PLANE = WO0 + N
+
+
+def tile_list_term_tree_cell_kernel(tc, tab_words, tab_scales, offs, wg_words, wg_scales, wu, cell, gain,
+                                             wo_words, wo_scales, out):
+    nc = tc.nc
+    with ExitStack() as ctx:
+        keep = ctx.enter_context(tc.tile_pool(name="keep", bufs=1))
+        work = ctx.enter_context(tc.tile_pool(name="work", bufs=2))
+        psum1 = ctx.enter_context(tc.psum_pool(name="psum1", bufs=1))
+        psum2 = ctx.enter_context(tc.psum_pool(name="psum2", bufs=2))
+
+        offsets = keep.tile([P, S // 16], U16, name="offsets")
+        nc.sync.dma_start(offsets[:], offs)
+
+        tab_rows = keep.tile([P, T], U8, name="tab_rows", tag="tab_rows", align_bytes=64)
+        wg_rows = keep.tile([P, 2 * H], U8, name="wg_rows", tag="rows1", align_bytes=64)
+        staged = keep.tile([P, PLANE], U8, name="staged", tag="staged", align_bytes=64)
+        planes = keep.tile([P, PASSES * PLANE], U8, name="planes", align_bytes=64)
+        nc.vector.memset(tab_rows[:].bitcast(I32), 0)
+        nc.vector.memset(wg_rows[:].bitcast(I32), 0)
+        nc.vector.memset(planes[:].bitcast(I32), 0)
+        warm_in = keep.tile([P, 1], F32, name="warm_in")
+        nc.vector.memset(warm_in[:], 0.0)
+        nc.sync.dma_start(tab_rows[0:P:4, :].bitcast(I32), tab_scales.bitcast(I32).rearrange("a q t -> q a t"))
+        nc.sync.dma_start(wg_rows[0:P:4, :].bitcast(I32), wg_scales.bitcast(I32).rearrange("a q c -> q a c"))
+        nc.sync.dma_start(staged[0:P:4, WO0:].bitcast(I32),
+                          wo_scales[0].bitcast(I32).unsqueeze(1).to_broadcast([16, PASSES, N // 4]))
+
+        gains = keep.tile([P, PACK], F32, name="gains")
+        nc.sync.dma_start(gains[:], gain.rearrange("(p t) -> p t", t=PACK))
+
+        wg_raw = keep.tile([P, PASSES * 2 * H * 2], U8, name="wg_raw", tag="raw", align_bytes=64)
+        nc.sync.dma_start(wg_raw[:].bitcast(I32).rearrange("p (a c) -> p a c", a=PASSES),
+                          wg_words.bitcast(I32).rearrange("a p c -> p a c"))
+        tab = []
+        for a in range(PASSES):
+            tab.append(keep.tile([P, T], I32, name=f"tab{a}", align_bytes=64))
+            nc.sync.dma_start(tab[a][:], tab_words[a].rearrange("p t i -> p (t i)").bitcast(I32))
+
+        def load_cell(h, tag):
+            tile = keep.tile([P, PACK, COLS], F32, name=f"cell{h}", tag=tag, align_bytes=64)
+            nc.sync.dma_start(tile[:], cell[:, h * COLS:(h + 1) * COLS].rearrange("(p t) j -> p t j", t=PACK))
+            return tile
+
+        def load_wu(tile, a, c):
+            rows = wu[a * P * PACK:(a + 1) * P * PACK, c * (H // 2):(c + 1) * (H // 2)]
+            nc.sync.dma_start(tile, rows.rearrange("(p i) r -> p i r", i=PACK))
+            return tile
+
+        wu_raw = []
+        for n in range(3):
+            early = keep.tile([P, PACK, H // 2], F32, name=f"wu_raw{n}", tag=f"wu_raw{n}", align_bytes=64)
+            wu_raw.append(load_wu(early[:], n // 2, n % 2))
+
+        warm = keep.tile([P, 1], F32, name="warm")
+        nc.scalar.activation(warm[:], warm_in[:], ACT.Sigmoid)
+
+        picked_rows = keep.tile([P, S], U8, name="picked_rows", tag="rows0", align_bytes=64)
+        nc.vector.tensor_copy(picked_rows[:], tab_rows[:].indirect(offsets[:]))
+        nc.vector.tensor_copy(staged[:, WG0:WO0].rearrange("p (g t m) -> p g t m", g=2, t=PACK),
+                              wg_rows[:].rearrange("p (g m t) -> p g t m", g=2, t=PACK))
+        nc.vector.tensor_copy(staged[:, :WG0].bitcast(I32), picked_rows[:].bitcast(I32))
+        for d in range(4):
+            nc.scalar.dma_start(planes[32 * d:32 * d + 4, :].bitcast(I32), staged[32 * d:32 * d + 32:4, :].bitcast(I32))
+
+        wg_codes = []
+        for g in range(2):
+            wg_codes.append(keep.tile([P, PASSES * H * 2], U8, name=f"wg_codes{g}", tag=f"rows{g}", align_bytes=64))
+        wg_in = wg_raw[:].bitcast(U16).rearrange("p (a g m t) -> p g a t m", a=PASSES, g=2, t=PACK)
+        for g in range(2):
+            nc.vector.tensor_copy(wg_codes[g][:].bitcast(U16).rearrange("p (a t m) -> p a t m", a=PASSES, t=PACK),
+                                  wg_in[:, g])
+
+        wu_last = keep.tile([P, PACK, H // 2], F32, name="wu_last", tag="raw", align_bytes=64)
+        wu_raw.append(load_wu(wu_last[:], 1, 1))
+
+        v = {}
+        for h in range(HALVES):
+            for a in range(PASSES):
+                v[a, h] = keep.tile([P, COLS], U32, name=f"v{a}{h}", tag="tab_rows" if a == h == 0 else f"v{a}{h}", align_bytes=64)
+                nc.vector.tensor_copy(v[a, h][:], tab[a][:].bitcast(U32).indirect(
+                    offsets[:, h * COLS // 16:(h + 1) * COLS // 16]))
+
+        wu_codes, wu_scales = [], []
+        for a in range(PASSES):
+            wu_bf = keep.tile([P, PACK, P, PACK], BF16, name=f"wu_bf{a}", tag=f"wu_bf{a}", align_bytes=64)
+            for c in range(2):
+                dst = wu_bf[:, :, c * 64:(c + 1) * 64, :].rearrange("p (u w) m i -> p u m i w", u=2)
+                src = wu_raw[2 * a + c].rearrange("p i (m u w) -> p u m i w", u=2, w=2)
+                if (a, c) == (1, 1):
+                    nc.vector.tensor_copy(dst, src)
+                else:
+                    nc.scalar.copy(dst, src)
+            wu_codes.append(keep.tile([P, H], U32, name=f"wu_codes{a}", align_bytes=64))
+            wu_scales.append(keep.tile([P, H], U8, name=f"wu_scales{a}", align_bytes=64))
+            step = PACK if a == 0 else 1
+            for t in range(0, PACK, step):
+                cols = slice(t * P, (t + step) * P)
+                nc.vector.quantize_mx(wu_codes[a][:, cols].bitcast(FP8X4), wu_scales[a][:, cols],
+                                      wu_bf[:, t:t + step].rearrange("p t m i -> p (t m i)"))
+
+        cells = [load_cell(0, "wu_raw0"), load_cell(1, "wu_bf0")]
+        wo_codes = keep.tile([P, N], I32, name="wo_codes", tag="wu_bf1", align_bytes=64)
+        acts = [keep.tile([P, 3 * PACK, COLS], F32, name=f"acts{h}", tag=tag, align_bytes=64)
+                for h, tag in enumerate(("wu_raw1", "raw"))]
+        nc.sync.dma_start(wo_codes[:], wo_words[0].rearrange("p c i -> p (c i)").bitcast(I32))
+
+        def plane(a, start, width):
+            return planes[:, a * PLANE + start:a * PLANE + start + width]
+
+        def product(h, weights, func, row, tag, banks):
+            acc = psum1.tile([P, COLS], F32, name="acc", tag=tag, bufs=banks)
+            for a in range(PASSES):
+                codes, scales = weights(a)
+                nc.tensor.matmul_mx(acc[:], lhsT=codes, lhsT_scale=scales, rhs=v[a, h][:].bitcast(FP8X4),
+                                    rhs_scale=plane(a, h * COLS, COLS), start=(a == 0), stop=(a == PASSES - 1))
+            nc.scalar.activation(acts[h][:, row, :], acc[:], func)
+            return acts[h][:, row, :]
+
+        def gate(h, g, t):
+            def weights(a):
+                first = (a * PACK + t) * P * 2
+                return (wg_codes[g][:, first:first + 2 * P].bitcast(FP4X4), plane(a, WG0 + g * H + t * P, P))
+            return product(h, weights, ACT.Sigmoid, g * PACK + t, "gates", 4)
+
+        def candidate(h, t):
+            def weights(a):
+                return (wu_codes[a][:, t * P:(t + 1) * P].bitcast(FP8X4), wu_scales[a][:, t * P:(t + 1) * P])
+            return product(h, weights, ACT.Tanh, 2 * PACK + t, "cands", 2)
+
+        for h in range(HALVES):
+            kept = work.tile([P, PACK, COLS], F32, name="kept")
+            fresh = work.tile([P, PACK, COLS], F32, name="fresh")
+
+            def make_fresh(t):
+                admit, cand = gate(h, 0, t), candidate(h, t)
+                nc.vector.scalar_tensor_tensor(fresh[:, t, :], admit, gains[:, t:t + 1], cand, MULT, MULT)
+
+            def make_kept(t):
+                forget = gate(h, 1, t)
+                nc.vector.scalar_tensor_tensor(kept[:, t, :], forget, gains[:, t:t + 1], cells[h][:, t, :], MULT, MULT)
+
+            for t in range(PACK):
+                make_fresh(t)
+                if h > 0:
+                    make_kept(t)
+            for t in range(PACK if h == 0 else 0):
+                make_kept(t)
+            for first, width in ((0, 256), (256, 256)) if h == 0 else ((0, 256), (256, 128), (384, 128)):
+                cols = slice(first, first + width)
+                h_bf = work.tile([P, width, PACK], BF16, name="h_bf", align_bytes=64)
+                nc.vector.tensor_tensor(h_bf[:].rearrange("p (c i) t -> p c t i", i=2),
+                                        fresh[:, :, cols].rearrange("p t (c i) -> p c t i", i=2),
+                                        kept[:, :, cols].rearrange("p t (c i) -> p c t i", i=2), ADD)
+                h_codes = work.tile([P, width], U32, name="h_codes", align_bytes=64)
+                h_scales = work.tile([P, width], U8, name="h_scales", align_bytes=64)
+                nc.vector.quantize_mx(h_codes[:].bitcast(FP8X4), h_scales[:], h_bf[:].rearrange("p j t -> p (j t)"))
+                acc = psum2.tile([P, N // P, width], F32, name="acc2")
+                for n in range(N // P):
+                    nc.tensor.matmul_mx(acc[:, n, :], lhsT=wo_codes[:, n * P:(n + 1) * P].bitcast(FP8X4),
+                                        lhsT_scale=plane(0, WO0 + n * P, P), rhs=h_codes[:].bitcast(FP8X4),
+                                        rhs_scale=h_scales[:], start=True, stop=True)
+                result = work.tile([P, N // P, width], F32, name="result", bufs=5)
+                nc.scalar.copy(result[:], acc[:])
+                j0 = h * COLS + first
+                nc.sync.dma_start(out[:, j0:j0 + width].rearrange("(n p) j -> p n j", p=P), result[:])

@@ -33,14 +33,13 @@ def tile_list_term_tree_cell_kernel(tc, tab_words, tab_scales, offs, wg_words, w
     with ExitStack() as ctx:
         keep = ctx.enter_context(tc.tile_pool(name="keep", bufs=1))
         work = ctx.enter_context(tc.tile_pool(name="work", bufs=2))
-        psum1 = ctx.enter_context(tc.psum_pool(name="psum1", bufs=1))
-        psum2 = ctx.enter_context(tc.psum_pool(name="psum2", bufs=2))
+        psum = ctx.enter_context(tc.psum_pool(name="psum", bufs=1))
 
         offsets = keep.tile([P, S // 16], U16, name="offsets")
         nc.sync.dma_start(offsets[:], offs)
 
         tab_rows = keep.tile([P, T], U8, name="tab_rows", tag="tab_rows", align_bytes=64)
-        wg_rows = keep.tile([P, 2 * H], U8, name="wg_rows", tag="rows1", align_bytes=64)
+        wg_rows = keep.tile([P, 2 * H], U8, name="wg_rows", tag="wg_rows", align_bytes=64)
         staged = keep.tile([P, PLANE], U8, name="staged", tag="staged", align_bytes=64)
         planes = keep.tile([P, PASSES * PLANE], U8, name="planes", align_bytes=64)
         nc.vector.memset(tab_rows[:].bitcast(I32), 0)
@@ -56,87 +55,76 @@ def tile_list_term_tree_cell_kernel(tc, tab_words, tab_scales, offs, wg_words, w
         gains = keep.tile([P, PACK], F32, name="gains")
         nc.sync.dma_start(gains[:], gain.rearrange("(p t) -> p t", t=PACK))
 
+        wo_codes = keep.tile([P, N], I32, name="wo_codes", align_bytes=64)
+        nc.sync.dma_start(wo_codes[:], wo_words[0].rearrange("p c i -> p (c i)").bitcast(I32))
+
         wg_raw = keep.tile([P, PASSES * 2 * H * 2], U8, name="wg_raw", tag="raw", align_bytes=64)
         nc.sync.dma_start(wg_raw[:].bitcast(I32).rearrange("p (a c) -> p a c", a=PASSES),
                           wg_words.bitcast(I32).rearrange("a p c -> p a c"))
         tab = []
         for a in range(PASSES):
-            tab.append(keep.tile([P, T], I32, name=f"tab{a}", align_bytes=64))
+            tab.append(keep.tile([P, T], I32, name=f"tab{a}", tag=f"tab{a}", align_bytes=64))
             nc.sync.dma_start(tab[a][:], tab_words[a].rearrange("p t i -> p (t i)").bitcast(I32))
-
-        def load_cell(h, tag):
-            tile = keep.tile([P, PACK, COLS], F32, name=f"cell{h}", tag=tag, align_bytes=64)
-            nc.sync.dma_start(tile[:], cell[:, h * COLS:(h + 1) * COLS].rearrange("(p t) j -> p t j", t=PACK))
-            return tile
-
-        def load_wu(tile, a, c):
-            rows = wu[a * P * PACK:(a + 1) * P * PACK, c * (H // 2):(c + 1) * (H // 2)]
-            nc.sync.dma_start(tile, rows.rearrange("(p i) r -> p i r", i=PACK))
-            return tile
-
-        wu_raw = []
-        for n in range(3):
-            early = keep.tile([P, PACK, H // 2], F32, name=f"wu_raw{n}", tag=f"wu_raw{n}", align_bytes=64)
-            wu_raw.append(load_wu(early[:], n // 2, n % 2))
 
         warm = keep.tile([P, 1], F32, name="warm")
         nc.scalar.activation(warm[:], warm_in[:], ACT.Sigmoid)
 
-        picked_rows = keep.tile([P, S], U8, name="picked_rows", tag="rows0", align_bytes=64)
+        picked_rows = keep.tile([P, S], U8, name="picked_rows", tag="picked_rows", align_bytes=64)
         nc.vector.tensor_copy(picked_rows[:], tab_rows[:].indirect(offsets[:]))
         nc.vector.tensor_copy(staged[:, WG0:WO0].rearrange("p (g t m) -> p g t m", g=2, t=PACK),
                               wg_rows[:].rearrange("p (g m t) -> p g t m", g=2, t=PACK))
         nc.vector.tensor_copy(staged[:, :WG0].bitcast(I32), picked_rows[:].bitcast(I32))
         for d in range(4):
-            nc.scalar.dma_start(planes[32 * d:32 * d + 4, :].bitcast(I32), staged[32 * d:32 * d + 32:4, :].bitcast(I32))
+            nc.sync.dma_start(planes[32 * d:32 * d + 4, :].bitcast(I32), staged[32 * d:32 * d + 32:4, :].bitcast(I32))
 
         wg_codes = []
-        for g in range(2):
-            wg_codes.append(keep.tile([P, PASSES * H * 2], U8, name=f"wg_codes{g}", tag=f"rows{g}", align_bytes=64))
+        for g, tag in enumerate(("tab_rows", "wg_rows")):
+            wg_codes.append(keep.tile([P, PASSES * H * 2], U8, name=f"wg_codes{g}", tag=tag, align_bytes=64))
         wg_in = wg_raw[:].bitcast(U16).rearrange("p (a g m t) -> p g a t m", a=PASSES, g=2, t=PACK)
         for g in range(2):
             nc.vector.tensor_copy(wg_codes[g][:].bitcast(U16).rearrange("p (a t m) -> p a t m", a=PASSES, t=PACK),
                                   wg_in[:, g])
 
-        wu_last = keep.tile([P, PACK, H // 2], F32, name="wu_last", tag="raw", align_bytes=64)
-        wu_raw.append(load_wu(wu_last[:], 1, 1))
+        wu_raw = []
+        for a, tag in enumerate(("picked_rows", "raw")):
+            wu_raw.append(keep.tile([P, PACK, H], F32, name=f"wu_raw{a}", tag=tag, align_bytes=64))
+            nc.sync.dma_start(wu_raw[a][:], wu[a * P * PACK:(a + 1) * P * PACK, :].rearrange("(p i) r -> p i r", i=PACK))
 
         v = {}
         for h in range(HALVES):
             for a in range(PASSES):
-                v[a, h] = keep.tile([P, COLS], U32, name=f"v{a}{h}", tag="tab_rows" if a == h == 0 else f"v{a}{h}", align_bytes=64)
+                v[a, h] = keep.tile([P, COLS], U32, name=f"v{a}{h}", tag="staged" if (a, h) == (0, 1) else f"v{a}{h}", align_bytes=64)
                 nc.vector.tensor_copy(v[a, h][:], tab[a][:].bitcast(U32).indirect(
                     offsets[:, h * COLS // 16:(h + 1) * COLS // 16]))
+
+        cells = keep.tile([P, PACK, S], F32, name="cells", tag="tab1", align_bytes=64)
+        for t in range(PACK):
+            nc.sync.dma_start(cells[:, t, :], cell.rearrange("(p t) j -> p t j", t=PACK)[:, t, :])
 
         wu_codes, wu_scales = [], []
         for a in range(PASSES):
             wu_bf = keep.tile([P, PACK, P, PACK], BF16, name=f"wu_bf{a}", tag=f"wu_bf{a}", align_bytes=64)
-            for c in range(2):
-                dst = wu_bf[:, :, c * 64:(c + 1) * 64, :].rearrange("p (u w) m i -> p u m i w", u=2)
-                src = wu_raw[2 * a + c].rearrange("p i (m u w) -> p u m i w", u=2, w=2)
-                if (a, c) == (1, 1):
-                    nc.vector.tensor_copy(dst, src)
-                else:
-                    nc.scalar.copy(dst, src)
             wu_codes.append(keep.tile([P, H], U32, name=f"wu_codes{a}", align_bytes=64))
             wu_scales.append(keep.tile([P, H], U8, name=f"wu_scales{a}", align_bytes=64))
-            step = PACK if a == 0 else 1
-            for t in range(0, PACK, step):
-                cols = slice(t * P, (t + step) * P)
+            for u in range(2):
+                dst = wu_bf[:, 2 * u:2 * u + 2].rearrange("p w m i -> p m i w")
+                src = wu_raw[a][:].rearrange("p i (m t) -> p m i t", t=PACK)[:, :, :, 2 * u:2 * u + 2]
+                if (a, u) == (1, 1):
+                    nc.scalar.copy(dst, src)
+                else:
+                    nc.vector.tensor_copy(dst, src)
+            for u in range(2):
+                cols = slice(2 * u * P, (2 * u + 2) * P)
                 nc.vector.quantize_mx(wu_codes[a][:, cols].bitcast(FP8X4), wu_scales[a][:, cols],
-                                      wu_bf[:, t:t + step].rearrange("p t m i -> p (t m i)"))
+                                      wu_bf[:, 2 * u:2 * u + 2].rearrange("p t m i -> p (t m i)"))
 
-        cells = [load_cell(0, "wu_raw0"), load_cell(1, "wu_bf0")]
-        wo_codes = keep.tile([P, N], I32, name="wo_codes", tag="wu_bf1", align_bytes=64)
-        acts = [keep.tile([P, 3 * PACK, COLS], F32, name=f"acts{h}", tag=tag, align_bytes=64)
-                for h, tag in enumerate(("wu_raw1", "raw"))]
-        nc.sync.dma_start(wo_codes[:], wo_words[0].rearrange("p c i -> p (c i)").bitcast(I32))
+        acts = [keep.tile([P, 3 * PACK, COLS], F32, name=f"acts{h}") for h in range(HALVES)]
 
         def plane(a, start, width):
             return planes[:, a * PLANE + start:a * PLANE + start + width]
 
         def product(h, weights, func, row, tag, banks):
-            acc = psum1.tile([P, COLS], F32, name="acc", tag=tag, bufs=banks)
+            acc = psum.tile([P, COLS], F32, name="acc", tag=tag, bufs=banks)
             for a in range(PASSES):
                 codes, scales = weights(a)
                 nc.tensor.matmul_mx(acc[:], lhsT=codes, lhsT_scale=scales, rhs=v[a, h][:].bitcast(FP8X4),
@@ -148,13 +136,14 @@ def tile_list_term_tree_cell_kernel(tc, tab_words, tab_scales, offs, wg_words, w
             def weights(a):
                 first = (a * PACK + t) * P * 2
                 return (wg_codes[g][:, first:first + 2 * P].bitcast(FP4X4), plane(a, WG0 + g * H + t * P, P))
-            return product(h, weights, ACT.Sigmoid, g * PACK + t, "gates", 4)
+            return product(h, weights, ACT.Sigmoid, g * PACK + t, "gates", 5)
 
         def candidate(h, t):
             def weights(a):
                 return (wu_codes[a][:, t * P:(t + 1) * P].bitcast(FP8X4), wu_scales[a][:, t * P:(t + 1) * P])
-            return product(h, weights, ACT.Tanh, 2 * PACK + t, "cands", 2)
+            return product(h, weights, ACT.Tanh, 2 * PACK + t, "cands", 3)
 
+        quantised = []
         for h in range(HALVES):
             kept = work.tile([P, PACK, COLS], F32, name="kept")
             fresh = work.tile([P, PACK, COLS], F32, name="fresh")
@@ -165,7 +154,11 @@ def tile_list_term_tree_cell_kernel(tc, tab_words, tab_scales, offs, wg_words, w
 
             def make_kept(t):
                 forget = gate(h, 1, t)
-                nc.vector.scalar_tensor_tensor(kept[:, t, :], forget, gains[:, t:t + 1], cells[h][:, t, :], MULT, MULT)
+                parts = 2 if t == PACK - 1 else 1
+                for c in range(parts):
+                    cols = slice(c * COLS // parts, (c + 1) * COLS // parts)
+                    nc.vector.scalar_tensor_tensor(kept[:, t, cols], forget[:, cols], gains[:, t:t + 1],
+                                                   cells[:, t, h * COLS:(h + 1) * COLS][:, cols], MULT, MULT)
 
             for t in range(PACK):
                 make_fresh(t)
@@ -173,21 +166,34 @@ def tile_list_term_tree_cell_kernel(tc, tab_words, tab_scales, offs, wg_words, w
                     make_kept(t)
             for t in range(PACK if h == 0 else 0):
                 make_kept(t)
-            for first, width in ((0, 256), (256, 256)) if h == 0 else ((0, 256), (256, 128), (384, 128)):
+
+            def add(first, width):
                 cols = slice(first, first + width)
-                h_bf = work.tile([P, width, PACK], BF16, name="h_bf", align_bytes=64)
+                h_bf = work.tile([P, width, PACK], BF16, name="h_bf", align_bytes=64, bufs=3)
                 nc.vector.tensor_tensor(h_bf[:].rearrange("p (c i) t -> p c t i", i=2),
                                         fresh[:, :, cols].rearrange("p t (c i) -> p c t i", i=2),
                                         kept[:, :, cols].rearrange("p t (c i) -> p c t i", i=2), ADD)
-                h_codes = work.tile([P, width], U32, name="h_codes", align_bytes=64)
-                h_scales = work.tile([P, width], U8, name="h_scales", align_bytes=64)
+                return h_bf
+
+            def quantise(first, width, h_bf):
+                h_codes = work.tile([P, width], U32, name="h_codes", align_bytes=64, bufs=5)
+                h_scales = work.tile([P, width], U8, name="h_scales", align_bytes=64, bufs=5)
                 nc.vector.quantize_mx(h_codes[:].bitcast(FP8X4), h_scales[:], h_bf[:].rearrange("p j t -> p (j t)"))
-                acc = psum2.tile([P, N // P, width], F32, name="acc2")
-                for n in range(N // P):
-                    nc.tensor.matmul_mx(acc[:, n, :], lhsT=wo_codes[:, n * P:(n + 1) * P].bitcast(FP8X4),
-                                        lhsT_scale=plane(0, WO0 + n * P, P), rhs=h_codes[:].bitcast(FP8X4),
-                                        rhs_scale=h_scales[:], start=True, stop=True)
-                result = work.tile([P, N // P, width], F32, name="result", bufs=5)
-                nc.scalar.copy(result[:], acc[:])
-                j0 = h * COLS + first
-                nc.sync.dma_start(out[:, j0:j0 + width].rearrange("(n p) j -> p n j", p=P), result[:])
+                quantised.append((h * COLS + first, width, h_codes, h_scales))
+
+            chunks = ((0, 256), (256, 256)) if h == 0 else ((0, 256), (256, 128), (384, 128))
+            sums = [add(*chunks[0])]
+            for c, chunk in enumerate(chunks):
+                if c + 1 < len(chunks):
+                    sums.append(add(*chunks[c + 1]))
+                quantise(*chunk, sums[c])
+
+        for first, width, h_codes, h_scales in quantised:
+            acc = psum.tile([P, N // P, width], F32, name="acc", tag="gates", bufs=5)
+            for n in range(N // P):
+                nc.tensor.matmul_mx(acc[:, n, :], lhsT=wo_codes[:, n * P:(n + 1) * P].bitcast(FP8X4),
+                                    lhsT_scale=plane(0, WO0 + n * P, P), rhs=h_codes[:].bitcast(FP8X4),
+                                    rhs_scale=h_scales[:], start=True, stop=True)
+            result = work.tile([P, N // P, width], F32, name="result", bufs=5)
+            nc.scalar.copy(result[:], acc[:])
+            nc.sync.dma_start(out[:, first:first + width].rearrange("(n p) j -> p n j", p=P), result[:])

@@ -24,7 +24,7 @@ COLS = 512
 HALVES = S // COLS
 WG0 = S
 WO0 = S + 2 * H
-PLANE = WO0 + N
+PLANE = WO0 + P
 
 
 def tile_list_term_tree_cell_kernel(tc, tab_words, tab_scales, offs, wg_words, wg_scales, wu, cell, gain,
@@ -50,7 +50,7 @@ def tile_list_term_tree_cell_kernel(tc, tab_words, tab_scales, offs, wg_words, w
         nc.sync.dma_start(tab_rows[0:P:4, :].bitcast(I32), tab_scales.bitcast(I32).rearrange("a q t -> q a t"))
         nc.sync.dma_start(wg_rows[0:P:4, :].bitcast(I32), wg_scales.bitcast(I32).rearrange("a q c -> q a c"))
         nc.sync.dma_start(staged[0:P:4, WO0:].bitcast(I32),
-                          wo_scales[0].bitcast(I32).unsqueeze(1).to_broadcast([16, PASSES, N // 4]))
+                          wo_scales[0].bitcast(I32).rearrange("q (n c) -> (q n) c", n=PASSES))
 
         gains = keep.tile([P, PACK], F32, name="gains")
         nc.sync.dma_start(gains[:], gain.rearrange("(p t) -> p t", t=PACK))
@@ -74,7 +74,7 @@ def tile_list_term_tree_cell_kernel(tc, tab_words, tab_scales, offs, wg_words, w
         nc.vector.tensor_copy(staged[:, WG0:WO0].rearrange("p (g t m) -> p g t m", g=2, t=PACK),
                               wg_rows[:].rearrange("p (g m t) -> p g t m", g=2, t=PACK))
         nc.vector.tensor_copy(staged[:, :WG0].bitcast(I32), picked_rows[:].bitcast(I32))
-        for d in range(4):
+        for d in (0, 2, 1, 3):
             nc.sync.dma_start(planes[32 * d:32 * d + 4, :].bitcast(I32), staged[32 * d:32 * d + 32:4, :].bitcast(I32))
 
         wg_codes = []
@@ -192,7 +192,7 @@ def tile_list_term_tree_cell_kernel(tc, tab_words, tab_scales, offs, wg_words, w
             acc = psum.tile([P, N // P, width], F32, name="acc", tag="gates", bufs=5)
             for n in range(N // P):
                 nc.tensor.matmul_mx(acc[:, n, :], lhsT=wo_codes[:, n * P:(n + 1) * P].bitcast(FP8X4),
-                                    lhsT_scale=plane(0, WO0 + n * P, P), rhs=h_codes[:].bitcast(FP8X4),
+                                    lhsT_scale=plane(n, WO0, P), rhs=h_codes[:].bitcast(FP8X4),
                                     rhs_scale=h_scales[:], start=True, stop=True)
             result = work.tile([P, N // P, width], F32, name="result", bufs=5)
             nc.scalar.copy(result[:], acc[:])

@@ -109,10 +109,10 @@ def tile_list_term_tree_cell_kernel(tc, tab_words, tab_scales, offs, wg_words, w
             for u in range(2):
                 dst = wu_bf[:, 2 * u:2 * u + 2].rearrange("p w m i -> p m i w")
                 src = wu_raw[a][:].rearrange("p i (m t) -> p m i t", t=PACK)[:, :, :, 2 * u:2 * u + 2]
-                if (a, u) == (1, 1):
-                    nc.scalar.copy(dst, src)
-                else:
+                if (a, u) == (1, 0):
                     nc.vector.tensor_copy(dst, src)
+                else:
+                    nc.scalar.copy(dst, src)
             for u in range(2):
                 cols = slice(2 * u * P, (2 * u + 2) * P)
                 nc.vector.quantize_mx(wu_codes[a][:, cols].bitcast(FP8X4), wu_scales[a][:, cols],

@@ -13,18 +13,29 @@ U16 = mybir.dt.uint16
 U8 = mybir.dt.uint8
 FP8X4 = mybir.dt.float8_e4m3fn_x4
 FP4X4 = mybir.dt.float4_e2m1fn_x4
-ACT = mybir.ActivationFunctionType
+SIGMOID = mybir.ActivationFunctionType.Sigmoid
+TANH = mybir.ActivationFunctionType.Tanh
 MULT = mybir.AluOpType.mult
 ADD = mybir.AluOpType.add
 
 P = 128
 PACK = 4
 PASSES = K // (P * PACK)
+GROUP = 16
+QUADRANT = 32
 COLS = 512
 HALVES = S // COLS
-WG0 = S
-WO0 = S + 2 * H
-PLANE = WO0 + P
+INPUT, FORGET, CANDIDATE = 0, 1, 2
+ALIGN = 64
+
+WG_SCALES = S
+WO_SCALES = WG_SCALES + 2 * H
+PLANE = WO_SCALES + P
+
+GATE_BANKS, CANDIDATE_BANKS = 5, 3
+
+CHUNKS = (((0, 256), (256, 256)), ((0, 256), (256, 128), (384, 128)))
+ALL_CHUNKS = sum(len(chunks) for chunks in CHUNKS)
 
 
 def tile_list_term_tree_cell_kernel(tc, tab_words, tab_scales, offs, wg_words, wg_scales, wu, cell, gain,
@@ -35,113 +46,107 @@ def tile_list_term_tree_cell_kernel(tc, tab_words, tab_scales, offs, wg_words, w
         work = ctx.enter_context(tc.tile_pool(name="work", bufs=2))
         psum = ctx.enter_context(tc.psum_pool(name="psum", bufs=1))
 
-        offsets = keep.tile([P, S // 16], U16, name="offsets")
+        offsets = keep.tile([P, S // GROUP], U16, name="offsets")
         nc.sync.dma_start(offsets[:], offs)
 
-        tab_rows = keep.tile([P, T], U8, name="tab_rows", tag="tab_rows", align_bytes=64)
-        wg_rows = keep.tile([P, 2 * H], U8, name="wg_rows", tag="wg_rows", align_bytes=64)
-        staged = keep.tile([P, PLANE], U8, name="staged", tag="staged", align_bytes=64)
-        planes = keep.tile([P, PASSES * PLANE], U8, name="planes", align_bytes=64)
+        tab_rows = keep.tile([P, T], U8, name="tab_rows", tag="tab_rows", align_bytes=ALIGN)
+        wg_rows = keep.tile([P, 2 * H], U8, name="wg_rows", tag="wg_rows", align_bytes=ALIGN)
+        staged = keep.tile([P, PLANE], U8, name="staged", tag="staged", align_bytes=ALIGN)
+        planes = keep.tile([P, PASSES * PLANE], U8, name="planes", align_bytes=ALIGN)
         nc.vector.memset(tab_rows[:].bitcast(I32), 0)
         nc.vector.memset(wg_rows[:].bitcast(I32), 0)
         nc.vector.memset(planes[:].bitcast(I32), 0)
-        warm_in = keep.tile([P, 1], F32, name="warm_in")
-        nc.vector.memset(warm_in[:], 0.0)
         nc.sync.dma_start(tab_rows[0:P:4, :].bitcast(I32), tab_scales.bitcast(I32).rearrange("a q t -> q a t"))
         nc.sync.dma_start(wg_rows[0:P:4, :].bitcast(I32), wg_scales.bitcast(I32).rearrange("a q c -> q a c"))
-        nc.sync.dma_start(staged[0:P:4, WO0:].bitcast(I32),
-                          wo_scales[0].bitcast(I32).rearrange("q (n c) -> (q n) c", n=PASSES))
+        nc.sync.dma_start(staged[0:P:4, WO_SCALES:].bitcast(I32),
+                          wo_scales[0].bitcast(I32).rearrange("q (n c) -> (q n) c", n=N // P))
 
         gains = keep.tile([P, PACK], F32, name="gains")
         nc.sync.dma_start(gains[:], gain.rearrange("(p t) -> p t", t=PACK))
 
-        wo_codes = keep.tile([P, N], I32, name="wo_codes", align_bytes=64)
+        wo_codes = keep.tile([P, N], I32, name="wo_codes", align_bytes=ALIGN)
         nc.sync.dma_start(wo_codes[:], wo_words[0].rearrange("p c i -> p (c i)").bitcast(I32))
 
-        wg_raw = keep.tile([P, PASSES * 2 * H * 2], U8, name="wg_raw", tag="raw", align_bytes=64)
+        wg_raw = keep.tile([P, PASSES * 2 * H * 2], U8, name="wg_raw", tag="wg_raw", align_bytes=ALIGN)
         nc.sync.dma_start(wg_raw[:].bitcast(I32).rearrange("p (a c) -> p a c", a=PASSES),
                           wg_words.bitcast(I32).rearrange("a p c -> p a c"))
-        tab = []
+        table = []
         for a in range(PASSES):
-            tab.append(keep.tile([P, T], I32, name=f"tab{a}", tag=f"tab{a}", align_bytes=64))
-            nc.sync.dma_start(tab[a][:], tab_words[a].rearrange("p t i -> p (t i)").bitcast(I32))
+            table.append(keep.tile([P, T], I32, name=f"table{a}", tag=f"table{a}", align_bytes=ALIGN))
+            nc.sync.dma_start(table[a][:], tab_words[a].rearrange("p t i -> p (t i)").bitcast(I32))
 
-        warm = keep.tile([P, 1], F32, name="warm")
-        nc.scalar.activation(warm[:], warm_in[:], ACT.Sigmoid)
-
-        picked_rows = keep.tile([P, S], U8, name="picked_rows", tag="picked_rows", align_bytes=64)
+        picked_rows = keep.tile([P, S], U8, name="picked_rows", tag="picked_rows", align_bytes=ALIGN)
         nc.vector.tensor_copy(picked_rows[:], tab_rows[:].indirect(offsets[:]))
-        nc.vector.tensor_copy(staged[:, WG0:WO0].rearrange("p (g t m) -> p g t m", g=2, t=PACK),
+        nc.vector.tensor_copy(staged[:, WG_SCALES:WO_SCALES].rearrange("p (g t m) -> p g t m", g=2, t=PACK),
                               wg_rows[:].rearrange("p (g m t) -> p g t m", g=2, t=PACK))
-        nc.vector.tensor_copy(staged[:, :WG0].bitcast(I32), picked_rows[:].bitcast(I32))
+        nc.vector.tensor_copy(staged[:, :WG_SCALES].bitcast(I32), picked_rows[:].bitcast(I32))
         for d in (0, 2, 1, 3):
-            nc.sync.dma_start(planes[32 * d:32 * d + 4, :].bitcast(I32), staged[32 * d:32 * d + 32:4, :].bitcast(I32))
+            first = QUADRANT * d
+            nc.sync.dma_start(planes[first:first + 4, :].bitcast(I32),
+                              staged[first:first + QUADRANT:4, :].bitcast(I32))
 
-        wg_codes = []
-        for g, tag in enumerate(("tab_rows", "wg_rows")):
-            wg_codes.append(keep.tile([P, PASSES * H * 2], U8, name=f"wg_codes{g}", tag=tag, align_bytes=64))
+        def plane(a, first, width):
+            return planes[:, a * PLANE + first:a * PLANE + first + width]
+
         wg_in = wg_raw[:].bitcast(U16).rearrange("p (a g m t) -> p g a t m", a=PASSES, g=2, t=PACK)
-        for g in range(2):
+        wg_codes = [keep.tile([P, PASSES * H * 2], U8, name=f"wg_codes{g}", tag=tag, align_bytes=ALIGN)
+                    for g, tag in enumerate(("tab_rows", "wg_rows"))]
+        for g in (INPUT, FORGET):
             nc.vector.tensor_copy(wg_codes[g][:].bitcast(U16).rearrange("p (a t m) -> p a t m", a=PASSES, t=PACK),
                                   wg_in[:, g])
 
         wu_raw = []
-        for a, tag in enumerate(("picked_rows", "raw")):
-            wu_raw.append(keep.tile([P, PACK, H], F32, name=f"wu_raw{a}", tag=tag, align_bytes=64))
-            nc.sync.dma_start(wu_raw[a][:], wu[a * P * PACK:(a + 1) * P * PACK, :].rearrange("(p i) r -> p i r", i=PACK))
+        for a, tag in enumerate(("picked_rows", "wg_raw")):
+            wu_raw.append(keep.tile([P, PACK, H], F32, name=f"wu_raw{a}", tag=tag, align_bytes=ALIGN))
+            nc.sync.dma_start(wu_raw[a][:],
+                              wu[a * P * PACK:(a + 1) * P * PACK, :].rearrange("(p i) r -> p i r", i=PACK))
 
-        v = {}
+        states = {}
         for h in range(HALVES):
+            entries = offsets[:, h * COLS // GROUP:(h + 1) * COLS // GROUP]
             for a in range(PASSES):
-                v[a, h] = keep.tile([P, COLS], U32, name=f"v{a}{h}", tag="staged" if (a, h) == (0, 1) else f"v{a}{h}", align_bytes=64)
-                nc.vector.tensor_copy(v[a, h][:], tab[a][:].bitcast(U32).indirect(
-                    offsets[:, h * COLS // 16:(h + 1) * COLS // 16]))
+                tag = "staged" if (a, h) == (0, 1) else f"states{a}{h}"
+                states[a, h] = keep.tile([P, COLS], U32, name=f"states{a}{h}", tag=tag, align_bytes=ALIGN)
+                nc.vector.tensor_copy(states[a, h][:], table[a][:].bitcast(U32).indirect(entries))
 
-        cells = keep.tile([P, PACK, S], F32, name="cells", tag="tab1", align_bytes=64)
+        cells = keep.tile([P, PACK, S], F32, name="cells", tag="table1", align_bytes=ALIGN)
         for t in range(PACK):
             nc.sync.dma_start(cells[:, t, :], cell.rearrange("(p t) j -> p t j", t=PACK)[:, t, :])
 
         wu_codes, wu_scales = [], []
         for a in range(PASSES):
-            wu_bf = keep.tile([P, PACK, P, PACK], BF16, name=f"wu_bf{a}", tag=f"wu_bf{a}", align_bytes=64)
-            wu_codes.append(keep.tile([P, H], U32, name=f"wu_codes{a}", align_bytes=64))
-            wu_scales.append(keep.tile([P, H], U8, name=f"wu_scales{a}", align_bytes=64))
-            for u in range(2):
-                dst = wu_bf[:, 2 * u:2 * u + 2].rearrange("p w m i -> p m i w")
-                src = wu_raw[a][:].rearrange("p i (m t) -> p m i t", t=PACK)[:, :, :, 2 * u:2 * u + 2]
-                if (a, u) == (1, 0):
-                    nc.vector.tensor_copy(dst, src)
-                else:
-                    nc.scalar.copy(dst, src)
-            for u in range(2):
-                cols = slice(2 * u * P, (2 * u + 2) * P)
+            wu_bf = keep.tile([P, PACK, P, PACK], BF16, name=f"wu_bf{a}", tag=f"wu_bf{a}", align_bytes=ALIGN)
+            wu_codes.append(keep.tile([P, H], U32, name=f"wu_codes{a}", align_bytes=ALIGN))
+            wu_scales.append(keep.tile([P, H], U8, name=f"wu_scales{a}", align_bytes=ALIGN))
+            wu_in = wu_raw[a][:].rearrange("p i (m t) -> p m i t", t=PACK)
+            for t, copy in ((0, nc.vector.tensor_copy), (2, nc.scalar.copy)):
+                copy(wu_bf[:, t:t + 2].rearrange("p t m i -> p m i t"), wu_in[:, :, :, t:t + 2])
+            for t in (0, 2):
+                cols = slice(t * P, (t + 2) * P)
                 nc.vector.quantize_mx(wu_codes[a][:, cols].bitcast(FP8X4), wu_scales[a][:, cols],
-                                      wu_bf[:, 2 * u:2 * u + 2].rearrange("p t m i -> p (t m i)"))
+                                      wu_bf[:, t:t + 2].rearrange("p t m i -> p (t m i)"))
 
-        acts = [keep.tile([P, 3 * PACK, COLS], F32, name=f"acts{h}") for h in range(HALVES)]
+        acts = [keep.tile([P, 3 * PACK, COLS], F32, name=f"acts{h}", tag=tag, align_bytes=ALIGN)
+                for h, tag in enumerate(("acts0", "wu_bf1"))]
 
-        def plane(a, start, width):
-            return planes[:, a * PLANE + start:a * PLANE + start + width]
-
-        def product(h, weights, func, row, tag, banks):
-            acc = psum.tile([P, COLS], F32, name="acc", tag=tag, bufs=banks)
+        def first_stage(h, kind, t):
+            if kind == CANDIDATE:
+                acc = psum.tile([P, COLS], F32, name="acc", tag="candidates", bufs=CANDIDATE_BANKS)
+            else:
+                acc = psum.tile([P, COLS], F32, name="acc", tag="gates", bufs=GATE_BANKS)
             for a in range(PASSES):
-                codes, scales = weights(a)
-                nc.tensor.matmul_mx(acc[:], lhsT=codes, lhsT_scale=scales, rhs=v[a, h][:].bitcast(FP8X4),
+                if kind == CANDIDATE:
+                    codes = wu_codes[a][:, t * P:(t + 1) * P].bitcast(FP8X4)
+                    scales = wu_scales[a][:, t * P:(t + 1) * P]
+                else:
+                    first = (a * PACK + t) * P * 2
+                    codes = wg_codes[kind][:, first:first + P * 2].bitcast(FP4X4)
+                    scales = plane(a, WG_SCALES + kind * H + t * P, P)
+                nc.tensor.matmul_mx(acc[:], lhsT=codes, lhsT_scale=scales, rhs=states[a, h][:].bitcast(FP8X4),
                                     rhs_scale=plane(a, h * COLS, COLS), start=(a == 0), stop=(a == PASSES - 1))
-            nc.scalar.activation(acts[h][:, row, :], acc[:], func)
-            return acts[h][:, row, :]
-
-        def gate(h, g, t):
-            def weights(a):
-                first = (a * PACK + t) * P * 2
-                return (wg_codes[g][:, first:first + 2 * P].bitcast(FP4X4), plane(a, WG0 + g * H + t * P, P))
-            return product(h, weights, ACT.Sigmoid, g * PACK + t, "gates", 5)
-
-        def candidate(h, t):
-            def weights(a):
-                return (wu_codes[a][:, t * P:(t + 1) * P].bitcast(FP8X4), wu_scales[a][:, t * P:(t + 1) * P])
-            return product(h, weights, ACT.Tanh, 2 * PACK + t, "cands", 3)
+            act = acts[h][:, kind * PACK + t, :]
+            nc.scalar.activation(act, acc[:], TANH if kind == CANDIDATE else SIGMOID)
+            return act
 
         quantised = []
         for h in range(HALVES):
@@ -149,39 +154,42 @@ def tile_list_term_tree_cell_kernel(tc, tab_words, tab_scales, offs, wg_words, w
             fresh = work.tile([P, PACK, COLS], F32, name="fresh")
 
             def make_fresh(t):
-                admit, cand = gate(h, 0, t), candidate(h, t)
-                nc.vector.scalar_tensor_tensor(fresh[:, t, :], admit, gains[:, t:t + 1], cand, MULT, MULT)
+                admit, candidate = first_stage(h, INPUT, t), first_stage(h, CANDIDATE, t)
+                nc.vector.scalar_tensor_tensor(fresh[:, t, :], admit, gains[:, t:t + 1], candidate, MULT, MULT)
 
             def make_kept(t):
-                forget = gate(h, 1, t)
-                parts = 2 if t == PACK - 1 else 1
-                for c in range(parts):
-                    cols = slice(c * COLS // parts, (c + 1) * COLS // parts)
+                forget = first_stage(h, FORGET, t)
+                width = COLS // 2 if t == PACK - 1 else COLS
+                for first in range(0, COLS, width):
+                    cols = slice(first, first + width)
                     nc.vector.scalar_tensor_tensor(kept[:, t, cols], forget[:, cols], gains[:, t:t + 1],
                                                    cells[:, t, h * COLS:(h + 1) * COLS][:, cols], MULT, MULT)
 
-            for t in range(PACK):
-                make_fresh(t)
-                if h > 0:
-                    make_kept(t)
-            for t in range(PACK if h == 0 else 0):
-                make_kept(t)
-
             def add(first, width):
                 cols = slice(first, first + width)
-                h_bf = work.tile([P, width, PACK], BF16, name="h_bf", align_bytes=64, bufs=3)
+                h_bf = work.tile([P, width, PACK], BF16, name="h_bf", align_bytes=ALIGN, bufs=len(CHUNKS[-1]))
                 nc.vector.tensor_tensor(h_bf[:].rearrange("p (c i) t -> p c t i", i=2),
                                         fresh[:, :, cols].rearrange("p t (c i) -> p c t i", i=2),
                                         kept[:, :, cols].rearrange("p t (c i) -> p c t i", i=2), ADD)
                 return h_bf
 
             def quantise(first, width, h_bf):
-                h_codes = work.tile([P, width], U32, name="h_codes", align_bytes=64, bufs=5)
-                h_scales = work.tile([P, width], U8, name="h_scales", align_bytes=64, bufs=5)
+                h_codes = work.tile([P, width], U32, name="h_codes", align_bytes=ALIGN, bufs=ALL_CHUNKS)
+                h_scales = work.tile([P, width], U8, name="h_scales", align_bytes=ALIGN, bufs=ALL_CHUNKS)
                 nc.vector.quantize_mx(h_codes[:].bitcast(FP8X4), h_scales[:], h_bf[:].rearrange("p j t -> p (j t)"))
                 quantised.append((h * COLS + first, width, h_codes, h_scales))
 
-            chunks = ((0, 256), (256, 256)) if h == 0 else ((0, 256), (256, 128), (384, 128))
+            if h == 0:
+                for t in range(PACK):
+                    make_fresh(t)
+                for t in range(PACK):
+                    make_kept(t)
+            else:
+                for t in range(PACK):
+                    make_fresh(t)
+                    make_kept(t)
+
+            chunks = CHUNKS[h]
             sums = [add(*chunks[0])]
             for c, chunk in enumerate(chunks):
                 if c + 1 < len(chunks):
@@ -189,11 +197,11 @@ def tile_list_term_tree_cell_kernel(tc, tab_words, tab_scales, offs, wg_words, w
                 quantise(*chunk, sums[c])
 
         for first, width, h_codes, h_scales in quantised:
-            acc = psum.tile([P, N // P, width], F32, name="acc", tag="gates", bufs=5)
+            acc = psum.tile([P, N // P, width], F32, name="acc", tag="gates", bufs=GATE_BANKS)
             for n in range(N // P):
                 nc.tensor.matmul_mx(acc[:, n, :], lhsT=wo_codes[:, n * P:(n + 1) * P].bitcast(FP8X4),
-                                    lhsT_scale=plane(n, WO0, P), rhs=h_codes[:].bitcast(FP8X4),
+                                    lhsT_scale=plane(n, WO_SCALES, P), rhs=h_codes[:].bitcast(FP8X4),
                                     rhs_scale=h_scales[:], start=True, stop=True)
-            result = work.tile([P, N // P, width], F32, name="result", bufs=5)
+            result = work.tile([P, N // P, width], F32, name="result", bufs=ALL_CHUNKS)
             nc.scalar.copy(result[:], acc[:])
             nc.sync.dma_start(out[:, first:first + width].rearrange("(n p) j -> p n j", p=P), result[:])

@@ -32,18 +32,21 @@ WG_SCALES = S
 WO_SCALES = WG_SCALES + 2 * H
 PLANE = WO_SCALES + P
 
-GATE_BANKS, CANDIDATE_BANKS = 5, 3
+BANKS = 4
+OUT_BANKS = 8 - BANKS
+WG_HALF = PASSES * H * 2
 
-CHUNKS = (((0, 256), (256, 256)), ((0, 256), (256, 128), (384, 128)))
+CHUNKS = (((0, 512),), ((0, 256), (256, 128), (384, 128)))
 ALL_CHUNKS = sum(len(chunks) for chunks in CHUNKS)
 
 
 def tile_list_term_tree_cell_kernel(tc, tab_words, tab_scales, offs, wg_words, wg_scales, wu, cell, gain,
-                                             wo_words, wo_scales, out):
+                                                 wo_words, wo_scales, out):
     nc = tc.nc
     with ExitStack() as ctx:
         keep = ctx.enter_context(tc.tile_pool(name="keep", bufs=1))
         work = ctx.enter_context(tc.tile_pool(name="work", bufs=2))
+        early = ctx.enter_context(tc.tile_pool(name="early", bufs=1))
         psum = ctx.enter_context(tc.psum_pool(name="psum", bufs=1))
 
         offsets = keep.tile([P, S // GROUP], U16, name="offsets")
@@ -67,15 +70,24 @@ def tile_list_term_tree_cell_kernel(tc, tab_words, tab_scales, offs, wg_words, w
         wo_codes = keep.tile([P, N], I32, name="wo_codes", align_bytes=ALIGN)
         nc.sync.dma_start(wo_codes[:], wo_words[0].rearrange("p c i -> p (c i)").bitcast(I32))
 
-        wg_raw = keep.tile([P, PASSES * 2 * H * 2], U8, name="wg_raw", tag="wg_raw", align_bytes=ALIGN)
-        nc.sync.dma_start(wg_raw[:].bitcast(I32).rearrange("p (a c) -> p a c", a=PASSES),
-                          wg_words.bitcast(I32).rearrange("a p c -> p a c"))
-        table = []
-        for a in range(PASSES):
-            table.append(keep.tile([P, T], I32, name=f"table{a}", tag=f"table{a}", align_bytes=ALIGN))
-            nc.sync.dma_start(table[a][:], tab_words[a].rearrange("p t i -> p (t i)").bitcast(I32))
+        def load_table(a, tag):
+            words = keep.tile([P, T], I32, name=f"table{a}", tag=tag, align_bytes=ALIGN)
+            nc.sync.dma_start(words[:], tab_words[a].rearrange("p t i -> p (t i)").bitcast(I32))
+            return words
 
-        picked_rows = keep.tile([P, S], U8, name="picked_rows", tag="picked_rows", align_bytes=ALIGN)
+        def load_wu(a, rows):
+            nc.sync.dma_start(rows[:], wu[a * P * PACK:(a + 1) * P * PACK, :].rearrange("(p i) r -> p i r", i=PACK))
+            return rows
+
+        def load_wg(g, words):
+            nc.sync.dma_start(words[:], wg_words.bitcast(I32).rearrange("a p (g c) -> g p a c", g=2)[g])
+            return words
+
+        table = [load_table(0, "table0")]
+        wg_raw = [load_wg(INPUT, keep.tile([P, PASSES, H // 2], I32, name="wg_raw0", tag="wg_raw0", align_bytes=ALIGN))]
+        table.append(load_table(1, "table1"))
+
+        picked_rows = early.tile([P, S], U8, name="picked_rows", align_bytes=ALIGN, offset=WG_HALF - S // 2)
         nc.vector.tensor_copy(picked_rows[:], tab_rows[:].indirect(offsets[:]))
         nc.vector.tensor_copy(staged[:, WG_SCALES:WO_SCALES].rearrange("p (g t m) -> p g t m", g=2, t=PACK),
                               wg_rows[:].rearrange("p (g m t) -> p g t m", g=2, t=PACK))
@@ -84,56 +96,67 @@ def tile_list_term_tree_cell_kernel(tc, tab_words, tab_scales, offs, wg_words, w
             first = QUADRANT * d
             nc.sync.dma_start(planes[first:first + 4, :].bitcast(I32),
                               staged[first:first + QUADRANT:4, :].bitcast(I32))
+        wg_raw.append(load_wg(FORGET, early.tile([P, PASSES, H // 2], I32, name="wg_raw1", align_bytes=ALIGN, offset=0)))
+        wu_raw = [load_wu(0, early.tile([P, PACK, H], F32, name="wu_raw0", align_bytes=ALIGN, offset=WG_HALF))]
 
         def plane(a, first, width):
             return planes[:, a * PLANE + first:a * PLANE + first + width]
 
-        wg_in = wg_raw[:].bitcast(U16).rearrange("p (a g m t) -> p g a t m", a=PASSES, g=2, t=PACK)
-        wg_codes = [keep.tile([P, PASSES * H * 2], U8, name=f"wg_codes{g}", tag=tag, align_bytes=ALIGN)
-                    for g, tag in enumerate(("tab_rows", "wg_rows"))]
-        for g in (INPUT, FORGET):
-            nc.vector.tensor_copy(wg_codes[g][:].bitcast(U16).rearrange("p (a t m) -> p a t m", a=PASSES, t=PACK),
-                                  wg_in[:, g])
+        wg_codes = [keep.tile([P, PASSES * H * 2], U8, name=f"wg_codes{g}", align_bytes=ALIGN) for g in (INPUT, FORGET)]
 
-        wu_raw = []
-        for a, tag in enumerate(("picked_rows", "wg_raw")):
-            wu_raw.append(keep.tile([P, PACK, H], F32, name=f"wu_raw{a}", tag=tag, align_bytes=ALIGN))
-            nc.sync.dma_start(wu_raw[a][:],
-                              wu[a * P * PACK:(a + 1) * P * PACK, :].rearrange("(p i) r -> p i r", i=PACK))
+        def deal_wg(g):
+            nc.vector.tensor_copy(wg_codes[g][:].bitcast(U16).rearrange("p (a t m) -> p a t m", a=PASSES, t=PACK),
+                                  wg_raw[g][:].rearrange("p a c -> p (a c)").bitcast(U16).rearrange("p (a m t) -> p a t m", a=PASSES, t=PACK))
 
         states = {}
-        for h in range(HALVES):
-            entries = offsets[:, h * COLS // GROUP:(h + 1) * COLS // GROUP]
-            for a in range(PASSES):
-                tag = "staged" if (a, h) == (0, 1) else f"states{a}{h}"
-                states[a, h] = keep.tile([P, COLS], U32, name=f"states{a}{h}", tag=tag, align_bytes=ALIGN)
-                nc.vector.tensor_copy(states[a, h][:], table[a][:].bitcast(U32).indirect(entries))
 
-        cells = keep.tile([P, PACK, S], F32, name="cells", tag="table1", align_bytes=ALIGN)
-        for t in range(PACK):
-            nc.sync.dma_start(cells[:, t, :], cell.rearrange("(p t) j -> p t j", t=PACK)[:, t, :])
+        def gather(a, h):
+            states[a, h] = keep.tile([P, COLS], U32, name=f"states{a}{h}", align_bytes=ALIGN)
+            nc.vector.tensor_copy(states[a, h][:], table[a][:].bitcast(U32).indirect(
+                offsets[:, h * COLS // GROUP:(h + 1) * COLS // GROUP]))
+
+        gather(0, 0)
+        deal_wg(INPUT)
+        wu_raw.append(load_wu(1, keep.tile([P, PACK, H], F32, name="wu_raw1", tag="wg_raw0", align_bytes=ALIGN)))
+        gather(0, 1)
+        gather(1, 0)
+        deal_wg(FORGET)
+        gather(1, 1)
 
         wu_codes, wu_scales = [], []
-        for a in range(PASSES):
+
+        def round_wu(a, on_vector):
             wu_bf = keep.tile([P, PACK, P, PACK], BF16, name=f"wu_bf{a}", tag=f"wu_bf{a}", align_bytes=ALIGN)
             wu_codes.append(keep.tile([P, H], U32, name=f"wu_codes{a}", align_bytes=ALIGN))
             wu_scales.append(keep.tile([P, H], U8, name=f"wu_scales{a}", align_bytes=ALIGN))
             wu_in = wu_raw[a][:].rearrange("p i (m t) -> p m i t", t=PACK)
-            for t, copy in ((0, nc.vector.tensor_copy), (2, nc.scalar.copy)):
-                copy(wu_bf[:, t:t + 2].rearrange("p t m i -> p m i t"), wu_in[:, :, :, t:t + 2])
-            for t in (0, 2):
-                cols = slice(t * P, (t + 2) * P)
+            wu_out = wu_bf[:].rearrange("p t m i -> p m i t")
+            nc.vector.tensor_copy(wu_out[:, :, :, 0:2], wu_in[:, :, :, 0:2])
+            nc.vector.tensor_copy(wu_out[:, :on_vector, :, 2:4], wu_in[:, :on_vector, :, 2:4])
+            if on_vector < P:
+                nc.scalar.copy(wu_out[:, on_vector:, :, 2:4], wu_in[:, on_vector:, :, 2:4])
+            step = 2 if a else PACK
+            for t in range(0, PACK, step):
+                cols = slice(t * P, (t + step) * P)
                 nc.vector.quantize_mx(wu_codes[a][:, cols].bitcast(FP8X4), wu_scales[a][:, cols],
-                                      wu_bf[:, t:t + 2].rearrange("p t m i -> p (t m i)"))
+                                      wu_bf[:, t:t + step].rearrange("p t m i -> p (t m i)"))
+
+        round_wu(0, P)
+        round_wu(1, 64)
+
+        cells = keep.tile([P, HALVES, PACK, COLS], F32, name="cells", tag="table0", align_bytes=ALIGN)
+        for h in range(HALVES):
+            for t in (0, 2):
+                nc.sync.dma_start(cells[:, h, t:t + 2, :],
+                                  cell.rearrange("(p t) j -> p t j", t=PACK)[:, t:t + 2, h * COLS:(h + 1) * COLS])
 
         acts = [keep.tile([P, 3 * PACK, COLS], F32, name=f"acts{h}", tag=tag, align_bytes=ALIGN)
-                for h, tag in enumerate(("acts0", "wu_bf1"))]
+                for h, tag in enumerate(("acts0", "acts1"))]
+
+        late_gates = keep.tile([P, PACK, COLS], F32, name="late_gates", tag="wg_raw0", align_bytes=ALIGN)
 
         def first_stage(h, kind, t):
-            if kind == CANDIDATE:
-                acc = psum.tile([P, COLS], F32, name="acc", tag="candidates", bufs=CANDIDATE_BANKS)
-            else:
-                acc = psum.tile([P, COLS], F32, name="acc", tag="gates", bufs=GATE_BANKS)
+            acc = psum.tile([P, COLS], F32, name="acc", tag="banks", bufs=BANKS)
             for a in range(PASSES):
                 if kind == CANDIDATE:
                     codes = wu_codes[a][:, t * P:(t + 1) * P].bitcast(FP8X4)
@@ -142,9 +165,13 @@ def tile_list_term_tree_cell_kernel(tc, tab_words, tab_scales, offs, wg_words, w
                     first = (a * PACK + t) * P * 2
                     codes = wg_codes[kind][:, first:first + P * 2].bitcast(FP4X4)
                     scales = plane(a, WG_SCALES + kind * H + t * P, P)
-                nc.tensor.matmul_mx(acc[:], lhsT=codes, lhsT_scale=scales, rhs=states[a, h][:].bitcast(FP8X4),
+                words = states[a, h][:]
+                nc.tensor.matmul_mx(acc[:], lhsT=codes, lhsT_scale=scales, rhs=words.bitcast(FP8X4),
                                     rhs_scale=plane(a, h * COLS, COLS), start=(a == 0), stop=(a == PASSES - 1))
-            act = acts[h][:, kind * PACK + t, :]
+            if h == 0 and kind != CANDIDATE and t >= 2:
+                act = late_gates[:, 2 * kind + t - 2, :]
+            else:
+                act = acts[h][:, kind * PACK + t, :]
             nc.scalar.activation(act, acc[:], TANH if kind == CANDIDATE else SIGMOID)
             return act
 
@@ -153,21 +180,20 @@ def tile_list_term_tree_cell_kernel(tc, tab_words, tab_scales, offs, wg_words, w
             kept = work.tile([P, PACK, COLS], F32, name="kept")
             fresh = work.tile([P, PACK, COLS], F32, name="fresh")
 
-            def make_fresh(t):
-                admit, candidate = first_stage(h, INPUT, t), first_stage(h, CANDIDATE, t)
-                nc.vector.scalar_tensor_tensor(fresh[:, t, :], admit, gains[:, t:t + 1], candidate, MULT, MULT)
+            made = {}
 
-            def make_kept(t):
-                forget = first_stage(h, FORGET, t)
-                width = COLS // 2 if t == PACK - 1 else COLS
-                for first in range(0, COLS, width):
-                    cols = slice(first, first + width)
-                    nc.vector.scalar_tensor_tensor(kept[:, t, cols], forget[:, cols], gains[:, t:t + 1],
-                                                   cells[:, t, h * COLS:(h + 1) * COLS][:, cols], MULT, MULT)
+            def products(kind, t):
+                made[kind, t] = first_stage(h, kind, t)
+                if kind == FORGET:
+                    nc.vector.scalar_tensor_tensor(kept[:, t, :], made[FORGET, t], gains[:, t:t + 1],
+                                                   cells[:, h, t, :], MULT, MULT)
+                elif (INPUT, t) in made and (CANDIDATE, t) in made:
+                    nc.vector.scalar_tensor_tensor(fresh[:, t, :], made[INPUT, t], gains[:, t:t + 1],
+                                                   made[CANDIDATE, t], MULT, MULT)
 
             def add(first, width):
                 cols = slice(first, first + width)
-                h_bf = work.tile([P, width, PACK], BF16, name="h_bf", align_bytes=ALIGN, bufs=len(CHUNKS[-1]))
+                h_bf = work.tile([P, width, PACK], BF16, name="h_bf", align_bytes=ALIGN, bufs=ALL_CHUNKS)
                 nc.vector.tensor_tensor(h_bf[:].rearrange("p (c i) t -> p c t i", i=2),
                                         fresh[:, :, cols].rearrange("p t (c i) -> p c t i", i=2),
                                         kept[:, :, cols].rearrange("p t (c i) -> p c t i", i=2), ADD)
@@ -177,17 +203,16 @@ def tile_list_term_tree_cell_kernel(tc, tab_words, tab_scales, offs, wg_words, w
                 h_codes = work.tile([P, width], U32, name="h_codes", align_bytes=ALIGN, bufs=ALL_CHUNKS)
                 h_scales = work.tile([P, width], U8, name="h_scales", align_bytes=ALIGN, bufs=ALL_CHUNKS)
                 nc.vector.quantize_mx(h_codes[:].bitcast(FP8X4), h_scales[:], h_bf[:].rearrange("p j t -> p (j t)"))
-                quantised.append((h * COLS + first, width, h_codes, h_scales))
+                for lo in range(0, width, 256):
+                    cols = slice(lo, min(lo + 256, width))
+                    quantised.append((h * COLS + first + lo, cols.stop - lo, h_codes[:, cols], h_scales[:, cols]))
 
             if h == 0:
-                for t in range(PACK):
-                    make_fresh(t)
-                for t in range(PACK):
-                    make_kept(t)
+                order = [(INPUT, 0), (INPUT, 1), (FORGET, 0), (FORGET, 1), (FORGET, 2), (FORGET, 3), (INPUT, 2), (CANDIDATE, 0), (INPUT, 3), (CANDIDATE, 1), (CANDIDATE, 2), (CANDIDATE, 3)]
             else:
-                for t in range(PACK):
-                    make_fresh(t)
-                    make_kept(t)
+                order = [(kind, t) for t in range(PACK) for kind in (INPUT, CANDIDATE, FORGET)]
+            for kind, t in order:
+                products(kind, t)
 
             chunks = CHUNKS[h]
             sums = [add(*chunks[0])]
@@ -197,11 +222,11 @@ def tile_list_term_tree_cell_kernel(tc, tab_words, tab_scales, offs, wg_words, w
                 quantise(*chunk, sums[c])
 
         for first, width, h_codes, h_scales in quantised:
-            acc = psum.tile([P, N // P, width], F32, name="acc", tag="gates", bufs=GATE_BANKS)
+            acc = psum.tile([P, N // P, width], F32, name="acc", tag="out_banks", bufs=OUT_BANKS)
             for n in range(N // P):
                 nc.tensor.matmul_mx(acc[:, n, :], lhsT=wo_codes[:, n * P:(n + 1) * P].bitcast(FP8X4),
-                                    lhsT_scale=plane(n, WO_SCALES, P), rhs=h_codes[:].bitcast(FP8X4),
-                                    rhs_scale=h_scales[:], start=True, stop=True)
-            result = work.tile([P, N // P, width], F32, name="result", bufs=ALL_CHUNKS)
+                                    lhsT_scale=plane(n, WO_SCALES, P), rhs=h_codes.bitcast(FP8X4),
+                                    rhs_scale=h_scales, start=True, stop=True)
+            result = work.tile([P, N // P, width], F32, name="result", bufs=5)
             nc.scalar.copy(result[:], acc[:])
             nc.sync.dma_start(out[:, first:first + width].rearrange("(n p) j -> p n j", p=P), result[:])

@@ -33,7 +33,7 @@ WO_SCALES = WG_SCALES + 2 * H
 PLANE = WO_SCALES + P
 
 BANKS = 4
-OUT_BANKS = 8 - BANKS
+ZEROED_BY_VECTOR = 3 * T // 4
 WG_HALF = PASSES * H * 2
 
 CHUNKS = (((0, 512),), ((0, 256), (256, 128), (384, 128)))
@@ -56,19 +56,14 @@ def tile_list_term_tree_cell_kernel(tc, tab_words, tab_scales, offs, wg_words, w
         wg_rows = keep.tile([P, 2 * H], U8, name="wg_rows", tag="wg_rows", align_bytes=ALIGN)
         staged = keep.tile([P, PLANE], U8, name="staged", tag="staged", align_bytes=ALIGN)
         planes = keep.tile([P, PASSES * PLANE], U8, name="planes", align_bytes=ALIGN)
-        nc.vector.memset(tab_rows[:].bitcast(I32), 0)
-        nc.vector.memset(wg_rows[:].bitcast(I32), 0)
+        nc.vector.memset(tab_rows[:, :ZEROED_BY_VECTOR].bitcast(I32), 0)
+        nc.gpsimd.memset(tab_rows[:, ZEROED_BY_VECTOR:].bitcast(I32), 0)
+        nc.gpsimd.memset(wg_rows[:].bitcast(I32), 0)
         nc.vector.memset(planes[:].bitcast(I32), 0)
         nc.sync.dma_start(tab_rows[0:P:4, :].bitcast(I32), tab_scales.bitcast(I32).rearrange("a q t -> q a t"))
         nc.sync.dma_start(wg_rows[0:P:4, :].bitcast(I32), wg_scales.bitcast(I32).rearrange("a q c -> q a c"))
         nc.sync.dma_start(staged[0:P:4, WO_SCALES:].bitcast(I32),
                           wo_scales[0].bitcast(I32).rearrange("q (n c) -> (q n) c", n=N // P))
-
-        gains = keep.tile([P, PACK], F32, name="gains")
-        nc.sync.dma_start(gains[:], gain.rearrange("(p t) -> p t", t=PACK))
-
-        wo_codes = keep.tile([P, N], I32, name="wo_codes", align_bytes=ALIGN)
-        nc.sync.dma_start(wo_codes[:], wo_words[0].rearrange("p c i -> p (c i)").bitcast(I32))
 
         def load_table(a, tag):
             words = keep.tile([P, T], I32, name=f"table{a}", tag=tag, align_bytes=ALIGN)
@@ -86,6 +81,9 @@ def tile_list_term_tree_cell_kernel(tc, tab_words, tab_scales, offs, wg_words, w
         table = [load_table(0, "table0")]
         wg_raw = [load_wg(INPUT, keep.tile([P, PASSES, H // 2], I32, name="wg_raw0", tag="wg_raw0", align_bytes=ALIGN))]
         table.append(load_table(1, "table1"))
+        gains = keep.tile([P, PACK], F32, name="gains")
+        nc.sync.dma_start(gains[:], gain.rearrange("(p t) -> p t", t=PACK))
+
 
         picked_rows = early.tile([P, S], U8, name="picked_rows", align_bytes=ALIGN, offset=WG_HALF - S // 2)
         nc.vector.tensor_copy(picked_rows[:], tab_rows[:].indirect(offsets[:]))
@@ -125,24 +123,21 @@ def tile_list_term_tree_cell_kernel(tc, tab_words, tab_scales, offs, wg_words, w
 
         wu_codes, wu_scales = [], []
 
-        def round_wu(a, on_vector):
+        def round_wu(a):
             wu_bf = keep.tile([P, PACK, P, PACK], BF16, name=f"wu_bf{a}", tag=f"wu_bf{a}", align_bytes=ALIGN)
             wu_codes.append(keep.tile([P, H], U32, name=f"wu_codes{a}", align_bytes=ALIGN))
             wu_scales.append(keep.tile([P, H], U8, name=f"wu_scales{a}", align_bytes=ALIGN))
             wu_in = wu_raw[a][:].rearrange("p i (m t) -> p m i t", t=PACK)
-            wu_out = wu_bf[:].rearrange("p t m i -> p m i t")
-            nc.vector.tensor_copy(wu_out[:, :, :, 0:2], wu_in[:, :, :, 0:2])
-            nc.vector.tensor_copy(wu_out[:, :on_vector, :, 2:4], wu_in[:, :on_vector, :, 2:4])
-            if on_vector < P:
-                nc.scalar.copy(wu_out[:, on_vector:, :, 2:4], wu_in[:, on_vector:, :, 2:4])
+            for t in (0, 2):
+                nc.vector.tensor_copy(wu_bf[:, t:t + 2].rearrange("p t m i -> p m i t"), wu_in[:, :, :, t:t + 2])
             step = 2 if a else PACK
             for t in range(0, PACK, step):
                 cols = slice(t * P, (t + step) * P)
                 nc.vector.quantize_mx(wu_codes[a][:, cols].bitcast(FP8X4), wu_scales[a][:, cols],
                                       wu_bf[:, t:t + step].rearrange("p t m i -> p (t m i)"))
 
-        round_wu(0, P)
-        round_wu(1, 64)
+        round_wu(0)
+        round_wu(1)
 
         cells = keep.tile([P, HALVES, PACK, COLS], F32, name="cells", tag="table0", align_bytes=ALIGN)
         for h in range(HALVES):
@@ -150,14 +145,16 @@ def tile_list_term_tree_cell_kernel(tc, tab_words, tab_scales, offs, wg_words, w
                 nc.sync.dma_start(cells[:, h, t:t + 2, :],
                                   cell.rearrange("(p t) j -> p t j", t=PACK)[:, t:t + 2, h * COLS:(h + 1) * COLS])
 
+        wo_codes = keep.tile([P, N], I32, name="wo_codes", tag="table1", align_bytes=ALIGN)
+        nc.sync.dma_start(wo_codes[:], wo_words[0].rearrange("p c i -> p (c i)").bitcast(I32))
+
         acts = [keep.tile([P, 3 * PACK, COLS], F32, name=f"acts{h}", tag=tag, align_bytes=ALIGN)
                 for h, tag in enumerate(("acts0", "acts1"))]
 
-        late_gates = keep.tile([P, PACK, COLS], F32, name="late_gates", tag="wg_raw0", align_bytes=ALIGN)
-
         def first_stage(h, kind, t):
             acc = psum.tile([P, COLS], F32, name="acc", tag="banks", bufs=BANKS)
-            for a in range(PASSES):
+            order = range(PASSES)[::-1] if kind == CANDIDATE else range(PASSES)
+            for a in order:
                 if kind == CANDIDATE:
                     codes = wu_codes[a][:, t * P:(t + 1) * P].bitcast(FP8X4)
                     scales = wu_scales[a][:, t * P:(t + 1) * P]
@@ -167,11 +164,8 @@ def tile_list_term_tree_cell_kernel(tc, tab_words, tab_scales, offs, wg_words, w
                     scales = plane(a, WG_SCALES + kind * H + t * P, P)
                 words = states[a, h][:]
                 nc.tensor.matmul_mx(acc[:], lhsT=codes, lhsT_scale=scales, rhs=words.bitcast(FP8X4),
-                                    rhs_scale=plane(a, h * COLS, COLS), start=(a == 0), stop=(a == PASSES - 1))
-            if h == 0 and kind != CANDIDATE and t >= 2:
-                act = late_gates[:, 2 * kind + t - 2, :]
-            else:
-                act = acts[h][:, kind * PACK + t, :]
+                                    rhs_scale=plane(a, h * COLS, COLS), start=(a == order[0]), stop=(a == order[-1]))
+            act = acts[h][:, kind * PACK + t, :]
             nc.scalar.activation(act, acc[:], TANH if kind == CANDIDATE else SIGMOID)
             return act
 
@@ -208,7 +202,7 @@ def tile_list_term_tree_cell_kernel(tc, tab_words, tab_scales, offs, wg_words, w
                     quantised.append((h * COLS + first + lo, cols.stop - lo, h_codes[:, cols], h_scales[:, cols]))
 
             if h == 0:
-                order = [(INPUT, 0), (INPUT, 1), (FORGET, 0), (FORGET, 1), (FORGET, 2), (FORGET, 3), (INPUT, 2), (CANDIDATE, 0), (INPUT, 3), (CANDIDATE, 1), (CANDIDATE, 2), (CANDIDATE, 3)]
+                order = [(INPUT, 0), (INPUT, 1), (INPUT, 2), (INPUT, 3), (FORGET, 0), (FORGET, 1), (FORGET, 2), (FORGET, 3), (CANDIDATE, 0), (CANDIDATE, 1), (CANDIDATE, 2), (CANDIDATE, 3)]
             else:
                 order = [(kind, t) for t in range(PACK) for kind in (INPUT, CANDIDATE, FORGET)]
             for kind, t in order:
@@ -222,11 +216,12 @@ def tile_list_term_tree_cell_kernel(tc, tab_words, tab_scales, offs, wg_words, w
                 quantise(*chunk, sums[c])
 
         for first, width, h_codes, h_scales in quantised:
-            acc = psum.tile([P, N // P, width], F32, name="acc", tag="out_banks", bufs=OUT_BANKS)
+            acc = psum.tile([P, N // P, width], F32, name="acc", tag="banks", bufs=BANKS)
             for n in range(N // P):
                 nc.tensor.matmul_mx(acc[:, n, :], lhsT=wo_codes[:, n * P:(n + 1) * P].bitcast(FP8X4),
                                     lhsT_scale=plane(n, WO_SCALES, P), rhs=h_codes.bitcast(FP8X4),
                                     rhs_scale=h_scales, start=True, stop=True)
             result = work.tile([P, N // P, width], F32, name="result", bufs=5)
             nc.scalar.copy(result[:], acc[:])
-            nc.sync.dma_start(out[:, first:first + width].rearrange("(n p) j -> p n j", p=P), result[:])
+            queue = nc.scalar if first + width == S else nc.sync
+            queue.dma_start(out[:, first:first + width].rearrange("(n p) j -> p n j", p=P), result[:])

@@ -1,6 +1,7 @@
 from contextlib import ExitStack
 
 import concourse.mybir as mybir
+from concourse.masks import make_identity
 
 K, T, S, H, N = 1024, 2048, 1024, 512, 256
 FLOPS = 2 * K * 3 * H * S + 2 * H * N * S
@@ -36,16 +37,12 @@ BANKS = 4
 ZEROED_BY_VECTOR = 3 * T // 4
 WG_HALF = PASSES * H * 2
 
-CHUNKS = (((0, 512),), ((0, 256), (256, 128), (384, 128)))
-ALL_CHUNKS = sum(len(chunks) for chunks in CHUNKS)
-
 
 def tile_list_term_tree_cell_kernel(tc, tab_words, tab_scales, offs, wg_words, wg_scales, wu, cell, gain,
                                                  wo_words, wo_scales, out):
     nc = tc.nc
     with ExitStack() as ctx:
         keep = ctx.enter_context(tc.tile_pool(name="keep", bufs=1))
-        work = ctx.enter_context(tc.tile_pool(name="work", bufs=2))
         early = ctx.enter_context(tc.tile_pool(name="early", bufs=1))
         psum = ctx.enter_context(tc.psum_pool(name="psum", bufs=1))
 
@@ -169,59 +166,85 @@ def tile_list_term_tree_cell_kernel(tc, tab_words, tab_scales, offs, wg_words, w
             nc.scalar.activation(act, acc[:], TANH if kind == CANDIDATE else SIGMOID)
             return act
 
-        quantised = []
-        for h in range(HALVES):
-            kept = work.tile([P, PACK, COLS], F32, name="kept")
-            fresh = work.tile([P, PACK, COLS], F32, name="fresh")
+        identity = keep.tile([P, P], F32, name="identity")
+        make_identity(nc, identity[:])
 
+        kept = [keep.tile([P, PACK, COLS], F32, name=f"kept{h}") for h in range(HALVES)]
+        fresh = [keep.tile([P, PACK, COLS], F32, name=f"fresh{h}") for h in range(HALVES)]
+
+        def products(h, order):
             made = {}
-
-            def products(kind, t):
+            for kind, t in order:
                 made[kind, t] = first_stage(h, kind, t)
                 if kind == FORGET:
-                    nc.vector.scalar_tensor_tensor(kept[:, t, :], made[FORGET, t], gains[:, t:t + 1],
+                    nc.vector.scalar_tensor_tensor(kept[h][:, t, :], made[FORGET, t], gains[:, t:t + 1],
                                                    cells[:, h, t, :], MULT, MULT)
-                elif (INPUT, t) in made and (CANDIDATE, t) in made:
-                    nc.vector.scalar_tensor_tensor(fresh[:, t, :], made[INPUT, t], gains[:, t:t + 1],
+                elif kind == CANDIDATE:
+                    nc.vector.scalar_tensor_tensor(fresh[h][:, t, :], made[INPUT, t], gains[:, t:t + 1],
                                                    made[CANDIDATE, t], MULT, MULT)
 
-            def add(first, width):
-                cols = slice(first, first + width)
-                h_bf = work.tile([P, width, PACK], BF16, name="h_bf", align_bytes=ALIGN, bufs=ALL_CHUNKS)
-                nc.vector.tensor_tensor(h_bf[:].rearrange("p (c i) t -> p c t i", i=2),
-                                        fresh[:, :, cols].rearrange("p t (c i) -> p c t i", i=2),
-                                        kept[:, :, cols].rearrange("p t (c i) -> p c t i", i=2), ADD)
-                return h_bf
+        def rounded(first, width):
+            return keep.tile([P, width, PACK], BF16, name=f"h_bf{first}", align_bytes=ALIGN)
 
-            def quantise(first, width, h_bf):
-                h_codes = work.tile([P, width], U32, name="h_codes", align_bytes=ALIGN, bufs=ALL_CHUNKS)
-                h_scales = work.tile([P, width], U8, name="h_scales", align_bytes=ALIGN, bufs=ALL_CHUNKS)
-                nc.vector.quantize_mx(h_codes[:].bitcast(FP8X4), h_scales[:], h_bf[:].rearrange("p j t -> p (j t)"))
-                for lo in range(0, width, 256):
-                    cols = slice(lo, min(lo + 256, width))
-                    quantised.append((h * COLS + first + lo, cols.stop - lo, h_codes[:, cols], h_scales[:, cols]))
+        def add(first, width):
+            h, cols = first // COLS, slice(first % COLS, first % COLS + width)
+            h_bf = rounded(first, width)
+            nc.vector.tensor_tensor(h_bf[:].rearrange("p (c i) t -> p c t i", i=2),
+                                    fresh[h][:, :, cols].rearrange("p t (c i) -> p c t i", i=2),
+                                    kept[h][:, :, cols].rearrange("p t (c i) -> p c t i", i=2), ADD)
+            return first, width, h_bf
 
-            if h == 0:
-                order = [(INPUT, 0), (INPUT, 1), (INPUT, 2), (INPUT, 3), (FORGET, 0), (FORGET, 1), (FORGET, 2), (FORGET, 3), (CANDIDATE, 0), (CANDIDATE, 1), (CANDIDATE, 2), (CANDIDATE, 3)]
-            else:
-                order = [(kind, t) for t in range(PACK) for kind in (INPUT, CANDIDATE, FORGET)]
-            for kind, t in order:
-                products(kind, t)
+        def add_turned(first):
+            h, cols = first // COLS, slice(first % COLS, first % COLS + P)
+            total = psum.tile([P, PACK, P], F32, name="total", tag="banks", bufs=BANKS)
+            for t in range(PACK):
+                for term, start in ((fresh[h], True), (kept[h], False)):
+                    nc.tensor.matmul(total[:, t, :], lhsT=term[:, t, cols], rhs=identity[:], is_transpose=True,
+                                     start=start, stop=not start)
+            turned = keep.tile([P, 2, P, 2], BF16, name=f"turned{first}", align_bytes=ALIGN)
+            nc.scalar.copy(turned[:], total[:].rearrange("j (u e) p -> j u p e", e=2))
+            return turned
 
-            chunks = CHUNKS[h]
-            sums = [add(*chunks[0])]
-            for c, chunk in enumerate(chunks):
-                if c + 1 < len(chunks):
-                    sums.append(add(*chunks[c + 1]))
-                quantise(*chunk, sums[c])
+        def turn_back(first, blocks):
+            words = psum.tile([P, len(blocks), 2, P], F32, name="words", tag="words", bufs=1)
+            for b, turned in enumerate(blocks):
+                pairs = turned[:].rearrange("j u p e -> j (u p e)").bitcast(F32)
+                for u in range(2):
+                    nc.tensor.transpose(words[:, b, u, :], pairs[:, u * P:(u + 1) * P], identity[:])
+            h_bf = rounded(first, len(blocks) * P)
+            pairs = h_bf[:].rearrange("p j t -> p (j t)").bitcast(F32)
+            nc.scalar.copy(pairs.rearrange("p (b j u) -> p b j u", b=len(blocks), u=2),
+                           words[:].rearrange("p b u j -> p b j u"))
+            return first, len(blocks) * P, h_bf
 
-        for first, width, h_codes, h_scales in quantised:
+        def quantise(first, width, h_bf):
+            h_codes = keep.tile([P, width], U32, name=f"h_codes{first}", align_bytes=ALIGN)
+            h_scales = keep.tile([P, width], U8, name=f"h_scales{first}", align_bytes=ALIGN)
+            nc.vector.quantize_mx(h_codes[:].bitcast(FP8X4), h_scales[:], h_bf[:].rearrange("p j t -> p (j t)"))
+            return first, width, h_codes, h_scales
+
+        def second_stage(chunk, copy, queue=nc.sync):
+            first, width, h_codes, h_scales = chunk
             acc = psum.tile([P, N // P, width], F32, name="acc", tag="banks", bufs=BANKS)
             for n in range(N // P):
                 nc.tensor.matmul_mx(acc[:, n, :], lhsT=wo_codes[:, n * P:(n + 1) * P].bitcast(FP8X4),
-                                    lhsT_scale=plane(n, WO_SCALES, P), rhs=h_codes.bitcast(FP8X4),
-                                    rhs_scale=h_scales, start=True, stop=True)
-            result = work.tile([P, N // P, width], F32, name="result", bufs=5)
-            nc.scalar.copy(result[:], acc[:])
-            queue = nc.scalar if first + width == S else nc.sync
+                                    lhsT_scale=plane(n, WO_SCALES, P), rhs=h_codes[:].bitcast(FP8X4),
+                                    rhs_scale=h_scales[:], start=True, stop=True)
+            result = keep.tile([P, N // P, width], F32, name=f"result{first}")
+            copy(result[:], acc[:])
             queue.dma_start(out[:, first:first + width].rearrange("(n p) j -> p n j", p=P), result[:])
+
+        products(0, [(kind, t) for kind in (INPUT, FORGET, CANDIDATE) for t in range(PACK)])
+        chunk_a = quantise(*add(0, 256))
+        products(1, [(kind, t) for t in range(PACK) for kind in (INPUT, CANDIDATE, FORGET)])
+        blocks = [add_turned(first) for first in (256, 384)]
+        second_stage(chunk_a, nc.scalar.copy)
+        sum_b = turn_back(256, blocks)
+        sum_c, sum_d = add(512, 256), add(768, 128)
+        chunk_c = quantise(*sum_c)
+        sum_e = add(896, 128)
+        chunk_b, chunk_d, chunk_e = quantise(*sum_b), quantise(*sum_d), quantise(*sum_e)
+        second_stage(chunk_c, nc.scalar.copy)
+        second_stage(chunk_b, nc.scalar.copy)
+        second_stage(chunk_d, nc.vector.tensor_copy)
+        second_stage(chunk_e, nc.vector.tensor_copy)

@@ -1,7 +1,6 @@
 from contextlib import ExitStack
 
 import concourse.mybir as mybir
-from concourse.masks import make_identity
 
 K, T, S, H, N = 1024, 2048, 1024, 512, 256
 FLOPS = 2 * K * 3 * H * S + 2 * H * N * S
@@ -24,18 +23,19 @@ PACK = 4
 PASSES = K // (P * PACK)
 GROUP = 16
 QUADRANT = 32
-COLS = 512
-HALVES = S // COLS
+BANK = 512
 INPUT, FORGET, CANDIDATE = 0, 1, 2
 ALIGN = 64
 
 WG_SCALES = S
 WO_SCALES = WG_SCALES + 2 * H
 PLANE = WO_SCALES + P
-
-BANKS = 4
-ZEROED_BY_VECTOR = 3 * T // 4
 WG_HALF = PASSES * H * 2
+WU_PASS = PACK * H * 4
+
+CHUNKS = ((0, 512), (512, 256), (768, 256))
+RING = 4
+ZEROED_BY_VECTOR = 3 * T // 4
 
 
 def tile_list_term_tree_cell_kernel(tc, tab_words, tab_scales, offs, wg_words, wg_scales, wu, cell, gain,
@@ -43,15 +43,15 @@ def tile_list_term_tree_cell_kernel(tc, tab_words, tab_scales, offs, wg_words, w
     nc = tc.nc
     with ExitStack() as ctx:
         keep = ctx.enter_context(tc.tile_pool(name="keep", bufs=1))
-        early = ctx.enter_context(tc.tile_pool(name="early", bufs=1))
+        shared = ctx.enter_context(tc.tile_pool(name="shared", bufs=1))
         psum = ctx.enter_context(tc.psum_pool(name="psum", bufs=1))
 
         offsets = keep.tile([P, S // GROUP], U16, name="offsets")
         nc.sync.dma_start(offsets[:], offs)
 
         tab_rows = keep.tile([P, T], U8, name="tab_rows", tag="tab_rows", align_bytes=ALIGN)
-        wg_rows = keep.tile([P, 2 * H], U8, name="wg_rows", tag="wg_rows", align_bytes=ALIGN)
-        staged = keep.tile([P, PLANE], U8, name="staged", tag="staged", align_bytes=ALIGN)
+        wg_rows = keep.tile([P, 2 * H], U8, name="wg_rows", align_bytes=ALIGN)
+        staged = keep.tile([P, PLANE], U8, name="staged", align_bytes=ALIGN)
         planes = keep.tile([P, PASSES * PLANE], U8, name="planes", align_bytes=ALIGN)
         nc.vector.memset(tab_rows[:, :ZEROED_BY_VECTOR].bitcast(I32), 0)
         nc.gpsimd.memset(tab_rows[:, ZEROED_BY_VECTOR:].bitcast(I32), 0)
@@ -62,27 +62,33 @@ def tile_list_term_tree_cell_kernel(tc, tab_words, tab_scales, offs, wg_words, w
         nc.sync.dma_start(staged[0:P:4, WO_SCALES:].bitcast(I32),
                           wo_scales[0].bitcast(I32).rearrange("q (n c) -> (q n) c", n=N // P))
 
-        def load_table(a, tag):
-            words = keep.tile([P, T], I32, name=f"table{a}", tag=tag, align_bytes=ALIGN)
-            nc.sync.dma_start(words[:], tab_words[a].rearrange("p t i -> p (t i)").bitcast(I32))
+        def load_table(a, queue):
+            words = keep.tile([P, T], I32, name=f"table{a}", tag=f"table{a}", align_bytes=ALIGN)
+            queue.dma_start(words[:], tab_words[a].rearrange("p t i -> p (t i)").bitcast(I32))
             return words
 
-        def load_wu(a, rows):
-            nc.sync.dma_start(rows[:], wu[a * P * PACK:(a + 1) * P * PACK, :].rearrange("(p i) r -> p i r", i=PACK))
-            return rows
-
-        def load_wg(g, words):
+        def load_wg(g, offset):
+            words = shared.tile([P, PASSES, H // 2], I32, name=f"wg_raw{g}", align_bytes=ALIGN, offset=offset)
             nc.sync.dma_start(words[:], wg_words.bitcast(I32).rearrange("a p (g c) -> g p a c", g=2)[g])
             return words
 
-        table = [load_table(0, "table0")]
-        wg_raw = [load_wg(INPUT, keep.tile([P, PASSES, H // 2], I32, name="wg_raw0", tag="wg_raw0", align_bytes=ALIGN))]
-        table.append(load_table(1, "table1"))
+        def load_wu(a, offset, parts):
+            rows = wu[a * P * PACK:(a + 1) * P * PACK, :].rearrange("(p i) r -> p i r", i=PACK)
+            width = H // parts
+            pieces = []
+            for part in range(parts):
+                pieces.append(shared.tile([P, PACK, width], F32, name=f"wu_raw{a}{part}", align_bytes=ALIGN,
+                                          offset=offset + part * WU_PASS // parts))
+                nc.sync.dma_start(pieces[part][:], rows[:, :, part * width:(part + 1) * width])
+            return pieces
+
+        wg_raw = [load_wg(INPUT, WG_HALF + WU_PASS + (WU_PASS - WG_HALF) // 2)]
+        table = [load_table(0, nc.sync)]
         gains = keep.tile([P, PACK], F32, name="gains")
         nc.sync.dma_start(gains[:], gain.rearrange("(p t) -> p t", t=PACK))
+        table.append(load_table(1, nc.sync))
 
-
-        picked_rows = early.tile([P, S], U8, name="picked_rows", align_bytes=ALIGN, offset=WG_HALF - S // 2)
+        picked_rows = shared.tile([P, S], U8, name="picked_rows", align_bytes=ALIGN, offset=WG_HALF - S // 2)
         nc.vector.tensor_copy(picked_rows[:], tab_rows[:].indirect(offsets[:]))
         nc.vector.tensor_copy(staged[:, WG_SCALES:WO_SCALES].rearrange("p (g t m) -> p g t m", g=2, t=PACK),
                               wg_rows[:].rearrange("p (g m t) -> p g t m", g=2, t=PACK))
@@ -91,131 +97,117 @@ def tile_list_term_tree_cell_kernel(tc, tab_words, tab_scales, offs, wg_words, w
             first = QUADRANT * d
             nc.sync.dma_start(planes[first:first + 4, :].bitcast(I32),
                               staged[first:first + QUADRANT:4, :].bitcast(I32))
-        wg_raw.append(load_wg(FORGET, early.tile([P, PASSES, H // 2], I32, name="wg_raw1", align_bytes=ALIGN, offset=0)))
-        wu_raw = [load_wu(0, early.tile([P, PACK, H], F32, name="wu_raw0", align_bytes=ALIGN, offset=WG_HALF))]
+        wg_raw.append(load_wg(FORGET, 0))
+        wu_raw = [load_wu(0, WG_HALF, 1)]
 
         def plane(a, first, width):
             return planes[:, a * PLANE + first:a * PLANE + first + width]
 
-        wg_codes = [keep.tile([P, PASSES * H * 2], U8, name=f"wg_codes{g}", align_bytes=ALIGN) for g in (INPUT, FORGET)]
+        wg_codes = [keep.tile([P, WG_HALF], U8, name=f"wg_codes{g}", align_bytes=ALIGN) for g in (INPUT, FORGET)]
 
         def deal_wg(g):
+            words = wg_raw[g][:].rearrange("p a c -> p (a c)").bitcast(U16)
             nc.vector.tensor_copy(wg_codes[g][:].bitcast(U16).rearrange("p (a t m) -> p a t m", a=PASSES, t=PACK),
-                                  wg_raw[g][:].rearrange("p a c -> p (a c)").bitcast(U16).rearrange("p (a m t) -> p a t m", a=PASSES, t=PACK))
+                                  words.rearrange("p (a m t) -> p a t m", a=PASSES, t=PACK))
 
         states = {}
 
-        def gather(a, h):
-            states[a, h] = keep.tile([P, COLS], U32, name=f"states{a}{h}", align_bytes=ALIGN)
-            nc.vector.tensor_copy(states[a, h][:], table[a][:].bitcast(U32).indirect(
-                offsets[:, h * COLS // GROUP:(h + 1) * COLS // GROUP]))
+        def gather(a, half):
+            tag = f"states{a}{half}"
+            states[a, half] = keep.tile([P, BANK], U32, name=f"states{a}{half}", tag=tag, align_bytes=ALIGN)
+            entries = offsets[:, half * BANK // GROUP:(half + 1) * BANK // GROUP]
+            nc.vector.tensor_copy(states[a, half][:], table[a][:].bitcast(U32).indirect(entries))
 
-        gather(0, 0)
         deal_wg(INPUT)
-        wu_raw.append(load_wu(1, keep.tile([P, PACK, H], F32, name="wu_raw1", tag="wg_raw0", align_bytes=ALIGN)))
+        gather(0, 0)
+        wu_raw.append(load_wu(1, WG_HALF + WU_PASS, 1))
         gather(0, 1)
         gather(1, 0)
         deal_wg(FORGET)
         gather(1, 1)
 
         wu_codes, wu_scales = [], []
-
-        def round_wu(a):
-            wu_bf = keep.tile([P, PACK, P, PACK], BF16, name=f"wu_bf{a}", tag=f"wu_bf{a}", align_bytes=ALIGN)
+        for a in range(PASSES):
+            wu_bf = keep.tile([P, PACK, P, PACK], BF16, name=f"wu_bf{a}", align_bytes=ALIGN)
             wu_codes.append(keep.tile([P, H], U32, name=f"wu_codes{a}", align_bytes=ALIGN))
             wu_scales.append(keep.tile([P, H], U8, name=f"wu_scales{a}", align_bytes=ALIGN))
-            wu_in = wu_raw[a][:].rearrange("p i (m t) -> p m i t", t=PACK)
-            for t in (0, 2):
-                nc.vector.tensor_copy(wu_bf[:, t:t + 2].rearrange("p t m i -> p m i t"), wu_in[:, :, :, t:t + 2])
+            rows = P // len(wu_raw[a])
+            for part, piece in enumerate(wu_raw[a]):
+                for t in (0, 2):
+                    nc.vector.tensor_copy(
+                        wu_bf[:, t:t + 2, part * rows:(part + 1) * rows].rearrange("p t m i -> p m i t"),
+                        piece[:].rearrange("p i (m t) -> p m i t", t=PACK)[:, :, :, t:t + 2])
             step = 2 if a else PACK
             for t in range(0, PACK, step):
                 cols = slice(t * P, (t + step) * P)
                 nc.vector.quantize_mx(wu_codes[a][:, cols].bitcast(FP8X4), wu_scales[a][:, cols],
                                       wu_bf[:, t:t + step].rearrange("p t m i -> p (t m i)"))
 
-        round_wu(0)
-        round_wu(1)
+        cells = keep.tile([P, PACK * S], F32, name="cells", tag="table0", align_bytes=ALIGN)
+        cell_rows = cell.rearrange("(p t) j -> p t j", t=PACK)
 
-        cells = keep.tile([P, HALVES, PACK, COLS], F32, name="cells", tag="table0", align_bytes=ALIGN)
-        for h in range(HALVES):
-            for t in (0, 2):
-                nc.sync.dma_start(cells[:, h, t:t + 2, :],
-                                  cell.rearrange("(p t) j -> p t j", t=PACK)[:, t:t + 2, h * COLS:(h + 1) * COLS])
+        def chunk_view(tile, first, width):
+            return tile[:, PACK * first:PACK * (first + width)].rearrange("p (t j) -> p t j", t=PACK)
+
+        for first, width in CHUNKS:
+            step = 2 * BANK // width
+            for t in range(0, PACK, step):
+                nc.sync.dma_start(chunk_view(cells, first, width)[:, t:t + step, :],
+                                  cell_rows[:, t:t + step, first:first + width])
 
         wo_codes = keep.tile([P, N], I32, name="wo_codes", tag="table1", align_bytes=ALIGN)
         nc.sync.dma_start(wo_codes[:], wo_words[0].rearrange("p c i -> p (c i)").bitcast(I32))
 
-        acts = [keep.tile([P, 3 * PACK, COLS], F32, name=f"acts{h}", tag=tag, align_bytes=ALIGN)
-                for h, tag in enumerate(("acts0", "acts1"))]
+        kept, fresh = {}, {}
 
-        def first_stage(h, kind, t):
-            acc = psum.tile([P, COLS], F32, name="acc", tag="banks", bufs=BANKS)
-            order = range(PASSES)[::-1] if kind == CANDIDATE else range(PASSES)
-            for a in order:
-                if kind == CANDIDATE:
-                    codes = wu_codes[a][:, t * P:(t + 1) * P].bitcast(FP8X4)
-                    scales = wu_scales[a][:, t * P:(t + 1) * P]
-                else:
-                    first = (a * PACK + t) * P * 2
-                    codes = wg_codes[kind][:, first:first + P * 2].bitcast(FP4X4)
-                    scales = plane(a, WG_SCALES + kind * H + t * P, P)
-                words = states[a, h][:]
-                nc.tensor.matmul_mx(acc[:], lhsT=codes, lhsT_scale=scales, rhs=words.bitcast(FP8X4),
-                                    rhs_scale=plane(a, h * COLS, COLS), start=(a == order[0]), stop=(a == order[-1]))
-            act = acts[h][:, kind * PACK + t, :]
-            nc.scalar.activation(act, acc[:], TANH if kind == CANDIDATE else SIGMOID)
-            return act
+        def first_stage(first, width, by_kind):
+            acts = keep.tile([P, 3, PACK, width], F32, name=f"acts{first}")
+            kept[first] = keep.tile([P, PACK, width], F32, name=f"kept{first}")
+            fresh[first] = keep.tile([P, PACK, width], F32, name=f"fresh{first}")
+            step = BANK // width
+            starts = range(0, PACK, step)
+            if by_kind:
+                order = [(kind, t0) for kind in (INPUT, FORGET, CANDIDATE) for t0 in starts]
+            else:
+                order = [(kind, t0) for t0 in starts for kind in (INPUT, CANDIDATE, FORGET)]
+            for kind, t0 in order:
+                acc = psum.tile([P, step, width], F32, name="acc", tag="ring", bufs=RING)
+                passes = range(PASSES)[::-1] if kind == CANDIDATE else range(PASSES)
+                for t in range(t0, t0 + step):
+                    for a in passes:
+                        if kind == CANDIDATE:
+                            codes = wu_codes[a][:, t * P:(t + 1) * P].bitcast(FP8X4)
+                            scales = wu_scales[a][:, t * P:(t + 1) * P]
+                        else:
+                            at = (a * PACK + t) * P * 2
+                            codes = wg_codes[kind][:, at:at + P * 2].bitcast(FP4X4)
+                            scales = plane(a, WG_SCALES + kind * H + t * P, P)
+                        words = states[a, first // BANK][:, first % BANK:first % BANK + width]
+                        nc.tensor.matmul_mx(acc[:, t - t0, :], lhsT=codes, lhsT_scale=scales,
+                                            rhs=words.bitcast(FP8X4), rhs_scale=plane(a, first, width),
+                                            start=(a == passes[0]), stop=(a == passes[-1]))
+                nc.scalar.activation(acts[:, kind, t0:t0 + step, :], acc[:], TANH if kind == CANDIDATE else SIGMOID)
+                for t in range(t0, t0 + step):
+                    if kind == FORGET:
+                        nc.vector.scalar_tensor_tensor(kept[first][:, t, :], acts[:, FORGET, t, :], gains[:, t:t + 1],
+                                                       chunk_view(cells, first, width)[:, t, :], MULT, MULT)
+                    elif kind == CANDIDATE:
+                        nc.vector.scalar_tensor_tensor(fresh[first][:, t, :], acts[:, INPUT, t, :], gains[:, t:t + 1],
+                                                       acts[:, CANDIDATE, t, :], MULT, MULT)
 
-        identity = keep.tile([P, P], F32, name="identity")
-        make_identity(nc, identity[:])
-
-        kept = [keep.tile([P, PACK, COLS], F32, name=f"kept{h}") for h in range(HALVES)]
-        fresh = [keep.tile([P, PACK, COLS], F32, name=f"fresh{h}") for h in range(HALVES)]
-
-        def products(h, order):
-            made = {}
-            for kind, t in order:
-                made[kind, t] = first_stage(h, kind, t)
-                if kind == FORGET:
-                    nc.vector.scalar_tensor_tensor(kept[h][:, t, :], made[FORGET, t], gains[:, t:t + 1],
-                                                   cells[:, h, t, :], MULT, MULT)
-                elif kind == CANDIDATE:
-                    nc.vector.scalar_tensor_tensor(fresh[h][:, t, :], made[INPUT, t], gains[:, t:t + 1],
-                                                   made[CANDIDATE, t], MULT, MULT)
+        def terms(first, width):
+            start = max(c for c, w in CHUNKS if c <= first)
+            cols = slice(first - start, first - start + width)
+            return fresh[start][:, :, cols], kept[start][:, :, cols]
 
         def rounded(first, width):
             return keep.tile([P, width, PACK], BF16, name=f"h_bf{first}", align_bytes=ALIGN)
 
         def add(first, width):
-            h, cols = first // COLS, slice(first % COLS, first % COLS + width)
             h_bf = rounded(first, width)
-            nc.vector.tensor_tensor(h_bf[:].rearrange("p (c i) t -> p c t i", i=2),
-                                    fresh[h][:, :, cols].rearrange("p t (c i) -> p c t i", i=2),
-                                    kept[h][:, :, cols].rearrange("p t (c i) -> p c t i", i=2), ADD)
+            one, other = [term.rearrange("p t (c i) -> p c t i", i=2) for term in terms(first, width)]
+            nc.vector.tensor_tensor(h_bf[:].rearrange("p (c i) t -> p c t i", i=2), one, other, ADD)
             return first, width, h_bf
-
-        def add_turned(first):
-            h, cols = first // COLS, slice(first % COLS, first % COLS + P)
-            total = psum.tile([P, PACK, P], F32, name="total", tag="banks", bufs=BANKS)
-            for t in range(PACK):
-                for term, start in ((fresh[h], True), (kept[h], False)):
-                    nc.tensor.matmul(total[:, t, :], lhsT=term[:, t, cols], rhs=identity[:], is_transpose=True,
-                                     start=start, stop=not start)
-            turned = keep.tile([P, 2, P, 2], BF16, name=f"turned{first}", align_bytes=ALIGN)
-            nc.scalar.copy(turned[:], total[:].rearrange("j (u e) p -> j u p e", e=2))
-            return turned
-
-        def turn_back(first, blocks):
-            words = psum.tile([P, len(blocks), 2, P], F32, name="words", tag="words", bufs=1)
-            for b, turned in enumerate(blocks):
-                pairs = turned[:].rearrange("j u p e -> j (u p e)").bitcast(F32)
-                for u in range(2):
-                    nc.tensor.transpose(words[:, b, u, :], pairs[:, u * P:(u + 1) * P], identity[:])
-            h_bf = rounded(first, len(blocks) * P)
-            pairs = h_bf[:].rearrange("p j t -> p (j t)").bitcast(F32)
-            nc.scalar.copy(pairs.rearrange("p (b j u) -> p b j u", b=len(blocks), u=2),
-                           words[:].rearrange("p b u j -> p b j u"))
-            return first, len(blocks) * P, h_bf
 
         def quantise(first, width, h_bf):
             h_codes = keep.tile([P, width], U32, name=f"h_codes{first}", align_bytes=ALIGN)
@@ -223,28 +215,26 @@ def tile_list_term_tree_cell_kernel(tc, tab_words, tab_scales, offs, wg_words, w
             nc.vector.quantize_mx(h_codes[:].bitcast(FP8X4), h_scales[:], h_bf[:].rearrange("p j t -> p (j t)"))
             return first, width, h_codes, h_scales
 
-        def second_stage(chunk, copy, queue=nc.sync):
+        def second_stage(chunk, copy):
             first, width, h_codes, h_scales = chunk
-            acc = psum.tile([P, N // P, width], F32, name="acc", tag="banks", bufs=BANKS)
+            acc = psum.tile([P, N // P, width], F32, name="acc", tag="ring", bufs=RING)
             for n in range(N // P):
                 nc.tensor.matmul_mx(acc[:, n, :], lhsT=wo_codes[:, n * P:(n + 1) * P].bitcast(FP8X4),
                                     lhsT_scale=plane(n, WO_SCALES, P), rhs=h_codes[:].bitcast(FP8X4),
                                     rhs_scale=h_scales[:], start=True, stop=True)
             result = keep.tile([P, N // P, width], F32, name=f"result{first}")
             copy(result[:], acc[:])
-            queue.dma_start(out[:, first:first + width].rearrange("(n p) j -> p n j", p=P), result[:])
+            nc.sync.dma_start(out[:, first:first + width].rearrange("(n p) j -> p n j", p=P), result[:])
 
-        products(0, [(kind, t) for kind in (INPUT, FORGET, CANDIDATE) for t in range(PACK)])
-        chunk_a = quantise(*add(0, 256))
-        products(1, [(kind, t) for t in range(PACK) for kind in (INPUT, CANDIDATE, FORGET)])
-        blocks = [add_turned(first) for first in (256, 384)]
-        second_stage(chunk_a, nc.scalar.copy)
-        sum_b = turn_back(256, blocks)
-        sum_c, sum_d = add(512, 256), add(768, 128)
-        chunk_c = quantise(*sum_c)
-        sum_e = add(896, 128)
-        chunk_b, chunk_d, chunk_e = quantise(*sum_b), quantise(*sum_d), quantise(*sum_e)
-        second_stage(chunk_c, nc.scalar.copy)
-        second_stage(chunk_b, nc.scalar.copy)
-        second_stage(chunk_d, nc.vector.tensor_copy)
+        first_stage(*CHUNKS[0], True)
+        sum_a, sum_b = add(0, 256), add(256, 256)
+        chunk_a, chunk_b = quantise(*sum_a), quantise(*sum_b)
+        first_stage(*CHUNKS[1], False)
+        chunk_c = quantise(*add(512, 256))
+        first_stage(*CHUNKS[2], False)
+        for chunk in (chunk_a, chunk_b, chunk_c):
+            second_stage(chunk, nc.scalar.copy)
+        sum_d, sum_e = add(768, 128), add(896, 128)
+        chunk_d, chunk_e = quantise(*sum_d), quantise(*sum_e)
+        second_stage(chunk_d, nc.scalar.copy)
         second_stage(chunk_e, nc.vector.tensor_copy)

@@ -1,6 +1,7 @@
 from contextlib import ExitStack
 
 import concourse.mybir as mybir
+from concourse.masks import make_identity
 
 K, T, S, H, N = 1024, 2048, 1024, 512, 256
 FLOPS = 2 * K * 3 * H * S + 2 * H * N * S
@@ -158,42 +159,39 @@ def tile_list_term_tree_cell_kernel(tc, tab_words, tab_scales, offs, wg_words, w
         wo_codes = keep.tile([P, N], I32, name="wo_codes", tag="table1", align_bytes=ALIGN)
         nc.sync.dma_start(wo_codes[:], wo_words[0].rearrange("p c i -> p (c i)").bitcast(I32))
 
-        kept, fresh = {}, {}
+        identity = keep.tile([P, P], F32, name="identity")
+        make_identity(nc, identity[:])
 
-        def first_stage(first, width, by_kind):
-            acts = keep.tile([P, 3, PACK, width], F32, name=f"acts{first}")
-            kept[first] = keep.tile([P, PACK, width], F32, name=f"kept{first}")
-            fresh[first] = keep.tile([P, PACK, width], F32, name=f"fresh{first}")
+        acts = {first: keep.tile([P, 3, PACK, width], F32, name=f"acts{first}") for first, width in CHUNKS}
+        kept = {first: keep.tile([P, PACK, width], F32, name=f"kept{first}") for first, width in CHUNKS}
+        fresh = {first: keep.tile([P, PACK, width], F32, name=f"fresh{first}") for first, width in CHUNKS}
+
+        def first_stage(chunk, kind, t0):
+            first, width = chunk
             step = BANK // width
-            starts = range(0, PACK, step)
-            if by_kind:
-                order = [(kind, t0) for kind in (INPUT, FORGET, CANDIDATE) for t0 in starts]
-            else:
-                order = [(kind, t0) for t0 in starts for kind in (INPUT, CANDIDATE, FORGET)]
-            for kind, t0 in order:
-                acc = psum.tile([P, step, width], F32, name="acc", tag="ring", bufs=RING)
-                passes = range(PASSES)[::-1] if kind == CANDIDATE else range(PASSES)
-                for t in range(t0, t0 + step):
-                    for a in passes:
-                        if kind == CANDIDATE:
-                            codes = wu_codes[a][:, t * P:(t + 1) * P].bitcast(FP8X4)
-                            scales = wu_scales[a][:, t * P:(t + 1) * P]
-                        else:
-                            at = (a * PACK + t) * P * 2
-                            codes = wg_codes[kind][:, at:at + P * 2].bitcast(FP4X4)
-                            scales = plane(a, WG_SCALES + kind * H + t * P, P)
-                        words = states[a, first // BANK][:, first % BANK:first % BANK + width]
-                        nc.tensor.matmul_mx(acc[:, t - t0, :], lhsT=codes, lhsT_scale=scales,
-                                            rhs=words.bitcast(FP8X4), rhs_scale=plane(a, first, width),
-                                            start=(a == passes[0]), stop=(a == passes[-1]))
-                nc.scalar.activation(acts[:, kind, t0:t0 + step, :], acc[:], TANH if kind == CANDIDATE else SIGMOID)
-                for t in range(t0, t0 + step):
-                    if kind == FORGET:
-                        nc.vector.scalar_tensor_tensor(kept[first][:, t, :], acts[:, FORGET, t, :], gains[:, t:t + 1],
-                                                       chunk_view(cells, first, width)[:, t, :], MULT, MULT)
-                    elif kind == CANDIDATE:
-                        nc.vector.scalar_tensor_tensor(fresh[first][:, t, :], acts[:, INPUT, t, :], gains[:, t:t + 1],
-                                                       acts[:, CANDIDATE, t, :], MULT, MULT)
+            acc = psum.tile([P, step, width], F32, name="acc", tag="ring", bufs=RING)
+            passes = range(PASSES)[::-1] if kind == CANDIDATE else range(PASSES)
+            for t in range(t0, t0 + step):
+                for a in passes:
+                    if kind == CANDIDATE:
+                        codes = wu_codes[a][:, t * P:(t + 1) * P].bitcast(FP8X4)
+                        scales = wu_scales[a][:, t * P:(t + 1) * P]
+                    else:
+                        at = (a * PACK + t) * P * 2
+                        codes = wg_codes[kind][:, at:at + P * 2].bitcast(FP4X4)
+                        scales = plane(a, WG_SCALES + kind * H + t * P, P)
+                    words = states[a, first // BANK][:, first % BANK:first % BANK + width]
+                    nc.tensor.matmul_mx(acc[:, t - t0, :], lhsT=codes, lhsT_scale=scales,
+                                        rhs=words.bitcast(FP8X4), rhs_scale=plane(a, first, width),
+                                        start=(a == passes[0]), stop=(a == passes[-1]))
+            nc.scalar.activation(acts[first][:, kind, t0:t0 + step, :], acc[:], TANH if kind == CANDIDATE else SIGMOID)
+            for t in range(t0, t0 + step):
+                if kind == FORGET:
+                    nc.vector.scalar_tensor_tensor(kept[first][:, t, :], acts[first][:, FORGET, t, :], gains[:, t:t + 1],
+                                                   chunk_view(cells, first, width)[:, t, :], MULT, MULT)
+                elif kind == CANDIDATE:
+                    nc.vector.scalar_tensor_tensor(fresh[first][:, t, :], acts[first][:, INPUT, t, :], gains[:, t:t + 1],
+                                                   acts[first][:, CANDIDATE, t, :], MULT, MULT)
 
         def terms(first, width):
             start = max(c for c, w in CHUNKS if c <= first)
@@ -208,6 +206,29 @@ def tile_list_term_tree_cell_kernel(tc, tab_words, tab_scales, offs, wg_words, w
             one, other = [term.rearrange("p t (c i) -> p c t i", i=2) for term in terms(first, width)]
             nc.vector.tensor_tensor(h_bf[:].rearrange("p (c i) t -> p c t i", i=2), one, other, ADD)
             return first, width, h_bf
+
+        def add_turned(first):
+            total = psum.tile([P, PACK, P], F32, name="total", tag="ring", bufs=RING)
+            one, other = terms(first, P)
+            for t in range(PACK):
+                for term, start in ((one, True), (other, False)):
+                    nc.tensor.matmul(total[:, t, :], lhsT=term[:, t, :], rhs=identity[:], is_transpose=True,
+                                     start=start, stop=not start)
+            turned = keep.tile([P, 2, P, 2], BF16, name=f"turned{first}", align_bytes=ALIGN)
+            nc.scalar.copy(turned[:], total[:].rearrange("j (u e) p -> j u p e", e=2))
+            return turned
+
+        def turn_back(first, blocks):
+            words = psum.tile([P, len(blocks), 2, P], F32, name="words", tag="words", bufs=1)
+            for b, turned in enumerate(blocks):
+                pairs = turned[:].rearrange("j u p e -> j (u p e)").bitcast(F32)
+                for u in range(2):
+                    nc.tensor.transpose(words[:, b, u, :], pairs[:, u * P:(u + 1) * P], identity[:])
+            h_bf = rounded(first, len(blocks) * P)
+            pairs = h_bf[:].rearrange("p j t -> p (j t)").bitcast(F32)
+            nc.scalar.copy(pairs.rearrange("p (b j u) -> p b j u", b=len(blocks), u=2),
+                           words[:].rearrange("p b u j -> p b j u"))
+            return first, len(blocks) * P, h_bf
 
         def quantise(first, width, h_bf):
             h_codes = keep.tile([P, width], U32, name=f"h_codes{first}", align_bytes=ALIGN)
@@ -226,15 +247,28 @@ def tile_list_term_tree_cell_kernel(tc, tab_words, tab_scales, offs, wg_words, w
             copy(result[:], acc[:])
             nc.sync.dma_start(out[:, first:first + width].rearrange("(n p) j -> p n j", p=P), result[:])
 
-        first_stage(*CHUNKS[0], True)
-        sum_a, sum_b = add(0, 256), add(256, 256)
+        wide, middle, last = CHUNKS
+        for kind in (INPUT, FORGET):
+            for t in range(PACK):
+                first_stage(wide, kind, t)
+        first_stage(middle, INPUT, 0)
+        for t in range(PACK):
+            first_stage(wide, CANDIDATE, t)
+        sum_a, sum_b = add(0, 256), add(256, 128)
         chunk_a, chunk_b = quantise(*sum_a), quantise(*sum_b)
-        first_stage(*CHUNKS[1], False)
+        for kind, t in ((CANDIDATE, 0), (FORGET, 0), (INPUT, 2), (CANDIDATE, 2), (FORGET, 2)):
+            first_stage(middle, kind, t)
         chunk_c = quantise(*add(512, 256))
-        first_stage(*CHUNKS[2], False)
-        for chunk in (chunk_a, chunk_b, chunk_c):
-            second_stage(chunk, nc.scalar.copy)
+        for t in (0, 2):
+            for kind in (INPUT, CANDIDATE, FORGET):
+                first_stage(last, kind, t)
+        blocks = [add_turned(384)]
+        second_stage(chunk_a, nc.scalar.copy)
+        sum_t = turn_back(384, blocks)
+        second_stage(chunk_c, nc.scalar.copy)
+        second_stage(chunk_b, nc.scalar.copy)
         sum_d, sum_e = add(768, 128), add(896, 128)
-        chunk_d, chunk_e = quantise(*sum_d), quantise(*sum_e)
+        chunk_t, chunk_d, chunk_e = quantise(*sum_t), quantise(*sum_d), quantise(*sum_e)
+        second_stage(chunk_t, nc.scalar.copy)
         second_stage(chunk_d, nc.scalar.copy)
         second_stage(chunk_e, nc.vector.tensor_copy)

@@ -36,6 +36,7 @@ WU_PASS = PACK * H * 4
 
 CHUNKS = ((0, 512), (512, 256), (768, 256))
 RING = 4
+OUTS = ((0, 256), (256, 256), (512, 256), (768, 128), (896, 128))
 ZEROED_BY_VECTOR = 3 * T // 4
 
 
@@ -116,8 +117,11 @@ def tile_list_term_tree_cell_kernel(tc, tab_words, tab_scales, offs, wg_words, w
         def gather(a, half):
             tag = f"states{a}{half}"
             states[a, half] = keep.tile([P, BANK], U32, name=f"states{a}{half}", tag=tag, align_bytes=ALIGN)
-            entries = offsets[:, half * BANK // GROUP:(half + 1) * BANK // GROUP]
-            nc.vector.tensor_copy(states[a, half][:], table[a][:].bitcast(U32).indirect(entries))
+            width = BANK // 2 if (a, half) == (1, 0) else BANK
+            for lo in range(0, BANK, width):
+                first = half * BANK + lo
+                entries = offsets[:, first // GROUP:(first + width) // GROUP]
+                nc.vector.tensor_copy(states[a, half][:, lo:lo + width], table[a][:].bitcast(U32).indirect(entries))
 
         deal_wg(INPUT)
         gather(0, 0)
@@ -166,13 +170,15 @@ def tile_list_term_tree_cell_kernel(tc, tab_words, tab_scales, offs, wg_words, w
         kept = {first: keep.tile([P, PACK, width], F32, name=f"kept{first}") for first, width in CHUNKS}
         fresh = {first: keep.tile([P, PACK, width], F32, name=f"fresh{first}") for first, width in CHUNKS}
 
-        def first_stage(chunk, kind, t0):
-            first, width = chunk
+        def first_stage(chunk, kind, t0, part=None):
+            start, whole = chunk
+            first, width = part or chunk
+            cols = slice(first - start, first - start + width)
             step = BANK // width
             acc = psum.tile([P, step, width], F32, name="acc", tag="ring", bufs=RING)
             passes = range(PASSES)[::-1] if kind == CANDIDATE else range(PASSES)
-            for t in range(t0, t0 + step):
-                for a in passes:
+            for a in passes:
+                for t in range(t0, t0 + step):
                     if kind == CANDIDATE:
                         codes = wu_codes[a][:, t * P:(t + 1) * P].bitcast(FP8X4)
                         scales = wu_scales[a][:, t * P:(t + 1) * P]
@@ -183,8 +189,8 @@ def tile_list_term_tree_cell_kernel(tc, tab_words, tab_scales, offs, wg_words, w
                     words = states[a, first // BANK][:, first % BANK:first % BANK + width]
                     nc.tensor.matmul_mx(acc[:, t - t0, :], lhsT=codes, lhsT_scale=scales,
                                         rhs=words.bitcast(FP8X4), rhs_scale=plane(a, first, width),
-                                        start=(a == passes[0]), stop=(a == passes[-1]))
-            nc.scalar.activation(acts[first][:, kind, t0:t0 + step, :], acc[:], TANH if kind == CANDIDATE else SIGMOID)
+                                        start=(a, t) == (passes[0], t0), stop=(a, t) == (passes[-1], t0 + step - 1))
+            nc.scalar.activation(acts[start][:, kind, t0:t0 + step, cols], acc[:], TANH if kind == CANDIDATE else SIGMOID)
             for t in range(t0, t0 + step):
                 if kind == FORGET:
                     nc.vector.scalar_tensor_tensor(kept[first][:, t, :], acts[first][:, FORGET, t, :], gains[:, t:t + 1],
@@ -230,45 +236,56 @@ def tile_list_term_tree_cell_kernel(tc, tab_words, tab_scales, offs, wg_words, w
                            words[:].rearrange("p b u j -> p b j u"))
             return first, len(blocks) * P, h_bf
 
+        h_codes = {first: keep.tile([P, width], U32, name=f"h_codes{first}", align_bytes=ALIGN) for first, width in OUTS}
+        h_scales = {first: keep.tile([P, width], U8, name=f"h_scales{first}", align_bytes=ALIGN) for first, width in OUTS}
+
         def quantise(first, width, h_bf):
-            h_codes = keep.tile([P, width], U32, name=f"h_codes{first}", align_bytes=ALIGN)
-            h_scales = keep.tile([P, width], U8, name=f"h_scales{first}", align_bytes=ALIGN)
-            nc.vector.quantize_mx(h_codes[:].bitcast(FP8X4), h_scales[:], h_bf[:].rearrange("p j t -> p (j t)"))
-            return first, width, h_codes, h_scales
+            start = max(c for c, w in OUTS if c <= first)
+            cols = slice(first - start, first - start + width)
+            nc.vector.quantize_mx(h_codes[start][:, cols].bitcast(FP8X4), h_scales[start][:, cols],
+                                  h_bf[:].rearrange("p j t -> p (j t)"))
 
         def second_stage(chunk, copy):
-            first, width, h_codes, h_scales = chunk
+            first, width = chunk
             acc = psum.tile([P, N // P, width], F32, name="acc", tag="ring", bufs=RING)
             for n in range(N // P):
                 nc.tensor.matmul_mx(acc[:, n, :], lhsT=wo_codes[:, n * P:(n + 1) * P].bitcast(FP8X4),
-                                    lhsT_scale=plane(n, WO_SCALES, P), rhs=h_codes[:].bitcast(FP8X4),
-                                    rhs_scale=h_scales[:], start=True, stop=True)
+                                    lhsT_scale=plane(n, WO_SCALES, P), rhs=h_codes[first][:].bitcast(FP8X4),
+                                    rhs_scale=h_scales[first][:], start=True, stop=True)
             result = keep.tile([P, N // P, width], F32, name=f"result{first}")
             copy(result[:], acc[:])
             nc.sync.dma_start(out[:, first:first + width].rearrange("(n p) j -> p n j", p=P), result[:])
 
         wide, middle, last = CHUNKS
-        for kind in (INPUT, FORGET):
-            for t in range(PACK):
-                first_stage(wide, kind, t)
-        first_stage(middle, INPUT, 0)
+        narrow = [(kind, t) for t in (0, 2) for kind in (INPUT, CANDIDATE, FORGET)]
+        ahead = [(INPUT, 0), (FORGET, 0)]
+        for part in ((0, 256), (256, 256)):
+            for t in (0, 2):
+                first_stage(wide, INPUT, t, part)
+        for t in range(PACK):
+            first_stage(wide, FORGET, t)
+        for kind, t in ahead:
+            first_stage(middle, kind, t)
         for t in range(PACK):
             first_stage(wide, CANDIDATE, t)
         sum_a, sum_b = add(0, 256), add(256, 128)
-        chunk_a, chunk_b = quantise(*sum_a), quantise(*sum_b)
-        for kind, t in ((CANDIDATE, 0), (FORGET, 0), (INPUT, 2), (CANDIDATE, 2), (FORGET, 2)):
-            first_stage(middle, kind, t)
-        chunk_c = quantise(*add(512, 256))
-        for t in (0, 2):
-            for kind in (INPUT, CANDIDATE, FORGET):
-                first_stage(last, kind, t)
+        quantise(*sum_a)
+        quantise(*sum_b)
+        for kind, t in narrow:
+            if (kind, t) not in ahead:
+                first_stage(middle, kind, t)
+        quantise(*add(512, 256))
+        for kind, t in narrow:
+            first_stage(last, kind, t)
         blocks = [add_turned(384)]
-        second_stage(chunk_a, nc.scalar.copy)
+        second_stage(OUTS[0], nc.scalar.copy)
         sum_t = turn_back(384, blocks)
-        second_stage(chunk_c, nc.scalar.copy)
-        second_stage(chunk_b, nc.scalar.copy)
-        sum_d, sum_e = add(768, 128), add(896, 128)
-        chunk_t, chunk_d, chunk_e = quantise(*sum_t), quantise(*sum_d), quantise(*sum_e)
-        second_stage(chunk_t, nc.scalar.copy)
-        second_stage(chunk_d, nc.scalar.copy)
-        second_stage(chunk_e, nc.vector.tensor_copy)
+        second_stage(OUTS[2], nc.scalar.copy)
+        sum_d = add(768, 128)
+        quantise(*sum_t)
+        second_stage(OUTS[1], nc.scalar.copy)
+        sum_e = add(896, 128)
+        quantise(*sum_d)
+        quantise(*sum_e)
+        second_stage(OUTS[3], nc.vector.tensor_copy)
+        second_stage(OUTS[4], nc.vector.tensor_copy)

@@ -28,15 +28,15 @@ BANK = 512
 INPUT, FORGET, CANDIDATE = 0, 1, 2
 ALIGN = 64
 
-WG_SCALES = S
-WO_SCALES = WG_SCALES + 2 * H
-PLANE = WO_SCALES + P
+EARLY = BANK + 2 * H
+LATE = BANK + P
 WG_HALF = PASSES * H * 2
 WU_PASS = PACK * H * 4
 
 CHUNKS = ((0, 512), (512, 256), (768, 256))
 RING = 4
 OUTS = ((0, 256), (256, 256), (512, 256), (768, 128), (896, 128))
+WU_END = WG_HALF + 2 * WU_PASS
 ZEROED_BY_VECTOR = 3 * T // 4
 
 
@@ -53,15 +53,16 @@ def tile_list_term_tree_cell_kernel(tc, tab_words, tab_scales, offs, wg_words, w
 
         tab_rows = keep.tile([P, T], U8, name="tab_rows", tag="tab_rows", align_bytes=ALIGN)
         wg_rows = keep.tile([P, 2 * H], U8, name="wg_rows", align_bytes=ALIGN)
-        staged = keep.tile([P, PLANE], U8, name="staged", align_bytes=ALIGN)
-        planes = keep.tile([P, PASSES * PLANE], U8, name="planes", align_bytes=ALIGN)
+        staged = [keep.tile([P, width], U8, name=f"staged{half}", align_bytes=ALIGN)
+                  for half, width in enumerate((EARLY, LATE))]
+        planes = [keep.tile([P, PASSES * EARLY], U8, name="planes0", align_bytes=ALIGN)]
         nc.vector.memset(tab_rows[:, :ZEROED_BY_VECTOR].bitcast(I32), 0)
         nc.gpsimd.memset(tab_rows[:, ZEROED_BY_VECTOR:].bitcast(I32), 0)
         nc.gpsimd.memset(wg_rows[:].bitcast(I32), 0)
-        nc.vector.memset(planes[:].bitcast(I32), 0)
+        nc.vector.memset(planes[0][:].bitcast(I32), 0)
         nc.sync.dma_start(tab_rows[0:P:4, :].bitcast(I32), tab_scales.bitcast(I32).rearrange("a q t -> q a t"))
         nc.sync.dma_start(wg_rows[0:P:4, :].bitcast(I32), wg_scales.bitcast(I32).rearrange("a q c -> q a c"))
-        nc.sync.dma_start(staged[0:P:4, WO_SCALES:].bitcast(I32),
+        nc.sync.dma_start(staged[1][0:P:4, BANK:].bitcast(I32),
                           wo_scales[0].bitcast(I32).rearrange("q (n c) -> (q n) c", n=N // P))
 
         def load_table(a, queue):
@@ -84,26 +85,31 @@ def tile_list_term_tree_cell_kernel(tc, tab_words, tab_scales, offs, wg_words, w
                 nc.sync.dma_start(pieces[part][:], rows[:, :, part * width:(part + 1) * width])
             return pieces
 
-        wg_raw = [load_wg(INPUT, WG_HALF + WU_PASS + (WU_PASS - WG_HALF) // 2)]
+        wg_raw = [load_wg(INPUT, WU_END - WG_HALF // 4)]
         table = [load_table(0, nc.sync)]
-        gains = keep.tile([P, PACK], F32, name="gains")
-        nc.sync.dma_start(gains[:], gain.rearrange("(p t) -> p t", t=PACK))
         table.append(load_table(1, nc.sync))
 
         picked_rows = shared.tile([P, S], U8, name="picked_rows", align_bytes=ALIGN, offset=WG_HALF - S // 2)
         nc.vector.tensor_copy(picked_rows[:], tab_rows[:].indirect(offsets[:]))
-        nc.vector.tensor_copy(staged[:, WG_SCALES:WO_SCALES].rearrange("p (g t m) -> p g t m", g=2, t=PACK),
+        nc.vector.tensor_copy(staged[0][:, BANK:].rearrange("p (g t m) -> p g t m", g=2, t=PACK),
                               wg_rows[:].rearrange("p (g m t) -> p g t m", g=2, t=PACK))
-        nc.vector.tensor_copy(staged[:, :WG_SCALES].bitcast(I32), picked_rows[:].bitcast(I32))
-        for d in (0, 2, 1, 3):
-            first = QUADRANT * d
-            nc.sync.dma_start(planes[first:first + 4, :].bitcast(I32),
-                              staged[first:first + QUADRANT:4, :].bitcast(I32))
+        for half in (1, 0):
+            nc.vector.tensor_copy(staged[half][:, :BANK].bitcast(I32),
+                                  picked_rows[:, half * BANK:(half + 1) * BANK].bitcast(I32))
+
+        def place(half):
+            for d in (0, 2, 1, 3):
+                first = QUADRANT * d
+                nc.sync.dma_start(planes[half][first:first + 4, :].bitcast(I32),
+                                  staged[half][first:first + QUADRANT:4, :].bitcast(I32))
+
+        place(0)
         wg_raw.append(load_wg(FORGET, 0))
         wu_raw = [load_wu(0, WG_HALF, 1)]
 
-        def plane(a, first, width):
-            return planes[:, a * PLANE + first:a * PLANE + first + width]
+        def plane(half, a, first, width):
+            first += a * (LATE if half else EARLY)
+            return planes[half][:, first:first + width]
 
         wg_codes = [keep.tile([P, WG_HALF], U8, name=f"wg_codes{g}", align_bytes=ALIGN) for g in (INPUT, FORGET)]
 
@@ -126,6 +132,11 @@ def tile_list_term_tree_cell_kernel(tc, tab_words, tab_scales, offs, wg_words, w
         deal_wg(INPUT)
         gather(0, 0)
         wu_raw.append(load_wu(1, WG_HALF + WU_PASS, 1))
+        gains = shared.tile([P, PACK], F32, name="gains", align_bytes=ALIGN, offset=WU_END)
+        nc.sync.dma_start(gains[:], gain.rearrange("(p t) -> p t", t=PACK))
+        planes.append(shared.tile([P, PASSES * LATE], U8, name="planes1", align_bytes=ALIGN, offset=WU_END + ALIGN))
+        nc.gpsimd.memset(planes[1][:].bitcast(I32), 0)
+        place(1)
         gather(0, 1)
         gather(1, 0)
         deal_wg(FORGET)
@@ -176,7 +187,7 @@ def tile_list_term_tree_cell_kernel(tc, tab_words, tab_scales, offs, wg_words, w
             cols = slice(first - start, first - start + width)
             step = BANK // width
             acc = psum.tile([P, step, width], F32, name="acc", tag="ring", bufs=RING)
-            passes = range(PASSES)[::-1] if kind == CANDIDATE else range(PASSES)
+            passes = range(PASSES) if (first, kind) == (0, INPUT) else range(PASSES)[::-1]
             for a in passes:
                 for t in range(t0, t0 + step):
                     if kind == CANDIDATE:
@@ -185,10 +196,10 @@ def tile_list_term_tree_cell_kernel(tc, tab_words, tab_scales, offs, wg_words, w
                     else:
                         at = (a * PACK + t) * P * 2
                         codes = wg_codes[kind][:, at:at + P * 2].bitcast(FP4X4)
-                        scales = plane(a, WG_SCALES + kind * H + t * P, P)
+                        scales = plane(0, a, BANK + kind * H + t * P, P)
                     words = states[a, first // BANK][:, first % BANK:first % BANK + width]
                     nc.tensor.matmul_mx(acc[:, t - t0, :], lhsT=codes, lhsT_scale=scales,
-                                        rhs=words.bitcast(FP8X4), rhs_scale=plane(a, first, width),
+                                        rhs=words.bitcast(FP8X4), rhs_scale=plane(first // BANK, a, first % BANK, width),
                                         start=(a, t) == (passes[0], t0), stop=(a, t) == (passes[-1], t0 + step - 1))
             nc.scalar.activation(acts[start][:, kind, t0:t0 + step, cols], acc[:], TANH if kind == CANDIDATE else SIGMOID)
             for t in range(t0, t0 + step):
@@ -250,7 +261,7 @@ def tile_list_term_tree_cell_kernel(tc, tab_words, tab_scales, offs, wg_words, w
             acc = psum.tile([P, N // P, width], F32, name="acc", tag="ring", bufs=RING)
             for n in range(N // P):
                 nc.tensor.matmul_mx(acc[:, n, :], lhsT=wo_codes[:, n * P:(n + 1) * P].bitcast(FP8X4),
-                                    lhsT_scale=plane(n, WO_SCALES, P), rhs=h_codes[first][:].bitcast(FP8X4),
+                                    lhsT_scale=plane(1, n, BANK, P), rhs=h_codes[first][:].bitcast(FP8X4),
                                     rhs_scale=h_scales[first][:], start=True, stop=True)
             result = keep.tile([P, N // P, width], F32, name=f"result{first}")
             copy(result[:], acc[:])

@@ -35,7 +35,7 @@ WU_PASS = PACK * H * 4
 
 CHUNKS = ((0, 512), (512, 256), (768, 256))
 RING = 4
-OUTS = ((0, 256), (256, 256), (512, 256), (768, 128), (896, 128))
+OUTS = ((0, 256), (256, 128), (384, 128), (512, 256), (768, 128), (896, 128))
 WU_END = WG_HALF + 2 * WU_PASS
 ZEROED_BY_VECTOR = 3 * T // 4
 
@@ -236,7 +236,7 @@ def tile_list_term_tree_cell_kernel(tc, tab_words, tab_scales, offs, wg_words, w
             return turned
 
         def turn_back(first, blocks):
-            words = psum.tile([P, len(blocks), 2, P], F32, name="words", tag="words", bufs=1)
+            words = psum.tile([P, len(blocks), 2, P], F32, name="words", tag="words", bufs=2)
             for b, turned in enumerate(blocks):
                 pairs = turned[:].rearrange("j u p e -> j (u p e)").bitcast(F32)
                 for u in range(2):
@@ -256,9 +256,9 @@ def tile_list_term_tree_cell_kernel(tc, tab_words, tab_scales, offs, wg_words, w
             nc.vector.quantize_mx(h_codes[start][:, cols].bitcast(FP8X4), h_scales[start][:, cols],
                                   h_bf[:].rearrange("p j t -> p (j t)"))
 
-        def second_stage(chunk, copy):
+        def second_stage(chunk, copy, tag="ring", bufs=RING):
             first, width = chunk
-            acc = psum.tile([P, N // P, width], F32, name="acc", tag="ring", bufs=RING)
+            acc = psum.tile([P, N // P, width], F32, name="acc", tag=tag, bufs=bufs)
             for n in range(N // P):
                 nc.tensor.matmul_mx(acc[:, n, :], lhsT=wo_codes[:, n * P:(n + 1) * P].bitcast(FP8X4),
                                     lhsT_scale=plane(1, n, BANK, P), rhs=h_codes[first][:].bitcast(FP8X4),
@@ -279,24 +279,23 @@ def tile_list_term_tree_cell_kernel(tc, tab_words, tab_scales, offs, wg_words, w
             first_stage(middle, kind, t)
         for t in range(PACK):
             first_stage(wide, CANDIDATE, t)
-        sum_a, sum_b = add(0, 256), add(256, 128)
-        quantise(*sum_a)
-        quantise(*sum_b)
+        quantise(*add(0, 256))
         for kind, t in narrow:
             if (kind, t) not in ahead:
                 first_stage(middle, kind, t)
         quantise(*add(512, 256))
         for kind, t in narrow:
             first_stage(last, kind, t)
-        blocks = [add_turned(384)]
-        second_stage(OUTS[0], nc.scalar.copy)
-        sum_t = turn_back(384, blocks)
-        second_stage(OUTS[2], nc.scalar.copy)
-        sum_d = add(768, 128)
-        quantise(*sum_t)
+        turned = [add_turned(first) for first in (256, 384)]
+        sum_a, sum_b = turn_back(256, turned[:1]), turn_back(384, turned[1:])
+        for chunk in (OUTS[0], OUTS[3]):
+            second_stage(chunk, nc.scalar.copy, "words", 2)
+        quantise(*sum_a)
         second_stage(OUTS[1], nc.scalar.copy)
-        sum_e = add(896, 128)
+        sum_d, sum_e = add(768, 128), add(896, 128)
+        quantise(*sum_b)
         quantise(*sum_d)
         quantise(*sum_e)
-        second_stage(OUTS[3], nc.vector.tensor_copy)
+        second_stage(OUTS[2], nc.vector.tensor_copy)
         second_stage(OUTS[4], nc.vector.tensor_copy)
+        second_stage(OUTS[5], nc.vector.tensor_copy)

@@ -36,7 +36,12 @@ WU_PASS = PACK * H * 4
 CHUNKS = ((0, 512), (512, 256), (768, 256))
 RING = 4
 OUTS = ((0, 256), (256, 128), (384, 128), (512, 256), (768, 128), (896, 128))
-WU_END = WG_HALF + 2 * WU_PASS
+AT_WO = PACK * S * 4
+AT_WG_FORGET = AT_WO - ALIGN
+AT_GAINS = AT_WG_FORGET + WG_HALF
+AT_PLANES = AT_GAINS + ALIGN
+AT_WU = AT_PLANES + PASSES * LATE
+AT_WG_INPUT = AT_GAINS - ALIGN
 ZEROED_BY_VECTOR = 3 * T // 4
 
 
@@ -52,13 +57,13 @@ def tile_list_term_tree_cell_kernel(tc, tab_words, tab_scales, offs, wg_words, w
         nc.sync.dma_start(offsets[:], offs)
 
         tab_rows = keep.tile([P, T], U8, name="tab_rows", tag="tab_rows", align_bytes=ALIGN)
-        wg_rows = keep.tile([P, 2 * H], U8, name="wg_rows", align_bytes=ALIGN)
+        wg_rows = keep.tile([P, 2 * H], U8, name="wg_rows", align_bytes=ALIGN)[:]
         staged = [keep.tile([P, width], U8, name=f"staged{half}", align_bytes=ALIGN)
                   for half, width in enumerate((EARLY, LATE))]
         planes = [keep.tile([P, PASSES * EARLY], U8, name="planes0", align_bytes=ALIGN)]
         nc.vector.memset(tab_rows[:, :ZEROED_BY_VECTOR].bitcast(I32), 0)
         nc.gpsimd.memset(tab_rows[:, ZEROED_BY_VECTOR:].bitcast(I32), 0)
-        nc.gpsimd.memset(wg_rows[:].bitcast(I32), 0)
+        nc.gpsimd.memset(wg_rows.bitcast(I32), 0)
         nc.vector.memset(planes[0][:].bitcast(I32), 0)
         nc.sync.dma_start(tab_rows[0:P:4, :].bitcast(I32), tab_scales.bitcast(I32).rearrange("a q t -> q a t"))
         nc.sync.dma_start(wg_rows[0:P:4, :].bitcast(I32), wg_scales.bitcast(I32).rearrange("a q c -> q a c"))
@@ -75,24 +80,18 @@ def tile_list_term_tree_cell_kernel(tc, tab_words, tab_scales, offs, wg_words, w
             nc.sync.dma_start(words[:], wg_words.bitcast(I32).rearrange("a p (g c) -> g p a c", g=2)[g])
             return words
 
-        def load_wu(a, offset, parts):
-            rows = wu[a * P * PACK:(a + 1) * P * PACK, :].rearrange("(p i) r -> p i r", i=PACK)
-            width = H // parts
-            pieces = []
-            for part in range(parts):
-                pieces.append(shared.tile([P, PACK, width], F32, name=f"wu_raw{a}{part}", align_bytes=ALIGN,
-                                          offset=offset + part * WU_PASS // parts))
-                nc.sync.dma_start(pieces[part][:], rows[:, :, part * width:(part + 1) * width])
-            return pieces
+        def load_wu(a):
+            rows = wu[a * P * PACK:(a + 1) * P * PACK, :].rearrange("(p i) r -> p (i r)", i=PACK)
+            nc.sync.dma_start(wu_raw[:, a * PACK * H:(a + 1) * PACK * H], rows)
 
-        wg_raw = [load_wg(INPUT, WU_END - WG_HALF // 4)]
+        wg_raw = [load_wg(INPUT, AT_WG_INPUT)]
         table = [load_table(0, nc.sync)]
         table.append(load_table(1, nc.sync))
 
-        picked_rows = shared.tile([P, S], U8, name="picked_rows", align_bytes=ALIGN, offset=WG_HALF - S // 2)
+        picked_rows = keep.tile([P, S], U8, name="picked_rows", align_bytes=ALIGN)
         nc.vector.tensor_copy(picked_rows[:], tab_rows[:].indirect(offsets[:]))
-        nc.vector.tensor_copy(staged[0][:, BANK:].rearrange("p (g t m) -> p g t m", g=2, t=PACK),
-                              wg_rows[:].rearrange("p (g m t) -> p g t m", g=2, t=PACK))
+        nc.gpsimd.tensor_copy(staged[0][:, BANK:].rearrange("p (g t m) -> p g t m", g=2, t=PACK),
+                              wg_rows.rearrange("p (g m t) -> p g t m", g=2, t=PACK))
         for half in (1, 0):
             nc.vector.tensor_copy(staged[half][:, :BANK].bitcast(I32),
                                   picked_rows[:, half * BANK:(half + 1) * BANK].bitcast(I32))
@@ -104,19 +103,25 @@ def tile_list_term_tree_cell_kernel(tc, tab_words, tab_scales, offs, wg_words, w
                                   staged[half][first:first + QUADRANT:4, :].bitcast(I32))
 
         place(0)
-        wg_raw.append(load_wg(FORGET, 0))
-        wu_raw = [load_wu(0, WG_HALF, 1)]
+        wg_raw.append(load_wg(FORGET, AT_WG_FORGET))
+        wu_raw = shared.tile([P, PASSES * PACK * H], F32, name="wu_raw", align_bytes=ALIGN, offset=AT_WU)
+        load_wu(0)
 
         def plane(half, a, first, width):
             first += a * (LATE if half else EARLY)
             return planes[half][:, first:first + width]
 
-        wg_codes = [keep.tile([P, WG_HALF], U8, name=f"wg_codes{g}", align_bytes=ALIGN) for g in (INPUT, FORGET)]
+        wg_codes = [keep.tile([P, WG_HALF], U8, name=f"wg_codes{g}", tag=f"wg_codes{g}", align_bytes=ALIGN) for g in (INPUT, FORGET)]
 
         def deal_wg(g):
             words = wg_raw[g][:].rearrange("p a c -> p (a c)").bitcast(U16)
-            nc.vector.tensor_copy(wg_codes[g][:].bitcast(U16).rearrange("p (a t m) -> p a t m", a=PASSES, t=PACK),
-                                  words.rearrange("p (a m t) -> p a t m", a=PASSES, t=PACK))
+            dealt = wg_codes[g][:].bitcast(U16).rearrange("p (a t m) -> p a t m", a=PASSES, t=PACK)
+            words = words.rearrange("p (a m t) -> p a t m", a=PASSES, t=PACK)
+            if g == INPUT:
+                for a in range(PASSES):
+                    nc.gpsimd.tensor_copy(dealt[:, a], words[:, a])
+            else:
+                nc.vector.tensor_copy(dealt, words)
 
         states = {}
 
@@ -131,10 +136,10 @@ def tile_list_term_tree_cell_kernel(tc, tab_words, tab_scales, offs, wg_words, w
 
         deal_wg(INPUT)
         gather(0, 0)
-        wu_raw.append(load_wu(1, WG_HALF + WU_PASS, 1))
-        gains = shared.tile([P, PACK], F32, name="gains", align_bytes=ALIGN, offset=WU_END)
+        load_wu(1)
+        gains = shared.tile([P, PACK], F32, name="gains", align_bytes=ALIGN, offset=AT_GAINS)
         nc.sync.dma_start(gains[:], gain.rearrange("(p t) -> p t", t=PACK))
-        planes.append(shared.tile([P, PASSES * LATE], U8, name="planes1", align_bytes=ALIGN, offset=WU_END + ALIGN))
+        planes.append(shared.tile([P, PASSES * LATE], U8, name="planes1", align_bytes=ALIGN, offset=AT_PLANES))
         nc.gpsimd.memset(planes[1][:].bitcast(I32), 0)
         place(1)
         gather(0, 1)
@@ -147,19 +152,16 @@ def tile_list_term_tree_cell_kernel(tc, tab_words, tab_scales, offs, wg_words, w
             wu_bf = keep.tile([P, PACK, P, PACK], BF16, name=f"wu_bf{a}", align_bytes=ALIGN)
             wu_codes.append(keep.tile([P, H], U32, name=f"wu_codes{a}", align_bytes=ALIGN))
             wu_scales.append(keep.tile([P, H], U8, name=f"wu_scales{a}", align_bytes=ALIGN))
-            rows = P // len(wu_raw[a])
-            for part, piece in enumerate(wu_raw[a]):
-                for t in (0, 2):
-                    nc.vector.tensor_copy(
-                        wu_bf[:, t:t + 2, part * rows:(part + 1) * rows].rearrange("p t m i -> p m i t"),
-                        piece[:].rearrange("p i (m t) -> p m i t", t=PACK)[:, :, :, t:t + 2])
+            rows = wu_raw[:, a * PACK * H:(a + 1) * PACK * H].rearrange("p (i m t) -> p m i t", i=PACK, t=PACK)
+            for t in (0, 2):
+                nc.vector.tensor_copy(wu_bf[:, t:t + 2].rearrange("p t m i -> p m i t"), rows[:, :, :, t:t + 2])
             step = 2 if a else PACK
             for t in range(0, PACK, step):
                 cols = slice(t * P, (t + step) * P)
                 nc.vector.quantize_mx(wu_codes[a][:, cols].bitcast(FP8X4), wu_scales[a][:, cols],
                                       wu_bf[:, t:t + step].rearrange("p t m i -> p (t m i)"))
 
-        cells = keep.tile([P, PACK * S], F32, name="cells", tag="table0", align_bytes=ALIGN)
+        cells = shared.tile([P, PACK * S], F32, name="cells", align_bytes=ALIGN, offset=0)
         cell_rows = cell.rearrange("(p t) j -> p t j", t=PACK)
 
         def chunk_view(tile, first, width):
@@ -171,7 +173,7 @@ def tile_list_term_tree_cell_kernel(tc, tab_words, tab_scales, offs, wg_words, w
                 nc.sync.dma_start(chunk_view(cells, first, width)[:, t:t + step, :],
                                   cell_rows[:, t:t + step, first:first + width])
 
-        wo_codes = keep.tile([P, N], I32, name="wo_codes", tag="table1", align_bytes=ALIGN)
+        wo_codes = shared.tile([P, N], I32, name="wo_codes", align_bytes=ALIGN, offset=AT_WO)
         nc.sync.dma_start(wo_codes[:], wo_words[0].rearrange("p c i -> p (c i)").bitcast(I32))
 
         identity = keep.tile([P, P], F32, name="identity")

@@ -56,6 +56,20 @@ def tile_list_term_tree_cell_kernel(tc, tab_words, tab_scales, offs, wg_words, w
         offsets = keep.tile([P, S // GROUP], U16, name="offsets")
         nc.sync.dma_start(offsets[:], offs)
 
+        def load_wg(g, offset):
+            words = shared.tile([P, PASSES, H // 2], I32, name=f"wg_raw{g}", align_bytes=ALIGN, offset=offset)
+            nc.sync.dma_start(words[:], wg_words.bitcast(I32).rearrange("a p (g c) -> g p a c", g=2)[g])
+            return words
+
+        wg_raw = [load_wg(INPUT, AT_WG_INPUT)]
+        wg_codes = [keep.tile([P, WG_HALF], U8, name=f"wg_codes{g}", align_bytes=ALIGN) for g in (INPUT, FORGET)]
+
+        def deal_wg(g, passes, engine):
+            words = wg_raw[g][:].rearrange("p a c -> p (a c)").bitcast(U16)
+            dealt = wg_codes[g][:].bitcast(U16).rearrange("p (a t m) -> p a t m", a=PASSES, t=PACK)
+            engine.tensor_copy(dealt[:, passes], words.rearrange("p (a m t) -> p a t m", a=PASSES, t=PACK)[:, passes])
+
+        deal_wg(INPUT, 0, nc.gpsimd)
         tab_rows = keep.tile([P, T], U8, name="tab_rows", tag="tab_rows", align_bytes=ALIGN)
         wg_rows = keep.tile([P, 2 * H], U8, name="wg_rows", align_bytes=ALIGN)[:]
         staged = [keep.tile([P, width], U8, name=f"staged{half}", align_bytes=ALIGN)
@@ -75,16 +89,10 @@ def tile_list_term_tree_cell_kernel(tc, tab_words, tab_scales, offs, wg_words, w
             queue.dma_start(words[:], tab_words[a].rearrange("p t i -> p (t i)").bitcast(I32))
             return words
 
-        def load_wg(g, offset):
-            words = shared.tile([P, PASSES, H // 2], I32, name=f"wg_raw{g}", align_bytes=ALIGN, offset=offset)
-            nc.sync.dma_start(words[:], wg_words.bitcast(I32).rearrange("a p (g c) -> g p a c", g=2)[g])
-            return words
-
         def load_wu(a):
             rows = wu[a * P * PACK:(a + 1) * P * PACK, :].rearrange("(p i) r -> p (i r)", i=PACK)
             nc.sync.dma_start(wu_raw[:, a * PACK * H:(a + 1) * PACK * H], rows)
 
-        wg_raw = [load_wg(INPUT, AT_WG_INPUT)]
         table = [load_table(0, nc.sync)]
         table.append(load_table(1, nc.sync))
 
@@ -111,18 +119,6 @@ def tile_list_term_tree_cell_kernel(tc, tab_words, tab_scales, offs, wg_words, w
             first += a * (LATE if half else EARLY)
             return planes[half][:, first:first + width]
 
-        wg_codes = [keep.tile([P, WG_HALF], U8, name=f"wg_codes{g}", tag=f"wg_codes{g}", align_bytes=ALIGN) for g in (INPUT, FORGET)]
-
-        def deal_wg(g):
-            words = wg_raw[g][:].rearrange("p a c -> p (a c)").bitcast(U16)
-            dealt = wg_codes[g][:].bitcast(U16).rearrange("p (a t m) -> p a t m", a=PASSES, t=PACK)
-            words = words.rearrange("p (a m t) -> p a t m", a=PASSES, t=PACK)
-            if g == INPUT:
-                for a in range(PASSES):
-                    nc.gpsimd.tensor_copy(dealt[:, a], words[:, a])
-            else:
-                nc.vector.tensor_copy(dealt, words)
-
         states = {}
 
         def gather(a, half):
@@ -134,7 +130,7 @@ def tile_list_term_tree_cell_kernel(tc, tab_words, tab_scales, offs, wg_words, w
                 entries = offsets[:, first // GROUP:(first + width) // GROUP]
                 nc.vector.tensor_copy(states[a, half][:, lo:lo + width], table[a][:].bitcast(U32).indirect(entries))
 
-        deal_wg(INPUT)
+        deal_wg(INPUT, 1, nc.gpsimd)
         gather(0, 0)
         load_wu(1)
         gains = shared.tile([P, PACK], F32, name="gains", align_bytes=ALIGN, offset=AT_GAINS)
@@ -144,7 +140,7 @@ def tile_list_term_tree_cell_kernel(tc, tab_words, tab_scales, offs, wg_words, w
         place(1)
         gather(0, 1)
         gather(1, 0)
-        deal_wg(FORGET)
+        deal_wg(FORGET, slice(0, PASSES), nc.vector)
         gather(1, 1)
 
         wu_codes, wu_scales = [], []

@@ -218,8 +218,8 @@ def tile_list_term_tree_cell_kernel(tc, tab_words, tab_scales, offs, wg_words, w
 
         def add(first, width):
             h_bf = rounded(first, width)
-            one, other = [term.rearrange("p t (c i) -> p c t i", i=2) for term in terms(first, width)]
-            nc.vector.tensor_tensor(h_bf[:].rearrange("p (c i) t -> p c t i", i=2), one, other, ADD)
+            one, other = [term.rearrange("p t (c i) -> p c t i", i=4) for term in terms(first, width)]
+            nc.vector.tensor_tensor(h_bf[:].rearrange("p (c i) t -> p c t i", i=4), one, other, ADD)
             return first, width, h_bf
 
         def add_turned(first):

@@ -67,7 +67,9 @@ def tile_list_term_tree_cell_kernel(tc, tab_words, tab_scales, offs, wg_words, w
         def deal_wg(g, passes, engine):
             words = wg_raw[g][:].rearrange("p a c -> p (a c)").bitcast(U16)
             dealt = wg_codes[g][:].bitcast(U16).rearrange("p (a t m) -> p a t m", a=PASSES, t=PACK)
-            engine.tensor_copy(dealt[:, passes], words.rearrange("p (a m t) -> p a t m", a=PASSES, t=PACK)[:, passes])
+            dealt = dealt.rearrange("p a t (b m) -> p a b t m", m=8)
+            words = words.rearrange("p (a b m t) -> p a b t m", a=PASSES, m=8, t=PACK)
+            engine.tensor_copy(dealt[:, passes], words[:, passes])
 
         deal_wg(INPUT, 0, nc.gpsimd)
         tab_rows = keep.tile([P, T], U8, name="tab_rows", tag="tab_rows", align_bytes=ALIGN)
@@ -290,10 +292,11 @@ def tile_list_term_tree_cell_kernel(tc, tab_words, tab_scales, offs, wg_words, w
             second_stage(chunk, nc.scalar.copy, "words", 2)
         quantise(*sum_a)
         second_stage(OUTS[1], nc.scalar.copy)
-        sum_d, sum_e = add(768, 128), add(896, 128)
+        sum_d = add(768, 128)
         quantise(*sum_b)
+        sum_e = add(896, 128)
         quantise(*sum_d)
         quantise(*sum_e)
-        second_stage(OUTS[2], nc.vector.tensor_copy)
-        second_stage(OUTS[4], nc.vector.tensor_copy)
+        second_stage(OUTS[2], nc.scalar.copy)
+        second_stage(OUTS[4], nc.scalar.copy)
         second_stage(OUTS[5], nc.vector.tensor_copy)

@@ -29,7 +29,7 @@ INPUT, FORGET, CANDIDATE = 0, 1, 2
 ALIGN = 64
 
 EARLY = BANK + 2 * H
-LATE = BANK + P
+LATE = BANK
 WG_HALF = PASSES * H * 2
 WU_PASS = PACK * H * 4
 
@@ -38,10 +38,12 @@ RING = 4
 OUTS = ((0, 256), (256, 128), (384, 128), (512, 256), (768, 128), (896, 128))
 AT_WO = PACK * S * 4
 AT_WG_FORGET = AT_WO - ALIGN
-AT_GAINS = AT_WG_FORGET + WG_HALF
-AT_PLANES = AT_GAINS + ALIGN
-AT_WU = AT_PLANES + PASSES * LATE
-AT_WG_INPUT = AT_GAINS - ALIGN
+AT_WG_INPUT = AT_WG_FORGET + WG_HALF - ALIGN
+AT_GAINS = AT_WG_INPUT + ALIGN
+AT_WU = AT_GAINS + ALIGN
+AT_INPUT = AT_WU + PASSES * WU_PASS
+AT_PICKED = AT_INPUT + WG_HALF // PASSES - ALIGN
+AT_PLANES = AT_PICKED + BANK - ALIGN
 ZEROED_BY_VECTOR = 3 * T // 4
 
 
@@ -56,26 +58,24 @@ def tile_list_term_tree_cell_kernel(tc, tab_words, tab_scales, offs, wg_words, w
         offsets = keep.tile([P, S // GROUP], U16, name="offsets")
         nc.sync.dma_start(offsets[:], offs)
 
-        def load_wg(g, offset):
-            words = shared.tile([P, PASSES, H // 2], I32, name=f"wg_raw{g}", align_bytes=ALIGN, offset=offset)
-            nc.sync.dma_start(words[:], wg_words.bitcast(I32).rearrange("a p (g c) -> g p a c", g=2)[g])
-            return words
+        wg_halves = wg_words.bitcast(I32).rearrange("a p (g c) -> g p a c", g=2)
+        input_raw = [keep.tile([P, H // 2], I32, name="input_raw0", align_bytes=ALIGN),
+                     shared.tile([P, H // 2], I32, name="input_raw1", align_bytes=ALIGN, offset=AT_WG_INPUT)]
+        for a in range(PASSES):
+            nc.sync.dma_start(input_raw[a][:], wg_halves[INPUT, :, a])
+        forget_codes = keep.tile([P, PASSES, 2 * H], U8, name="forget_codes", align_bytes=ALIGN)
+        wg_codes = {(INPUT, 0): keep.tile([P, 2 * H], U8, name="input_codes0", align_bytes=ALIGN)[:],
+                    (INPUT, 1): shared.tile([P, 2 * H], U8, name="input_codes1", align_bytes=ALIGN, offset=AT_INPUT)[:],
+                    (FORGET, 0): forget_codes[:, 0], (FORGET, 1): forget_codes[:, 1]}
 
-        wg_raw = [load_wg(INPUT, AT_WG_INPUT)]
-        wg_codes = [keep.tile([P, WG_HALF], U8, name=f"wg_codes{g}", align_bytes=ALIGN) for g in (INPUT, FORGET)]
+        def deal_wg(engine, dealt, raw):
+            engine.tensor_copy(dealt.bitcast(U16).rearrange("p (a t b m) -> p a b t m", t=PACK, b=P // 8, m=8),
+                               raw.bitcast(U16).rearrange("p (a b m t) -> p a b t m", b=P // 8, m=8, t=PACK))
 
-        def deal_wg(g, passes, engine):
-            words = wg_raw[g][:].rearrange("p a c -> p (a c)").bitcast(U16)
-            dealt = wg_codes[g][:].bitcast(U16).rearrange("p (a t m) -> p a t m", a=PASSES, t=PACK)
-            dealt = dealt.rearrange("p a t (b m) -> p a b t m", m=8)
-            words = words.rearrange("p (a b m t) -> p a b t m", a=PASSES, m=8, t=PACK)
-            engine.tensor_copy(dealt[:, passes], words[:, passes])
-
-        deal_wg(INPUT, 0, nc.gpsimd)
+        deal_wg(nc.gpsimd, wg_codes[INPUT, 0], input_raw[0][:])
         tab_rows = keep.tile([P, T], U8, name="tab_rows", tag="tab_rows", align_bytes=ALIGN)
         wg_rows = keep.tile([P, 2 * H], U8, name="wg_rows", align_bytes=ALIGN)[:]
-        staged = [keep.tile([P, width], U8, name=f"staged{half}", align_bytes=ALIGN)
-                  for half, width in enumerate((EARLY, LATE))]
+        staged = [keep.tile([P, EARLY], U8, name="staged", align_bytes=ALIGN)]
         planes = [keep.tile([P, PASSES * EARLY], U8, name="planes0", align_bytes=ALIGN)]
         nc.vector.memset(tab_rows[:, :ZEROED_BY_VECTOR].bitcast(I32), 0)
         nc.gpsimd.memset(tab_rows[:, ZEROED_BY_VECTOR:].bitcast(I32), 0)
@@ -83,8 +83,6 @@ def tile_list_term_tree_cell_kernel(tc, tab_words, tab_scales, offs, wg_words, w
         nc.vector.memset(planes[0][:].bitcast(I32), 0)
         nc.sync.dma_start(tab_rows[0:P:4, :].bitcast(I32), tab_scales.bitcast(I32).rearrange("a q t -> q a t"))
         nc.sync.dma_start(wg_rows[0:P:4, :].bitcast(I32), wg_scales.bitcast(I32).rearrange("a q c -> q a c"))
-        nc.sync.dma_start(staged[1][0:P:4, BANK:].bitcast(I32),
-                          wo_scales[0].bitcast(I32).rearrange("q (n c) -> (q n) c", n=N // P))
 
         def load_table(a, queue):
             words = keep.tile([P, T], I32, name=f"table{a}", tag=f"table{a}", align_bytes=ALIGN)
@@ -98,13 +96,15 @@ def tile_list_term_tree_cell_kernel(tc, tab_words, tab_scales, offs, wg_words, w
         table = [load_table(0, nc.sync)]
         table.append(load_table(1, nc.sync))
 
-        picked_rows = keep.tile([P, S], U8, name="picked_rows", align_bytes=ALIGN)
-        nc.vector.tensor_copy(picked_rows[:], tab_rows[:].indirect(offsets[:]))
         nc.gpsimd.tensor_copy(staged[0][:, BANK:].rearrange("p (g t m) -> p g t m", g=2, t=PACK),
                               wg_rows.rearrange("p (g m t) -> p g t m", g=2, t=PACK))
-        for half in (1, 0):
-            nc.vector.tensor_copy(staged[half][:, :BANK].bitcast(I32),
-                                  picked_rows[:, half * BANK:(half + 1) * BANK].bitcast(I32))
+        picked = [shared.tile([P, BANK], U8, name="picked0", align_bytes=ALIGN, offset=AT_PICKED),
+                  keep.tile([P, BANK], U8, name="picked1", align_bytes=ALIGN)]
+        for half in range(2):
+            entries = offsets[:, half * BANK // GROUP:(half + 1) * BANK // GROUP]
+            nc.vector.tensor_copy(picked[half][:], tab_rows[:].indirect(entries))
+        nc.vector.tensor_copy(staged[0][:, :BANK].bitcast(I32), picked[0][:].bitcast(I32))
+        staged.append(picked[1])
 
         def place(half):
             for d in (0, 2, 1, 3):
@@ -113,7 +113,8 @@ def tile_list_term_tree_cell_kernel(tc, tab_words, tab_scales, offs, wg_words, w
                                   staged[half][first:first + QUADRANT:4, :].bitcast(I32))
 
         place(0)
-        wg_raw.append(load_wg(FORGET, AT_WG_FORGET))
+        forget_raw = shared.tile([P, PASSES, H // 2], I32, name="forget_raw", align_bytes=ALIGN, offset=AT_WG_FORGET)
+        nc.sync.dma_start(forget_raw[:], wg_halves[FORGET])
         wu_raw = shared.tile([P, PASSES * PACK * H], F32, name="wu_raw", align_bytes=ALIGN, offset=AT_WU)
         load_wu(0)
 
@@ -132,7 +133,7 @@ def tile_list_term_tree_cell_kernel(tc, tab_words, tab_scales, offs, wg_words, w
                 entries = offsets[:, first // GROUP:(first + width) // GROUP]
                 nc.vector.tensor_copy(states[a, half][:, lo:lo + width], table[a][:].bitcast(U32).indirect(entries))
 
-        deal_wg(INPUT, 1, nc.gpsimd)
+        deal_wg(nc.gpsimd, wg_codes[INPUT, 1], input_raw[1][:])
         gather(0, 0)
         load_wu(1)
         gains = shared.tile([P, PACK], F32, name="gains", align_bytes=ALIGN, offset=AT_GAINS)
@@ -142,7 +143,7 @@ def tile_list_term_tree_cell_kernel(tc, tab_words, tab_scales, offs, wg_words, w
         place(1)
         gather(0, 1)
         gather(1, 0)
-        deal_wg(FORGET, slice(0, PASSES), nc.vector)
+        deal_wg(nc.vector, forget_codes[:].rearrange("p a c -> p (a c)"), forget_raw[:].rearrange("p a c -> p (a c)"))
         gather(1, 1)
 
         wu_codes, wu_scales = [], []
@@ -174,6 +175,12 @@ def tile_list_term_tree_cell_kernel(tc, tab_words, tab_scales, offs, wg_words, w
         wo_codes = shared.tile([P, N], I32, name="wo_codes", align_bytes=ALIGN, offset=AT_WO)
         nc.sync.dma_start(wo_codes[:], wo_words[0].rearrange("p c i -> p (c i)").bitcast(I32))
 
+        wo_plane = shared.tile([P, N], U8, name="wo_plane", align_bytes=ALIGN, offset=AT_WO + N * PACK)
+        nc.vector.memset(wo_plane[:].bitcast(I32), 0)
+        for d in range(P // QUADRANT):
+            nc.sync.dma_start(wo_plane[QUADRANT * d:QUADRANT * d + 4, :].bitcast(I32),
+                              wo_scales[0, 4 * d:4 * d + 4, :].bitcast(I32))
+
         identity = keep.tile([P, P], F32, name="identity")
         make_identity(nc, identity[:])
 
@@ -194,8 +201,7 @@ def tile_list_term_tree_cell_kernel(tc, tab_words, tab_scales, offs, wg_words, w
                         codes = wu_codes[a][:, t * P:(t + 1) * P].bitcast(FP8X4)
                         scales = wu_scales[a][:, t * P:(t + 1) * P]
                     else:
-                        at = (a * PACK + t) * P * 2
-                        codes = wg_codes[kind][:, at:at + P * 2].bitcast(FP4X4)
+                        codes = wg_codes[kind, a][:, t * P * 2:(t + 1) * P * 2].bitcast(FP4X4)
                         scales = plane(0, a, BANK + kind * H + t * P, P)
                     words = states[a, first // BANK][:, first % BANK:first % BANK + width]
                     nc.tensor.matmul_mx(acc[:, t - t0, :], lhsT=codes, lhsT_scale=scales,
@@ -261,7 +267,7 @@ def tile_list_term_tree_cell_kernel(tc, tab_words, tab_scales, offs, wg_words, w
             acc = psum.tile([P, N // P, width], F32, name="acc", tag=tag, bufs=bufs)
             for n in range(N // P):
                 nc.tensor.matmul_mx(acc[:, n, :], lhsT=wo_codes[:, n * P:(n + 1) * P].bitcast(FP8X4),
-                                    lhsT_scale=plane(1, n, BANK, P), rhs=h_codes[first][:].bitcast(FP8X4),
+                                    lhsT_scale=wo_plane[:, n * P:(n + 1) * P], rhs=h_codes[first][:].bitcast(FP8X4),
                                     rhs_scale=h_scales[first][:], start=True, stop=True)
             result = keep.tile([P, N // P, width], F32, name=f"result{first}")
             copy(result[:], acc[:])

@@ -29,7 +29,7 @@ INPUT, FORGET, CANDIDATE = 0, 1, 2
 ALIGN = 64
 
 EARLY = BANK + 2 * H
-LATE = BANK
+LATE = BANK // 2
 WG_HALF = PASSES * H * 2
 WU_PASS = PACK * H * 4
 
@@ -98,19 +98,22 @@ def tile_list_term_tree_cell_kernel(tc, tab_words, tab_scales, offs, wg_words, w
 
         nc.gpsimd.tensor_copy(staged[0][:, BANK:].rearrange("p (g t m) -> p g t m", g=2, t=PACK),
                               wg_rows.rearrange("p (g m t) -> p g t m", g=2, t=PACK))
-        picked = [shared.tile([P, BANK], U8, name="picked0", align_bytes=ALIGN, offset=AT_PICKED),
-                  keep.tile([P, BANK], U8, name="picked1", align_bytes=ALIGN)]
-        for half in range(2):
-            entries = offsets[:, half * BANK // GROUP:(half + 1) * BANK // GROUP]
-            nc.vector.tensor_copy(picked[half][:], tab_rows[:].indirect(entries))
-        nc.vector.tensor_copy(staged[0][:, :BANK].bitcast(I32), picked[0][:].bitcast(I32))
-        staged.append(picked[1])
+        def pick_scales(first, picked):
+            entries = offsets[:, first // GROUP:(first + picked.shape[1]) // GROUP]
+            nc.vector.tensor_copy(picked[:], tab_rows[:].indirect(entries))
+            return picked
 
-        def place(half):
+        picked = pick_scales(0, shared.tile([P, BANK], U8, name="picked0", align_bytes=ALIGN, offset=AT_PICKED))
+        staged.append(pick_scales(BANK, keep.tile([P, LATE], U8, name="picked1", align_bytes=ALIGN)))
+        nc.vector.tensor_copy(staged[0][:, :BANK].bitcast(I32), picked[:].bitcast(I32))
+        staged.append(pick_scales(BANK + LATE, shared.tile([P, LATE], U8, name="picked2", align_bytes=ALIGN,
+                                                           offset=AT_PICKED + ALIGN)))
+
+        def place(chunk):
             for d in (0, 2, 1, 3):
                 first = QUADRANT * d
-                nc.sync.dma_start(planes[half][first:first + 4, :].bitcast(I32),
-                                  staged[half][first:first + QUADRANT:4, :].bitcast(I32))
+                nc.sync.dma_start(planes[chunk][first:first + 4, :].bitcast(I32),
+                                  staged[chunk][first:first + QUADRANT:4, :].bitcast(I32))
 
         place(0)
         forget_raw = shared.tile([P, PASSES, H // 2], I32, name="forget_raw", align_bytes=ALIGN, offset=AT_WG_FORGET)
@@ -118,9 +121,9 @@ def tile_list_term_tree_cell_kernel(tc, tab_words, tab_scales, offs, wg_words, w
         wu_raw = shared.tile([P, PASSES * PACK * H], F32, name="wu_raw", align_bytes=ALIGN, offset=AT_WU)
         load_wu(0)
 
-        def plane(half, a, first, width):
-            first += a * (LATE if half else EARLY)
-            return planes[half][:, first:first + width]
+        def plane(chunk, a, first, width):
+            first += a * (LATE if chunk else EARLY)
+            return planes[chunk][:, first:first + width]
 
         states = {}
 
@@ -166,17 +169,24 @@ def tile_list_term_tree_cell_kernel(tc, tab_words, tab_scales, offs, wg_words, w
         def chunk_view(tile, first, width):
             return tile[:, PACK * first:PACK * (first + width)].rearrange("p (t j) -> p t j", t=PACK)
 
-        for first, width in CHUNKS:
+        def load_cells(first, width):
             step = 2 * BANK // width
             for t in range(0, PACK, step):
                 nc.sync.dma_start(chunk_view(cells, first, width)[:, t:t + step, :],
                                   cell_rows[:, t:t + step, first:first + width])
 
+        load_cells(*CHUNKS[0])
+        last_planes = shared.tile([P, PASSES * LATE + N], U8, name="last_planes", align_bytes=ALIGN, offset=AT_WO + N * PACK)
+        nc.vector.memset(last_planes[:].bitcast(I32), 0)
+        planes.append(last_planes[:, :PASSES * LATE])
+        place(2)
+        for chunk in CHUNKS[1:]:
+            load_cells(*chunk)
+
         wo_codes = shared.tile([P, N], I32, name="wo_codes", align_bytes=ALIGN, offset=AT_WO)
         nc.sync.dma_start(wo_codes[:], wo_words[0].rearrange("p c i -> p (c i)").bitcast(I32))
 
-        wo_plane = shared.tile([P, N], U8, name="wo_plane", align_bytes=ALIGN, offset=AT_WO + N * PACK)
-        nc.vector.memset(wo_plane[:].bitcast(I32), 0)
+        wo_plane = last_planes[:, PASSES * LATE:]
         for d in range(P // QUADRANT):
             nc.sync.dma_start(wo_plane[QUADRANT * d:QUADRANT * d + 4, :].bitcast(I32),
                               wo_scales[0, 4 * d:4 * d + 4, :].bitcast(I32))
@@ -205,7 +215,7 @@ def tile_list_term_tree_cell_kernel(tc, tab_words, tab_scales, offs, wg_words, w
                         scales = plane(0, a, BANK + kind * H + t * P, P)
                     words = states[a, first // BANK][:, first % BANK:first % BANK + width]
                     nc.tensor.matmul_mx(acc[:, t - t0, :], lhsT=codes, lhsT_scale=scales,
-                                        rhs=words.bitcast(FP8X4), rhs_scale=plane(first // BANK, a, first % BANK, width),
+                                        rhs=words.bitcast(FP8X4), rhs_scale=plane([c for c, w in CHUNKS].index(start), a, first - start, width),
                                         start=(a, t) == (passes[0], t0), stop=(a, t) == (passes[-1], t0 + step - 1))
             nc.scalar.activation(acts[start][:, kind, t0:t0 + step, cols], acc[:], TANH if kind == CANDIDATE else SIGMOID)
             for t in range(t0, t0 + step):

@@ -40,7 +40,8 @@ AT_WO = PACK * S * 4
 AT_WG_FORGET = AT_WO - ALIGN
 AT_WG_INPUT = AT_WG_FORGET + WG_HALF - ALIGN
 AT_GAINS = AT_WG_INPUT + ALIGN
-AT_WU = AT_GAINS + ALIGN
+AT_IDENTITY = AT_GAINS + ALIGN
+AT_WU = AT_IDENTITY + P * 4
 AT_INPUT = AT_WU + PASSES * WU_PASS
 AT_PICKED = AT_INPUT + WG_HALF // PASSES - ALIGN
 AT_PLANES = AT_PICKED + BANK - ALIGN
@@ -79,7 +80,7 @@ def tile_list_term_tree_cell_kernel(tc, tab_words, tab_scales, offs, wg_words, w
         planes = [keep.tile([P, PASSES * EARLY], U8, name="planes0", align_bytes=ALIGN)]
         nc.vector.memset(tab_rows[:, :ZEROED_BY_VECTOR].bitcast(I32), 0)
         nc.gpsimd.memset(tab_rows[:, ZEROED_BY_VECTOR:].bitcast(I32), 0)
-        nc.gpsimd.memset(wg_rows.bitcast(I32), 0)
+        nc.vector.memset(wg_rows.bitcast(I32), 0)
         nc.vector.memset(planes[0][:].bitcast(I32), 0)
         nc.sync.dma_start(tab_rows[0:P:4, :].bitcast(I32), tab_scales.bitcast(I32).rearrange("a q t -> q a t"))
         nc.sync.dma_start(wg_rows[0:P:4, :].bitcast(I32), wg_scales.bitcast(I32).rearrange("a q c -> q a c"))
@@ -191,7 +192,7 @@ def tile_list_term_tree_cell_kernel(tc, tab_words, tab_scales, offs, wg_words, w
             nc.sync.dma_start(wo_plane[QUADRANT * d:QUADRANT * d + 4, :].bitcast(I32),
                               wo_scales[0, 4 * d:4 * d + 4, :].bitcast(I32))
 
-        identity = keep.tile([P, P], F32, name="identity")
+        identity = shared.tile([P, P], F32, name="identity", align_bytes=ALIGN, offset=AT_IDENTITY)
         make_identity(nc, identity[:])
 
         acts = {first: keep.tile([P, 3, PACK, width], F32, name=f"acts{first}") for first, width in CHUNKS}

@@ -147,7 +147,7 @@ def tile_list_term_tree_cell_kernel(tc, tab_words, tab_scales, offs, wg_words, w
         place(1)
         gather(0, 1)
         gather(1, 0)
-        deal_wg(nc.vector, forget_codes[:].rearrange("p a c -> p (a c)"), forget_raw[:].rearrange("p a c -> p (a c)"))
+        deal_wg(nc.gpsimd, forget_codes[:].rearrange("p a c -> p (a c)"), forget_raw[:].rearrange("p a c -> p (a c)"))
         gather(1, 1)
 
         wu_codes, wu_scales = [], []
@@ -178,7 +178,7 @@ def tile_list_term_tree_cell_kernel(tc, tab_words, tab_scales, offs, wg_words, w
 
         load_cells(*CHUNKS[0])
         last_planes = shared.tile([P, PASSES * LATE + N], U8, name="last_planes", align_bytes=ALIGN, offset=AT_WO + N * PACK)
-        nc.vector.memset(last_planes[:].bitcast(I32), 0)
+        nc.gpsimd.memset(last_planes[:].bitcast(I32), 0)
         planes.append(last_planes[:, :PASSES * LATE])
         place(2)
         for chunk in CHUNKS[1:]:

@@ -90,9 +90,12 @@ def tile_list_term_tree_cell_kernel(tc, tab_words, tab_scales, offs, wg_words, w
             queue.dma_start(words[:], tab_words[a].rearrange("p t i -> p (t i)").bitcast(I32))
             return words
 
-        def load_wu(a):
-            rows = wu[a * P * PACK:(a + 1) * P * PACK, :].rearrange("(p i) r -> p (i r)", i=PACK)
-            nc.sync.dma_start(wu_raw[:, a * PACK * H:(a + 1) * PACK * H], rows)
+        def load_wu(a, first, width):
+            at = a * PACK * H + PACK * first
+            rows = wu_raw[:, at:at + PACK * width].rearrange("p (i r) -> p i r", i=PACK)
+            nc.sync.dma_start(rows, wu[a * P * PACK:(a + 1) * P * PACK, first:first + width]
+                              .rearrange("(p i) r -> p i r", i=PACK))
+            return first, width, rows
 
         table = [load_table(0, nc.sync)]
         table.append(load_table(1, nc.sync))
@@ -120,7 +123,7 @@ def tile_list_term_tree_cell_kernel(tc, tab_words, tab_scales, offs, wg_words, w
         forget_raw = shared.tile([P, PASSES, H // 2], I32, name="forget_raw", align_bytes=ALIGN, offset=AT_WG_FORGET)
         nc.sync.dma_start(forget_raw[:], wg_halves[FORGET])
         wu_raw = shared.tile([P, PASSES * PACK * H], F32, name="wu_raw", align_bytes=ALIGN, offset=AT_WU)
-        load_wu(0)
+        wu_parts = [[load_wu(0, first, H // 2) for first in (0, H // 2)]]
 
         def plane(chunk, a, first, width):
             first += a * (LATE if chunk else EARLY)
@@ -139,7 +142,7 @@ def tile_list_term_tree_cell_kernel(tc, tab_words, tab_scales, offs, wg_words, w
 
         deal_wg(nc.gpsimd, wg_codes[INPUT, 1], input_raw[1][:])
         gather(0, 0)
-        load_wu(1)
+        wu_parts.append([load_wu(1, first, H // 2) for first in (0, H // 2)])
         gains = shared.tile([P, PACK], F32, name="gains", align_bytes=ALIGN, offset=AT_GAINS)
         nc.sync.dma_start(gains[:], gain.rearrange("(p t) -> p t", t=PACK))
         planes.append(shared.tile([P, PASSES * LATE], U8, name="planes1", align_bytes=ALIGN, offset=AT_PLANES))
@@ -155,9 +158,11 @@ def tile_list_term_tree_cell_kernel(tc, tab_words, tab_scales, offs, wg_words, w
             wu_bf = keep.tile([P, PACK, P, PACK], BF16, name=f"wu_bf{a}", align_bytes=ALIGN)
             wu_codes.append(keep.tile([P, H], U32, name=f"wu_codes{a}", align_bytes=ALIGN))
             wu_scales.append(keep.tile([P, H], U8, name=f"wu_scales{a}", align_bytes=ALIGN))
-            rows = wu_raw[:, a * PACK * H:(a + 1) * PACK * H].rearrange("p (i m t) -> p m i t", i=PACK, t=PACK)
-            for t in (0, 2):
-                nc.vector.tensor_copy(wu_bf[:, t:t + 2].rearrange("p t m i -> p m i t"), rows[:, :, :, t:t + 2])
+            for first, width, rows in wu_parts[a]:
+                channels = slice(first // PACK, (first + width) // PACK)
+                for t in (0, 2):
+                    nc.vector.tensor_copy(wu_bf[:, t:t + 2, channels].rearrange("p t m i -> p m i t"),
+                                          rows.rearrange("p i (m t) -> p m i t", t=PACK)[:, :, :, t:t + 2])
             step = 2 if a else PACK
             for t in range(0, PACK, step):
                 cols = slice(t * P, (t + step) * P)

@@ -142,6 +142,11 @@ def tile_list_term_tree_cell_kernel(tc, tab_words, tab_scales, offs, wg_words, w
 
         deal_wg(nc.gpsimd, wg_codes[INPUT, 1], input_raw[1][:])
         gather(0, 0)
+        unread = psum.tile([P, BANK], F32, name="unread")
+        for t in range(2):
+            nc.tensor.matmul_mx(unread[:], lhsT=wg_codes[INPUT, 0][:, t * 2 * P:(t + 1) * 2 * P].bitcast(FP4X4),
+                                lhsT_scale=staged[0][:, BANK:BANK + P], rhs=states[0, 0][:, :BANK].bitcast(FP8X4),
+                                rhs_scale=staged[0][:, :BANK], start=True, stop=True)
         wu_parts.append([load_wu(1, first, H // 2) for first in (0, H // 2)])
         gains = shared.tile([P, PACK], F32, name="gains", align_bytes=ALIGN, offset=AT_GAINS)
         nc.sync.dma_start(gains[:], gain.rearrange("(p t) -> p t", t=PACK))

@@ -28,7 +28,8 @@ BANK = 512
 INPUT, FORGET, CANDIDATE = 0, 1, 2
 ALIGN = 64
 
-EARLY = BANK + 2 * H
+FIRST_PICK = 3 * S // 4
+EARLY = FIRST_PICK + 2 * H
 LATE = BANK // 2
 WG_HALF = PASSES * H * 2
 WU_PASS = PACK * H * 4
@@ -44,7 +45,7 @@ AT_IDENTITY = AT_GAINS + ALIGN
 AT_WU = AT_IDENTITY + P * 4
 AT_INPUT = AT_WU + PASSES * WU_PASS
 AT_PICKED = AT_INPUT + WG_HALF // PASSES - ALIGN
-AT_PLANES = AT_PICKED + BANK - ALIGN
+AT_FRESH = AT_PICKED + FIRST_PICK
 ZEROED_BY_VECTOR = 3 * T // 4
 
 
@@ -100,18 +101,16 @@ def tile_list_term_tree_cell_kernel(tc, tab_words, tab_scales, offs, wg_words, w
         table = [load_table(0, nc.sync)]
         table.append(load_table(1, nc.sync))
 
-        nc.gpsimd.tensor_copy(staged[0][:, BANK:].rearrange("p (g t m) -> p g t m", g=2, t=PACK),
+        nc.gpsimd.tensor_copy(staged[0][:, FIRST_PICK:].rearrange("p (g t m) -> p g t m", g=2, t=PACK),
                               wg_rows.rearrange("p (g m t) -> p g t m", g=2, t=PACK))
         def pick_scales(first, picked):
             entries = offsets[:, first // GROUP:(first + picked.shape[1]) // GROUP]
             nc.vector.tensor_copy(picked[:], tab_rows[:].indirect(entries))
             return picked
 
-        picked = pick_scales(0, shared.tile([P, BANK], U8, name="picked0", align_bytes=ALIGN, offset=AT_PICKED))
-        staged.append(pick_scales(BANK, keep.tile([P, LATE], U8, name="picked1", align_bytes=ALIGN)))
-        nc.vector.tensor_copy(staged[0][:, :BANK].bitcast(I32), picked[:].bitcast(I32))
-        staged.append(pick_scales(BANK + LATE, shared.tile([P, LATE], U8, name="picked2", align_bytes=ALIGN,
-                                                           offset=AT_PICKED + ALIGN)))
+        picked = pick_scales(0, shared.tile([P, FIRST_PICK], U8, name="picked0", align_bytes=ALIGN, offset=AT_PICKED))
+        staged.append(pick_scales(FIRST_PICK, keep.tile([P, LATE], U8, name="picked1", align_bytes=ALIGN)))
+        nc.vector.tensor_copy(staged[0][:, :FIRST_PICK].bitcast(I32), picked[:].bitcast(I32))
 
         def place(chunk):
             for d in (0, 2, 1, 3):
@@ -145,14 +144,11 @@ def tile_list_term_tree_cell_kernel(tc, tab_words, tab_scales, offs, wg_words, w
         unread = psum.tile([P, BANK], F32, name="unread")
         for t in range(2):
             nc.tensor.matmul_mx(unread[:], lhsT=wg_codes[INPUT, 0][:, t * 2 * P:(t + 1) * 2 * P].bitcast(FP4X4),
-                                lhsT_scale=staged[0][:, BANK:BANK + P], rhs=states[0, 0][:, :BANK].bitcast(FP8X4),
+                                lhsT_scale=staged[0][:, FIRST_PICK:FIRST_PICK + P], rhs=states[0, 0][:, :BANK].bitcast(FP8X4),
                                 rhs_scale=staged[0][:, :BANK], start=True, stop=True)
         wu_parts.append([load_wu(1, first, H // 2) for first in (0, H // 2)])
         gains = shared.tile([P, PACK], F32, name="gains", align_bytes=ALIGN, offset=AT_GAINS)
         nc.sync.dma_start(gains[:], gain.rearrange("(p t) -> p t", t=PACK))
-        planes.append(shared.tile([P, PASSES * LATE], U8, name="planes1", align_bytes=ALIGN, offset=AT_PLANES))
-        nc.gpsimd.memset(planes[1][:].bitcast(I32), 0)
-        place(1)
         gather(0, 1)
         gather(1, 0)
         deal_wg(nc.gpsimd, forget_codes[:].rearrange("p a c -> p (a c)"), forget_raw[:].rearrange("p a c -> p (a c)"))
@@ -181,7 +177,7 @@ def tile_list_term_tree_cell_kernel(tc, tab_words, tab_scales, offs, wg_words, w
             return tile[:, PACK * first:PACK * (first + width)].rearrange("p (t j) -> p t j", t=PACK)
 
         def load_cells(first, width):
-            step = 2 * BANK // width
+            step = BANK // width
             for t in range(0, PACK, step):
                 nc.sync.dma_start(chunk_view(cells, first, width)[:, t:t + step, :],
                                   cell_rows[:, t:t + step, first:first + width])
@@ -190,7 +186,7 @@ def tile_list_term_tree_cell_kernel(tc, tab_words, tab_scales, offs, wg_words, w
         last_planes = shared.tile([P, PASSES * LATE + N], U8, name="last_planes", align_bytes=ALIGN, offset=AT_WO + N * PACK)
         nc.gpsimd.memset(last_planes[:].bitcast(I32), 0)
         planes.append(last_planes[:, :PASSES * LATE])
-        place(2)
+        place(1)
         for chunk in CHUNKS[1:]:
             load_cells(*chunk)
 
@@ -207,7 +203,12 @@ def tile_list_term_tree_cell_kernel(tc, tab_words, tab_scales, offs, wg_words, w
 
         acts = {first: keep.tile([P, 3, PACK, width], F32, name=f"acts{first}") for first, width in CHUNKS}
         kept = {first: keep.tile([P, PACK, width], F32, name=f"kept{first}") for first, width in CHUNKS}
-        fresh = {first: keep.tile([P, PACK, width], F32, name=f"fresh{first}") for first, width in CHUNKS}
+        fresh = {first: keep.tile([P, PACK, width], F32, name=f"fresh{first}") for first, width in CHUNKS[1:]}
+        fresh[0] = shared.tile([P, PACK, BANK], F32, name="fresh0", align_bytes=ALIGN, offset=AT_FRESH)
+        third_gate = shared.tile([P, 1, BANK], F32, name="third_gate", align_bytes=ALIGN, offset=AT_FRESH)
+
+        def activated(start, kind, t0, step=1):
+            return third_gate[:] if (start, kind, t0) == (0, FORGET, 2) else acts[start][:, kind, t0:t0 + step]
 
         def first_stage(chunk, kind, t0, part=None):
             start, whole = chunk
@@ -223,15 +224,15 @@ def tile_list_term_tree_cell_kernel(tc, tab_words, tab_scales, offs, wg_words, w
                         scales = wu_scales[a][:, t * P:(t + 1) * P]
                     else:
                         codes = wg_codes[kind, a][:, t * P * 2:(t + 1) * P * 2].bitcast(FP4X4)
-                        scales = plane(0, a, BANK + kind * H + t * P, P)
+                        scales = plane(0, a, FIRST_PICK + kind * H + t * P, P)
                     words = states[a, first // BANK][:, first % BANK:first % BANK + width]
                     nc.tensor.matmul_mx(acc[:, t - t0, :], lhsT=codes, lhsT_scale=scales,
-                                        rhs=words.bitcast(FP8X4), rhs_scale=plane([c for c, w in CHUNKS].index(start), a, first - start, width),
+                                        rhs=words.bitcast(FP8X4), rhs_scale=plane(first // FIRST_PICK, a, first % FIRST_PICK, width),
                                         start=(a, t) == (passes[0], t0), stop=(a, t) == (passes[-1], t0 + step - 1))
-            nc.scalar.activation(acts[start][:, kind, t0:t0 + step, cols], acc[:], TANH if kind == CANDIDATE else SIGMOID)
+            nc.scalar.activation(activated(start, kind, t0, step)[:, :, cols], acc[:], TANH if kind == CANDIDATE else SIGMOID)
             for t in range(t0, t0 + step):
                 if kind == FORGET:
-                    nc.vector.scalar_tensor_tensor(kept[first][:, t, :], acts[first][:, FORGET, t, :], gains[:, t:t + 1],
+                    nc.vector.scalar_tensor_tensor(kept[first][:, t, :], activated(first, FORGET, t)[:, 0], gains[:, t:t + 1],
                                                    chunk_view(cells, first, width)[:, t, :], MULT, MULT)
                 elif kind == CANDIDATE:
                     nc.vector.scalar_tensor_tensor(fresh[first][:, t, :], acts[first][:, INPUT, t, :], gains[:, t:t + 1],
@@ -296,7 +297,7 @@ def tile_list_term_tree_cell_kernel(tc, tab_words, tab_scales, offs, wg_words, w
 
         wide, middle, last = CHUNKS
         narrow = [(kind, t) for t in (0, 2) for kind in (INPUT, CANDIDATE, FORGET)]
-        ahead = [(INPUT, 0), (FORGET, 0)]
+        ahead = [(INPUT, 0), (INPUT, 2)]
         for part in ((0, 256), (256, 256)):
             for t in (0, 2):
                 first_stage(wide, INPUT, t, part)

from contextlib import ExitStack

import concourse.mybir as mybir
from concourse.masks import make_identity

K, T, S, H, N = 1024, 2048, 1024, 512, 256
FLOPS = 2 * K * 3 * H * S + 2 * H * N * S

F32 = mybir.dt.float32
BF16 = mybir.dt.bfloat16
I32 = mybir.dt.int32
U32 = mybir.dt.uint32
U16 = mybir.dt.uint16
U8 = mybir.dt.uint8
FP8X4 = mybir.dt.float8_e4m3fn_x4
FP4X4 = mybir.dt.float4_e2m1fn_x4
SIGMOID = mybir.ActivationFunctionType.Sigmoid
TANH = mybir.ActivationFunctionType.Tanh
MULT = mybir.AluOpType.mult
ADD = mybir.AluOpType.add

P = 128
PACK = 4
PASSES = K // (P * PACK)
GROUP = 16
QUADRANT = 32
BANK = 512
INPUT, FORGET, CANDIDATE = 0, 1, 2
ALIGN = 64

FIRST_PICK = 3 * S // 4
EARLY = FIRST_PICK + 2 * H
LATE = BANK // 2
WG_HALF = PASSES * H * 2
WU_PASS = PACK * H * 4

CHUNKS = ((0, 512), (512, 256), (768, 256))
RING = 4
OUTS = ((0, 256), (256, 128), (384, 128), (512, 256), (768, 128), (896, 128))
AT_WO = PACK * S * 4
AT_WG_FORGET = AT_WO - ALIGN
AT_WG_INPUT = AT_WG_FORGET + WG_HALF - ALIGN
AT_GAINS = AT_WG_INPUT + ALIGN
AT_IDENTITY = AT_GAINS + ALIGN
AT_WU = AT_IDENTITY + P * 4
AT_INPUT = AT_WU + PASSES * WU_PASS
AT_PICKED = AT_INPUT + WG_HALF // PASSES - ALIGN
AT_FRESH = AT_PICKED + FIRST_PICK
ZEROED_BY_VECTOR = 3 * T // 4


def tile_list_term_tree_cell_kernel(tc, tab_words, tab_scales, offs, wg_words, wg_scales, wu, cell, gain,
                                                 wo_words, wo_scales, out):
    nc = tc.nc
    with ExitStack() as ctx:
        keep = ctx.enter_context(tc.tile_pool(name="keep", bufs=1))
        shared = ctx.enter_context(tc.tile_pool(name="shared", bufs=1))
        psum = ctx.enter_context(tc.psum_pool(name="psum", bufs=1))

        offsets = keep.tile([P, S // GROUP], U16, name="offsets")
        nc.sync.dma_start(offsets[:], offs)

        wg_halves = wg_words.bitcast(I32).rearrange("a p (g c) -> g p a c", g=2)
        input_raw = [keep.tile([P, H // 2], I32, name="input_raw0", align_bytes=ALIGN),
                     shared.tile([P, H // 2], I32, name="input_raw1", align_bytes=ALIGN, offset=AT_WG_INPUT)]
        for a in range(PASSES):
            nc.sync.dma_start(input_raw[a][:], wg_halves[INPUT, :, a])
        forget_codes = keep.tile([P, PASSES, 2 * H], U8, name="forget_codes", align_bytes=ALIGN)
        wg_codes = {(INPUT, 0): keep.tile([P, 2 * H], U8, name="input_codes0", align_bytes=ALIGN)[:],
                    (INPUT, 1): shared.tile([P, 2 * H], U8, name="input_codes1", align_bytes=ALIGN, offset=AT_INPUT)[:],
                    (FORGET, 0): forget_codes[:, 0], (FORGET, 1): forget_codes[:, 1]}

        def deal_wg(engine, dealt, raw):
            engine.tensor_copy(dealt.bitcast(U16).rearrange("p (a t b m) -> p a b t m", t=PACK, b=P // 8, m=8),
                               raw.bitcast(U16).rearrange("p (a b m t) -> p a b t m", b=P // 8, m=8, t=PACK))

        deal_wg(nc.gpsimd, wg_codes[INPUT, 0], input_raw[0][:])
        tab_rows = keep.tile([P, T], U8, name="tab_rows", tag="tab_rows", align_bytes=ALIGN)
        wg_rows = keep.tile([P, 2 * H], U8, name="wg_rows", align_bytes=ALIGN)[:]
        staged = [keep.tile([P, EARLY], U8, name="staged", align_bytes=ALIGN)]
        planes = [keep.tile([P, PASSES * EARLY], U8, name="planes0", align_bytes=ALIGN)]
        nc.vector.memset(tab_rows[:, :ZEROED_BY_VECTOR].bitcast(I32), 0)
        nc.gpsimd.memset(tab_rows[:, ZEROED_BY_VECTOR:].bitcast(I32), 0)
        nc.vector.memset(wg_rows.bitcast(I32), 0)
        nc.vector.memset(planes[0][:].bitcast(I32), 0)
        nc.sync.dma_start(tab_rows[0:P:4, :].bitcast(I32), tab_scales.bitcast(I32).rearrange("a q t -> q a t"))
        nc.sync.dma_start(wg_rows[0:P:4, :].bitcast(I32), wg_scales.bitcast(I32).rearrange("a q c -> q a c"))

        def load_table(a, queue):
            words = keep.tile([P, T], I32, name=f"table{a}", tag=f"table{a}", align_bytes=ALIGN)
            queue.dma_start(words[:], tab_words[a].rearrange("p t i -> p (t i)").bitcast(I32))
            return words

        def load_wu(a, first, width):
            at = a * PACK * H + PACK * first
            rows = wu_raw[:, at:at + PACK * width].rearrange("p (i r) -> p i r", i=PACK)
            nc.sync.dma_start(rows, wu[a * P * PACK:(a + 1) * P * PACK, first:first + width]
                              .rearrange("(p i) r -> p i r", i=PACK))
            return first, width, rows

        table = [load_table(0, nc.sync)]
        table.append(load_table(1, nc.sync))

        nc.gpsimd.tensor_copy(staged[0][:, FIRST_PICK:].rearrange("p (g t m) -> p g t m", g=2, t=PACK),
                              wg_rows.rearrange("p (g m t) -> p g t m", g=2, t=PACK))
        def pick_scales(first, picked):
            entries = offsets[:, first // GROUP:(first + picked.shape[1]) // GROUP]
            nc.vector.tensor_copy(picked[:], tab_rows[:].indirect(entries))
            return picked

        picked = pick_scales(0, shared.tile([P, FIRST_PICK], U8, name="picked0", align_bytes=ALIGN, offset=AT_PICKED))
        staged.append(pick_scales(FIRST_PICK, keep.tile([P, LATE], U8, name="picked1", align_bytes=ALIGN)))
        nc.vector.tensor_copy(staged[0][:, :FIRST_PICK].bitcast(I32), picked[:].bitcast(I32))

        def place(chunk):
            for d in (0, 2, 1, 3):
                first = QUADRANT * d
                nc.sync.dma_start(planes[chunk][first:first + 4, :].bitcast(I32),
                                  staged[chunk][first:first + QUADRANT:4, :].bitcast(I32))

        place(0)
        forget_raw = shared.tile([P, PASSES, H // 2], I32, name="forget_raw", align_bytes=ALIGN, offset=AT_WG_FORGET)
        nc.sync.dma_start(forget_raw[:], wg_halves[FORGET])
        wu_raw = shared.tile([P, PASSES * PACK * H], F32, name="wu_raw", align_bytes=ALIGN, offset=AT_WU)
        wu_parts = [[load_wu(0, first, H // 2) for first in (0, H // 2)]]

        def plane(chunk, a, first, width):
            first += a * (LATE if chunk else EARLY)
            return planes[chunk][:, first:first + width]

        states = {}

        def gather(a, half):
            tag = f"states{a}{half}"
            states[a, half] = keep.tile([P, BANK], U32, name=f"states{a}{half}", tag=tag, align_bytes=ALIGN)
            width = BANK // 2 if (a, half) == (1, 0) else BANK
            for lo in range(0, BANK, width):
                first = half * BANK + lo
                entries = offsets[:, first // GROUP:(first + width) // GROUP]
                nc.vector.tensor_copy(states[a, half][:, lo:lo + width], table[a][:].bitcast(U32).indirect(entries))

        deal_wg(nc.gpsimd, wg_codes[INPUT, 1], input_raw[1][:])
        gather(0, 0)
        unread = psum.tile([P, BANK], F32, name="unread")
        for t in range(2):
            nc.tensor.matmul_mx(unread[:], lhsT=wg_codes[INPUT, 0][:, t * 2 * P:(t + 1) * 2 * P].bitcast(FP4X4),
                                lhsT_scale=staged[0][:, FIRST_PICK:FIRST_PICK + P], rhs=states[0, 0][:, :BANK].bitcast(FP8X4),
                                rhs_scale=staged[0][:, :BANK], start=True, stop=True)
        wu_parts.append([load_wu(1, first, H // 2) for first in (0, H // 2)])
        gains = shared.tile([P, PACK], F32, name="gains", align_bytes=ALIGN, offset=AT_GAINS)
        nc.sync.dma_start(gains[:], gain.rearrange("(p t) -> p t", t=PACK))
        gather(0, 1)
        gather(1, 0)
        deal_wg(nc.gpsimd, forget_codes[:].rearrange("p a c -> p (a c)"), forget_raw[:].rearrange("p a c -> p (a c)"))
        gather(1, 1)

        wu_codes, wu_scales = [], []
        for a in range(PASSES):
            wu_bf = keep.tile([P, PACK, P, PACK], BF16, name=f"wu_bf{a}", align_bytes=ALIGN)
            wu_codes.append(keep.tile([P, H], U32, name=f"wu_codes{a}", align_bytes=ALIGN))
            wu_scales.append(keep.tile([P, H], U8, name=f"wu_scales{a}", align_bytes=ALIGN))
            for first, width, rows in wu_parts[a]:
                channels = slice(first // PACK, (first + width) // PACK)
                for t in (0, 2):
                    nc.vector.tensor_copy(wu_bf[:, t:t + 2, channels].rearrange("p t m i -> p m i t"),
                                          rows.rearrange("p i (m t) -> p m i t", t=PACK)[:, :, :, t:t + 2])
            step = 2 if a else PACK
            for t in range(0, PACK, step):
                cols = slice(t * P, (t + step) * P)
                nc.vector.quantize_mx(wu_codes[a][:, cols].bitcast(FP8X4), wu_scales[a][:, cols],
                                      wu_bf[:, t:t + step].rearrange("p t m i -> p (t m i)"))

        cells = shared.tile([P, PACK * S], F32, name="cells", align_bytes=ALIGN, offset=0)
        cell_rows = cell.rearrange("(p t) j -> p t j", t=PACK)

        def chunk_view(tile, first, width):
            return tile[:, PACK * first:PACK * (first + width)].rearrange("p (t j) -> p t j", t=PACK)

        def load_cells(first, width):
            step = BANK // width
            for t in range(0, PACK, step):
                nc.sync.dma_start(chunk_view(cells, first, width)[:, t:t + step, :],
                                  cell_rows[:, t:t + step, first:first + width])

        load_cells(*CHUNKS[0])
        last_planes = shared.tile([P, PASSES * LATE + N], U8, name="last_planes", align_bytes=ALIGN, offset=AT_WO + N * PACK)
        nc.gpsimd.memset(last_planes[:].bitcast(I32), 0)
        planes.append(last_planes[:, :PASSES * LATE])
        place(1)
        for chunk in CHUNKS[1:]:
            load_cells(*chunk)

        wo_codes = shared.tile([P, N], I32, name="wo_codes", align_bytes=ALIGN, offset=AT_WO)
        nc.sync.dma_start(wo_codes[:], wo_words[0].rearrange("p c i -> p (c i)").bitcast(I32))

        wo_plane = last_planes[:, PASSES * LATE:]
        for d in range(P // QUADRANT):
            nc.sync.dma_start(wo_plane[QUADRANT * d:QUADRANT * d + 4, :].bitcast(I32),
                              wo_scales[0, 4 * d:4 * d + 4, :].bitcast(I32))

        identity = shared.tile([P, P], F32, name="identity", align_bytes=ALIGN, offset=AT_IDENTITY)
        make_identity(nc, identity[:])

        acts = {first: keep.tile([P, 3, PACK, width], F32, name=f"acts{first}") for first, width in CHUNKS}
        kept = {first: keep.tile([P, PACK, width], F32, name=f"kept{first}") for first, width in CHUNKS}
        fresh = {first: keep.tile([P, PACK, width], F32, name=f"fresh{first}") for first, width in CHUNKS[1:]}
        fresh[0] = shared.tile([P, PACK, BANK], F32, name="fresh0", align_bytes=ALIGN, offset=AT_FRESH)
        third_gate = shared.tile([P, 1, BANK], F32, name="third_gate", align_bytes=ALIGN, offset=AT_FRESH)

        def activated(start, kind, t0, step=1):
            return third_gate[:] if (start, kind, t0) == (0, FORGET, 2) else acts[start][:, kind, t0:t0 + step]

        def first_stage(chunk, kind, t0, part=None):
            start, whole = chunk
            first, width = part or chunk
            cols = slice(first - start, first - start + width)
            step = BANK // width
            acc = psum.tile([P, step, width], F32, name="acc", tag="ring", bufs=RING)
            passes = range(PASSES) if (first, kind) == (0, INPUT) else range(PASSES)[::-1]
            for a in passes:
                for t in range(t0, t0 + step):
                    if kind == CANDIDATE:
                        codes = wu_codes[a][:, t * P:(t + 1) * P].bitcast(FP8X4)
                        scales = wu_scales[a][:, t * P:(t + 1) * P]
                    else:
                        codes = wg_codes[kind, a][:, t * P * 2:(t + 1) * P * 2].bitcast(FP4X4)
                        scales = plane(0, a, FIRST_PICK + kind * H + t * P, P)
                    words = states[a, first // BANK][:, first % BANK:first % BANK + width]
                    nc.tensor.matmul_mx(acc[:, t - t0, :], lhsT=codes, lhsT_scale=scales,
                                        rhs=words.bitcast(FP8X4), rhs_scale=plane(first // FIRST_PICK, a, first % FIRST_PICK, width),
                                        start=(a, t) == (passes[0], t0), stop=(a, t) == (passes[-1], t0 + step - 1))
            nc.scalar.activation(activated(start, kind, t0, step)[:, :, cols], acc[:], TANH if kind == CANDIDATE else SIGMOID)
            for t in range(t0, t0 + step):
                if kind == FORGET:
                    nc.vector.scalar_tensor_tensor(kept[first][:, t, :], activated(first, FORGET, t)[:, 0], gains[:, t:t + 1],
                                                   chunk_view(cells, first, width)[:, t, :], MULT, MULT)
                elif kind == CANDIDATE:
                    nc.vector.scalar_tensor_tensor(fresh[first][:, t, :], acts[first][:, INPUT, t, :], gains[:, t:t + 1],
                                                   acts[first][:, CANDIDATE, t, :], MULT, MULT)

        def terms(first, width):
            start = max(c for c, w in CHUNKS if c <= first)
            cols = slice(first - start, first - start + width)
            return fresh[start][:, :, cols], kept[start][:, :, cols]

        def rounded(first, width):
            return keep.tile([P, width, PACK], BF16, name=f"h_bf{first}", align_bytes=ALIGN)

        def add(first, width):
            h_bf = rounded(first, width)
            one, other = [term.rearrange("p t (c i) -> p c t i", i=4) for term in terms(first, width)]
            nc.vector.tensor_tensor(h_bf[:].rearrange("p (c i) t -> p c t i", i=4), one, other, ADD)
            return first, width, h_bf

        def add_turned(first):
            total = psum.tile([P, PACK, P], F32, name="total", tag="ring", bufs=RING)
            one, other = terms(first, P)
            for t in range(PACK):
                for term, start in ((one, True), (other, False)):
                    nc.tensor.matmul(total[:, t, :], lhsT=term[:, t, :], rhs=identity[:], is_transpose=True,
                                     start=start, stop=not start)
            turned = keep.tile([P, 2, P, 2], BF16, name=f"turned{first}", align_bytes=ALIGN)
            nc.scalar.copy(turned[:], total[:].rearrange("j (u e) p -> j u p e", e=2))
            return turned

        def turn_back(first, blocks):
            words = psum.tile([P, len(blocks), 2, P], F32, name="words", tag="words", bufs=2)
            for b, turned in enumerate(blocks):
                pairs = turned[:].rearrange("j u p e -> j (u p e)").bitcast(F32)
                for u in range(2):
                    nc.tensor.transpose(words[:, b, u, :], pairs[:, u * P:(u + 1) * P], identity[:])
            h_bf = rounded(first, len(blocks) * P)
            pairs = h_bf[:].rearrange("p j t -> p (j t)").bitcast(F32)
            nc.scalar.copy(pairs.rearrange("p (b j u) -> p b j u", b=len(blocks), u=2),
                           words[:].rearrange("p b u j -> p b j u"))
            return first, len(blocks) * P, h_bf

        h_codes = {first: keep.tile([P, width], U32, name=f"h_codes{first}", align_bytes=ALIGN) for first, width in OUTS}
        h_scales = {first: keep.tile([P, width], U8, name=f"h_scales{first}", align_bytes=ALIGN) for first, width in OUTS}

        def quantise(first, width, h_bf):
            start = max(c for c, w in OUTS if c <= first)
            cols = slice(first - start, first - start + width)
            nc.vector.quantize_mx(h_codes[start][:, cols].bitcast(FP8X4), h_scales[start][:, cols],
                                  h_bf[:].rearrange("p j t -> p (j t)"))

        def second_stage(chunk, copy, tag="ring", bufs=RING):
            first, width = chunk
            acc = psum.tile([P, N // P, width], F32, name="acc", tag=tag, bufs=bufs)
            for n in range(N // P):
                nc.tensor.matmul_mx(acc[:, n, :], lhsT=wo_codes[:, n * P:(n + 1) * P].bitcast(FP8X4),
                                    lhsT_scale=wo_plane[:, n * P:(n + 1) * P], rhs=h_codes[first][:].bitcast(FP8X4),
                                    rhs_scale=h_scales[first][:], start=True, stop=True)
            result = keep.tile([P, N // P, width], F32, name=f"result{first}")
            copy(result[:], acc[:])
            nc.sync.dma_start(out[:, first:first + width].rearrange("(n p) j -> p n j", p=P), result[:])

        wide, middle, last = CHUNKS
        narrow = [(kind, t) for t in (0, 2) for kind in (INPUT, CANDIDATE, FORGET)]
        ahead = [(INPUT, 0), (INPUT, 2)]
        for part in ((0, 256), (256, 256)):
            for t in (0, 2):
                first_stage(wide, INPUT, t, part)
        for t in range(PACK):
            first_stage(wide, FORGET, t)
        for kind, t in ahead:
            first_stage(middle, kind, t)
        for t in range(PACK):
            first_stage(wide, CANDIDATE, t)
        quantise(*add(0, 256))
        for kind, t in narrow:
            if (kind, t) not in ahead:
                first_stage(middle, kind, t)
        quantise(*add(512, 256))
        for kind, t in narrow:
            first_stage(last, kind, t)
        turned = [add_turned(first) for first in (256, 384)]
        sum_a, sum_b = turn_back(256, turned[:1]), turn_back(384, turned[1:])
        for chunk in (OUTS[0], OUTS[3]):
            second_stage(chunk, nc.scalar.copy, "words", 2)
        quantise(*sum_a)
        second_stage(OUTS[1], nc.scalar.copy)
        sum_d = add(768, 128)
        quantise(*sum_b)
        sum_e = add(896, 128)
        quantise(*sum_d)
        quantise(*sum_e)
        second_stage(OUTS[2], nc.scalar.copy)
        second_stage(OUTS[4], nc.scalar.copy)
        second_stage(OUTS[5], nc.vector.tensor_copy)
